import numpy as np, ml_dtypes
CORES = [6,15,38,47]
N = 4
import mx_ref
BF = ml_dtypes.bfloat16
def gentries(a):
    return np.ascontiguousarray(a.reshape(8, 16, -1).transpose(0, 2, 1)).reshape(8, -1)
def gtable(e):
    e = np.asarray(e); return np.ascontiguousarray(e.reshape(8, -1, 16).transpose(0, 2, 1)).reshape(128, -1).astype(np.int32)
def tile(rs):
    return np.stack(rs, axis=2).reshape(128, -1).astype(BF)
def pick(q, e):
    c = np.concatenate([q[0].reshape(128, -1, 4), np.zeros((128, 1, 4), np.uint8)], axis=1); s = np.concatenate([q[1], np.ones((16, 1), np.uint8)], axis=1)
    return (np.ascontiguousarray(c[:, e].reshape(128, -1)), np.ascontiguousarray(s[:, e]))
def join(*qs):
    return (np.concatenate([q[0] for q in qs], axis=1), np.concatenate([q[1] for q in qs], axis=1))
def put(q, e, v):
    c, s = q[0].reshape(128, -1, 4).copy(), q[1].copy(); c[:, e] = v[0].reshape(128, -1, 4); s[:, e] = v[1]
    return (c.reshape(128, -1), s)
def pk(c, s):
    return (np.ascontiguousarray(c), mx_ref.live(s))
def emit(q):
    return q[0], q[1]
def packed(v, rng):
    q = [mx_ref.quantize(np.ascontiguousarray(v[r])) for r in range(N)]
    return np.stack([a for a, b in q]), np.stack([mx_ref.plane(b, rng) for a, b in q])
def values_of_codes():
    e, c = np.zeros((128, 128, 4), np.float32), np.zeros((128, 2, 4), np.uint8)
    e[np.arange(128), np.arange(128), 0] = 1
    c[:127, :, 0] = np.arange(256).reshape(2, 128).T[:127]
    return mx_ref.matmul(mx_ref.quantize(e.reshape(128, 512).astype(BF)), (c.reshape(128, 8), np.full((16, 2), 127, np.uint8))).T.reshape(-1).astype(np.float64)
CODE_VALUE, SCALE_VALUE = values_of_codes(), 2.0 ** (np.arange(256) - 127.0)
def decode(q):
    return (CODE_VALUE[q[0]].reshape(16, 8, -1, 4) * SCALE_VALUE[q[1]][:, None, :, None] + 0.0).reshape(128, -1).astype(np.float32)
def f(rng, *shape):
    return mx_ref.flush((rng.standard_normal(shape, dtype=np.float32) * np.exp2(rng.integers(-2, 3, shape[:-1] + (1,)))).astype(BF))
def wide(rng, *shape, cols=0):
    v = rng.standard_normal(shape, dtype=np.float32) * np.exp2(rng.integers(-12, 13, shape)).astype(np.float32)
    if cols: v *= np.repeat(np.exp2(rng.integers(-cols, cols + 1, shape[:-2] + (1, shape[-1] // 4))) * (rng.random(shape[:-2] + (1, shape[-1] // 4)) > 0.0625), 4, axis=-1).astype(np.float32)
    return mx_ref.flush(v.astype(BF))
C, B, L, M, R = 320, 48, 416, 160, 3
MASK = [1, 2, 3]
def big(v):
    v = v.astype(np.float32)
    v[np.abs(v) < np.float32(2.0 ** -16)] = 0
    return v.astype(BF)
def numbers_of(rng):
    return {"x": big(f(rng, N, 128, 4 * C)), "u": np.array(f(rng, N, 128, 512)), "v": np.array(f(rng, N, 128, 512))}
def rings(rng, ends=False):
    p = [np.arange(C)[::1 - 2 * (h % 2)] if ends else rng.permutation(C) for h in range(8)]
    e = np.zeros((8, L), np.int64)
    for g in range(8):
        a, b = (g - 1) % 8, (g + 1) % 8
        e[g] = rng.permutation(np.concatenate([C * g + np.arange(C), C * a + p[a][:B], C * b + p[b][B:2 * B]]))
        if ends: e[g] = np.sort(e[g])[::1 - 2 * (g // 2 % 2)]
    return np.stack([gtable(e)] * N)
def layers(rng):
    return big(np.clip(f(rng, N, 128, 2048).astype(np.float32) * np.float32(0.25), -1.75, 1.75)).reshape(N, 8, 16, 4, 8, 16, 4)
def weights(rng, w):
    c, s = packed(np.ascontiguousarray(w).reshape(N, 128, 2048), rng)
    return {"wc": c, "ws": s}
def setup_inputs(rng):
    return {**numbers_of(rng), "ring": rings(rng), **weights(rng, layers(rng))}
def setup_inputs_ties(rng):
    d = numbers_of(rng)
    o = rng.permutation(N)
    same = rng.random((N, 8, C)) < rng.random((N, 8, 1))
    same[o[0]] = True
    same[o[0], rng.integers(8)] = False
    a = rng.integers(0, 3, (N, 8, C))
    b = np.where(same, a, rng.integers(0, 3, (N, 8, C)))
    least = max(257 if C > 256 else 0, 17 * C // 20) | 1
    for r in o[1:]:
        n = rng.permutation(np.arange(least, 19 * C // 20 + 1, 2))[:3]
        for i, g in enumerate(rng.permutation(8)[:3]):
            b[r, g] = a[r, g]
            j = rng.permutation(C)[:n[i]]
            more = rng.integers(1, 3, n[i])
            less = rng.integers(0, more)
            a[r, g, j] = more if o[r] % 2 else less
            b[r, g, j] = less if o[r] % 2 else more
    x = d["x"].reshape(N, 8, 16, C, 4)
    x[:, :, 0] = 0
    x[:, :, 0, :, 0] = a.astype(np.float32).astype(BF)
    x[:, :, 0, :, 1] = b.astype(np.float32).astype(BF)
    u = d["u"].reshape(N, 128, 128, 4)
    u[:, :, ::16] = 0
    for r in range(N):
        for h in range(0, 128, 16):
            u[r, h, h, 0] = 1.0 if o[r] % 2 else -1.0
            u[r, h, h, 1] = -1.0 if o[r] % 2 else 1.0
    w = layers(rng)
    w[:, :, :, :, :, 0] = 0
    return {"x": x.reshape(N, 128, 4 * C), "u": u.reshape(N, 128, 512), "v": d["v"], "ring": rings(rng), **weights(rng, w)}
def setup_inputs_near(rng):
    d = numbers_of(rng)
    o = rng.permutation(N) % 4
    k = rng.integers(0, 4, (N, 8, C))
    a = np.array([1.125, -1.125, 1.0, -1.0])[k]
    b = np.array([-1.25, 1.25, -1.125, 1.125])[k]
    x = d["x"].astype(np.float32).reshape(N, 8, 16, C, 4)
    x[:, :, :8] = 0
    u = d["u"].reshape(N, 128, 128, 4)
    u[:, :, ::16] = 0
    i = np.arange(32)
    s = np.exp2(-12.0 - i // 2 % 4)
    for r in range(N):
        z = 2.0 ** -30 if o[r] < 2 else 1.0
        x[r, :, 0, :, 0] = a[r] * z
        x[r, :, 1, :, 0] = b[r] * z
        for g in range(8):
            j = rng.permutation(C)[:32]
            x[r, g, 0, j, 0] = 0
            x[r, g, 1, j, 0] = 0
            x[r, g, 2, j, 0] = 1.96875
            x[r, g, 3, j, 0] = np.where(i % 2 == 0, 1.5, 1.125) * s
            x[r, g, 4, j, 0] = np.where(i % 2 == 0, -1.375, -1.0) * s
        for g in rng.permutation(8)[:4]:
            j = rng.integers(C)
            x[r, g, :8, j] = 0
            x[r, g, 0, j, 0] = 2.0 ** 14 * rng.choice([-1.0, 1.0])
        for h in range(0, 128, 16):
            z = 2.0 ** -30 if o[r] % 2 == 0 else 1.0
            u[r, h, h, 0] = 1.125 * z
            u[r, h + 1, h, 0] = z
            u[r, h + 3, h, 0] = z
            u[r, h + 4, h, 0] = z
    w = layers(rng)
    w[:, :, :8] = 0
    w[:, :, :, :, :, :8] = 0
    for g in range(8): w[:, g, 2, 0, g, 2, 0] = -0.5
    return {"x": x.reshape(N, 128, 4 * C).astype(BF), "u": u.reshape(N, 128, 512), "v": d["v"], "ring": rings(rng), **weights(rng, w)}
def setup_inputs_late(rng):
    d = numbers_of(rng)
    x = d["x"].astype(np.float32).reshape(N, 8, 16, C, 4)
    x[:, :, 0] = ((rng.permutation(N) % 2) * 0.25 - 0.125)[:, None, None, None]
    s = (N, 8, 8, C, 4)
    x[:, :, 8:] = rng.choice([-1.0, 1.0], s) * (1.0 + 0.125 * (2 * rng.integers(0, 4, s) + 1)) * np.exp2(10.0 - rng.integers(8, 15, s))
    x[:, :, 8, :, 0] = rng.choice([-1.0, 1.0], (N, 8, C)) * 1.96875 * 2.0 ** 10
    u = d["u"].reshape(N, 128, 128, 4)
    u[:, :, ::16] = 0
    for h in range(0, 128, 16): u[:, h, h, 0] = 1.0
    w = layers(rng)
    w[:, :, 8] = 0
    w[:, :, :, :, :, 8:] = (w[:, :, :, :, :, 8:].astype(np.float32) * np.float32(0.125)).astype(BF)
    w[:, :, :, 0, :, 8] = 0
    for g in range(8): w[:, g, 8, 0, g, 8, 0] = -0.5
    return {"x": x.reshape(N, 128, 4 * C).astype(BF), "u": u.reshape(N, 128, 512), "v": d["v"], "ring": rings(rng), **weights(rng, w)}
def setup_inputs_ends(rng):
    d = numbers_of(rng)
    o = rng.permutation(N)
    x = np.zeros((N, 8, 16, C, 4), np.float32)
    u = d["u"].reshape(N, 128, 128, 4)
    u[:, :, ::16] = 0
    v = rng.choice([-1.0, 1.0], (N, 128, 512)).astype(np.float32)
    w = np.zeros((N, 8, 16, 4, 8, 16, 4), np.float32)
    for r in range(N):
        i = o[r] % 4
        k = np.array([1.0, 1.0, 1.0, -1.0, -1.0, -1.0, 0.0, 0.0])[rng.permutation(8)]
        x[r, :, :8] = k[:, None, None, None] * (2.0 ** 14 if i % 2 == 0 else 2.0 ** -30)
        x[r, :, 8:] = 2.0 ** 14 * rng.choice([-1.0, 1.0], (1, 1, C, 1) if i < 2 else (8, 8, C, 4))
        z = 2.0 ** 30 if i // 2 == 0 else 2.0 ** -30
        s = rng.choice([-1.0, 1.0])
        for h in range(0, 128, 16): u[r, h:h + 8, h] = s * z
        v[r] *= np.float32(z)
        w[r, :, 8:, :, :, 8:] = 1.96875 if i == 0 else -1.96875 if i == 3 else (1.96875 if i == 1 else 2.0 ** -30) * rng.choice([-1.0, 1.0], (8, 8, 4, 8, 8, 4))
    return {"x": x.reshape(N, 128, 4 * C).astype(BF), "u": u.reshape(N, 128, 512), "v": v.astype(BF), "ring": rings(rng, True), **weights(rng, w.astype(BF))}
def setup_inputs_spread(rng):
    d = setup_inputs(rng)
    d["x"] = big(wide(rng, N, 128, 4 * C, cols=3).astype(np.float32) * np.float32(0.03125))
    return d
def check_inputs(d):
    b = []
    for k, most in (("x", 2.0 ** 14), ("u", 2.0 ** 30), ("v", 2.0 ** 30)):
        a = np.abs(d[k].astype(np.float32))
        if not (np.isfinite(a).all() and ((a == 0) | (a >= 2.0 ** -30) & (a <= most)).all()): b.append("a value of " + k)
    if (d["ring"] != d["ring"][:1]).any(): b.append("ring isn't the same on all ranks")
    e = gentries(d["ring"][0])
    if not ((e >= 0) & (e < 8 * C)).all(): b.append("an entry of ring")
    for g in range(8):
        h = e[g] // C
        if np.unique(e[g]).size != L: b.append("a place twice in a ring")
        if np.count_nonzero(h == g) != C or np.count_nonzero(h == (g - 1) % 8) != B or np.count_nonzero(h == (g + 1) % 8) != B: b.append("the groups of a ring's places")
    for k in range(2):
        if np.unique(e[k::2]).size != 4 * L: b.append("rings of equal parity share a place")
    none, least, most = [emit(mx_ref.quantize(np.full((128, 16), k, np.float32).astype(BF)))[1][0, 0] for k in (0.0, 2.0 ** -30, 1.96875)]
    for r in range(N):
        if ((d["wc"][r] == 0x7F) | (d["wc"][r] == 0xFF)).any(): b.append("wc: a code that is no number")
        s = mx_ref.live(d["ws"][r])
        if ((s != none) & ((s < least) | (s > most))).any(): b.append("ws: a scale out of range")
        elif (np.abs(decode(pk(d["wc"][r], d["ws"][r]))) > 2.0).any(): b.append("a number of W beyond 2 in size")
    return b
def turned(e, a):
    now = np.arange(8 * C)
    for first in (1, 0):
        new = now.copy()
        for g in range(first, 8, 2): new[np.roll(e[g], -a[g])] = now[e[g]]
        now = new
    return now.reshape(8, C)
def reference(x, u, v, ring, wc, ws):
    qu = [mx_ref.quantize(u[r]) for r in range(N)]
    lay = [pk(wc[r], ws[r]) for r in range(N)]
    now = [x[r] for r in range(N)]
    e = gentries(ring[0])
    ac = np.zeros((N, 8, R), np.float32)
    for t in range(R):
        own, sent = [], []
        for r in range(N):
            q = mx_ref.quantize(now[r])
            s = mx_ref.matmul(qu[r], q)
            a = np.count_nonzero(s[::16] > 0, axis=1)
            ac[r, :, t] = a
            p = turned(e, a)
            own.append(np.ascontiguousarray(decode(q).reshape(8, 16, C, 4)[p // C, :, p % C].transpose(0, 2, 1, 3)).reshape(128, 4 * C).astype(BF))
            sent.append(decode(mx_ref.quantize(np.ascontiguousarray(own[r][:, :4 * M]))).astype(BF))
        for r in range(N):
            z = np.concatenate([sent[r ^ MASK[t]], own[r][:, 4 * M:]], axis=1)
            q = mx_ref.quantize(z)
            now[r] = tile([mx_ref.matmul(pick(lay[r], np.arange(128 * b, 128 * b + 128)), q) * np.float32(0.03125) + z[:, b::4].astype(np.float32) for b in range(4)])
    y = np.zeros((N, 128, C), np.float32)
    oc, osc = np.zeros((N, 128, 4 * C), np.uint8), np.zeros((N, 16, C), np.uint8)
    for r in range(N):
        q = mx_ref.quantize(now[r])
        y[r] = mx_ref.matmul(mx_ref.quantize(v[r]), q)
        oc[r], osc[r] = emit(q)
    return {"y": y, "ac": ac, "oc": oc, "osc": osc}

@@ -1,0 +1,501 @@
+import numpy as np
+from concourse.mybir import dt, AluOpType, ActivationFunctionType
+
+N = 4
+MASKS = (1, 2, 3)
+NC, HALF, GRP, RING, DBL = 320, 160, 16, 416, 736
+CEN = 7 * NC
+WINC = 15 * NC
+IDB = 3 * DBL
+INV = WINC
+ABS = 2500
+OP = AluOpType
+FN = ActivationFunctionType
+
+SCRATCH = {
+    "win": ("sbuf", [128, 4 * WINC], "bfloat16"),
+    "map": ("sbuf", [128, 2 * WINC], "float32"),
+    "src": ("sbuf", [128, IDB + WINC], "float32"),
+    "idt": ("sbuf", [128, 2560], "float32"),
+    "iv1": ("sbuf", [128, RING], "float32"), "iv2": ("sbuf", [128, RING], "float32"),
+    "ri": ("sbuf", [128, 130], "int32"), "eu": ("sbuf", [128, 78], "uint16"), "xu": ("sbuf", [128, 52], "uint16"),
+    "kl": ("sbuf", [128, 40], "int32"), "xk": ("sbuf", [128, 40], "uint16"), "xe": ("sbuf", [128, 40], "uint16"),
+    "pI": ("sbuf", [128, 8], "int32"), "gI": ("sbuf", [128, 8], "int32"), "pr": ("sbuf", [128, 8], "int32"), "p7": ("sbuf", [128, 8], "int32"),
+    "kI": ("sbuf", [128, 8], "int32"), "ul": ("sbuf", [128, 8], "uint16"),
+    "sc": ("sbuf", [128, 32], "float32"),
+    "jj": ("sbuf", [128, 48], "int32"), "cst": ("sbuf", [128, 48], "int32"), "mk": ("sbuf", [128, 48], "float32"), "kp8": ("sbuf", [128, 48], "float32"),
+    "jm": ("sbuf", [128, 640], "float32"), "jd": ("sbuf", [128, 640], "float32"), "mask": ("sbuf", [128, 640], "float32"), "keep": ("sbuf", [128, 640], "float32"),
+    "j20": ("sbuf", [128, 20], "float32"), "j832": ("sbuf", [128, 20], "float32"),
+    "hm0": ("sbuf", [128, 640], "float32"), "hs0": ("sbuf", [128, 640], "float32"),
+    "hm1": ("sbuf", [128, 640], "float32"), "hs1": ("sbuf", [128, 640], "float32"),
+    "ph": ("sbuf", [128, 52], "float32"), "pe": ("sbuf", [128, 40], "float32"), "lt": ("sbuf", [128, 20], "float32"), "rt": ("sbuf", [128, 20], "float32"),
+    "w1": ("sbuf", [128, 26], "float32"), "w2": ("sbuf", [128, 26], "float32"), "w3": ("sbuf", [128, 26], "float32"), "w4": ("sbuf", [128, 26], "float32"),
+    "bA": ("sbuf", [128, 92], "float32"), "mL": ("sbuf", [128, 92], "float32"), "mR": ("sbuf", [128, 92], "float32"),
+    "g1": ("sbuf", [128, 72], "float32"), "g2": ("sbuf", [128, 72], "float32"), "g3": ("sbuf", [128, 72], "float32"),
+    "ta": ("sbuf", [128, 92], "float32"), "tb": ("sbuf", [128, 92], "float32"), "tq": ("sbuf", [128, 92], "float32"), "tw": ("sbuf", [128, 20], "float32"), "te": ("sbuf", [128, 20], "float32"),
+    "oA": ("sbuf", [128, 72], "uint16"), "oB": ("sbuf", [128, 20], "uint16"), "l4": ("sbuf", [128, 80], "uint16"),
+    "tab": ("sbuf", [128, 1152], "float32"),
+    "bm": ("sbuf", [128, 2 * HALF], "float32"), "bs": ("sbuf", [128, 2 * HALF], "float32"),
+    "cm": ("sbuf", [128, 48], "float32"), "cs": ("sbuf", [128, 48], "float32"), "acs": ("sbuf", [128, 4], "float32"),
+    "ew": ("sbuf", [128, 516], "bfloat16"), "e1": ("sbuf", [128, 516], "bfloat16"), "e32": ("sbuf", [128, 516], "bfloat16"),
+    "qe": ("sbuf", [128, 1024], "float8_e4m3fn_x4"), "se": ("sbuf", [128, 1024], "uint8"),
+    "ct": ("sbuf", [128, 512], "bfloat16"), "qc": ("sbuf", [128, 128], "float8_e4m3fn_x4"), "sct": ("sbuf", [128, 128], "uint8"),
+    "ft": ("sbuf", [128, 512], "bfloat16"), "qf": ("sbuf", [128, 128], "float8_e4m3fn_x4"), "sf": ("sbuf", [128, 128], "uint8"),
+    "ut": ("sbuf", [128, 512], "bfloat16"), "qu": ("sbuf", [128, 128], "float8_e4m3fn_x4"), "su": ("sbuf", [128, 128], "uint8"),
+    "qu2": ("sbuf", [128, 128], "float8_e4m3fn_x4"), "su2": ("sbuf", [128, 128], "uint8"),
+    "vt": ("sbuf", [128, 512], "bfloat16"), "qv": ("sbuf", [128, 128], "float8_e4m3fn_x4"), "sv": ("sbuf", [128, 128], "uint8"),
+    "wq": ("sbuf", [128, 512], "float8_e4m3fn_x4"), "wsb": ("sbuf", [128, 512], "uint8"),
+    "qx": ("sbuf", [128, NC], "float8_e4m3fn_x4"), "sx": ("sbuf", [128, NC], "uint8"),
+    "gr": ("sbuf", [128, 4 * HALF], "bfloat16"), "q1": ("sbuf", [128, HALF], "float8_e4m3fn_x4"), "s1": ("sbuf", [128, HALF], "uint8"),
+    "gt": ("sbuf", [128, 4 * HALF], "bfloat16"), "q2": ("sbuf", [128, HALF], "float8_e4m3fn_x4"), "s2": ("sbuf", [128, HALF], "uint8"),
+    "ow": ("sbuf", [128, 4 * HALF], "bfloat16"), "qo": ("sbuf", [128, HALF], "float8_e4m3fn_x4"), "so": ("sbuf", [128, HALF], "uint8"),
+    "zo": ("sbuf", [128, 4 * HALF], "bfloat16"), "zg": ("sbuf", [128, 4 * HALF], "bfloat16"),
+    "qzo": ("sbuf", [128, HALF], "float8_e4m3fn_x4"), "szo": ("sbuf", [128, HALF], "uint8"),
+    "qzg": ("sbuf", [128, HALF], "float8_e4m3fn_x4"), "szg": ("sbuf", [128, HALF], "uint8"),
+    "yt": ("sbuf", [128, NC], "float32"),
+}
+for _r in range(3):
+    SCRATCH["lc%d" % _r] = ("sbuf", [128, HALF], "float8_e4m3fn_x4")
+    SCRATCH["ls%d" % _r] = ("sbuf", [128, HALF], "uint8")
+for _b in range(8):
+    SCRATCH["ps%d" % _b] = ("psum", [128, 512], "float32")
+SEMAPHORES = ["cV", "cS", "cT", "cG", "dX", "dR", "dQ", "dH", "dU", "dV", "dW", "shO", "shG", "dL", "dE", "dOut", "arr0", "arr1", "arr2", "sent"]
+
+
+def shifts(lo, hi):
+    out = []
+
+    def piece(p0, p1, q0):
+        slot = q0 // GRP - p0 // GRP + 7
+        out.append((p0, p1, q0, 4 * (NC * slot + lo), 4 * (hi - lo)))
+    for m in (1, 2):
+        k = GRP * m
+        piece(0, 128 - k, k)
+        piece(128 - k, 128, 0)
+        piece(k, 128, 0)
+        piece(0, k, 128 - k)
+    for grp in (1, 3, 5, 7):
+        for d in (3, -3):
+            piece(GRP * grp, GRP * grp + GRP, GRP * ((grp + d) % 8))
+    return out
+
+
+def rank_program(g, core, T, topo):
+    rank = T.rank_of(core)
+    if rank is None:
+        return
+    eng = {"V": g.vector, "S": g.scalar, "T": g.tensor, "G": g, "Y": g.sync}
+    own_sem = {"V": "cV", "S": "cS", "T": "cT", "G": "cG"}
+    total = {s: 0 for s in SEMAPHORES}
+    local = ("dX", "dR", "dQ", "dH", "dU", "dV", "dW", "shO", "shG", "dL", "dE", "dOut")
+    known = {e: {} for e in eng}
+    writer, reader = {}, {}
+
+    def gate(e, r, w):
+        need = []
+        for t in r:
+            need += writer.get(t, [])
+        for t in w:
+            need += writer.get(t, [])
+            need += [x for x in reader.get(t, []) if x[3] != e]
+        best = {}
+        for sem, val, clk, _ in need:
+            v = total[sem] if sem in local else val
+            best[sem] = max(best.get(sem, 0), v)
+        clks = {}
+        for sem, val, clk, _ in need:
+            for s, v in clk.items():
+                if s != sem and s not in local:
+                    clks.setdefault(s, []).append((sem, v))
+        for sem in best:
+            v = best[sem]
+            if known[e].get(sem, 0) >= v:
+                continue
+            if any(o != sem and o in best and x >= v for o, x in clks.get(sem, [])):
+                continue
+            eng[e].wait_ge(T.sem[sem], v)
+        for sem, val, clk, _ in need:
+            for s, v in clk.items():
+                known[e][s] = max(known[e].get(s, 0), v)
+        for sem in best:
+            known[e][sem] = max(known[e].get(sem, 0), best[sem])
+
+    def mark(e, sem, val, r, w):
+        clk = dict(known[e])
+        clk[sem] = val
+        x = (sem, val, clk, e)
+        for t in w:
+            writer[t] = [x]
+            reader[t] = []
+        for t in r:
+            reader.setdefault(t, []).append(x)
+
+    def op(e, call, r, w):
+        gate(e, r, w)
+        s = own_sem[e]
+        total[s] += 1
+        call().then_inc(T.sem[s], 1)
+        mark(e, s, total[s], r, w)
+
+    def dma(e, sem, out, in_, r, w):
+        if sem not in ("shO", "shG"):
+            gate(e, r, w)
+        total[sem] += 16
+        eng[e].dma_start(out, in_).then_inc(T.sem[sem], 16)
+        mark(e, sem, total[sem], r, w)
+
+    def ts(out, in0, s1, o1, r, w, s2=None, o2=None):
+        if o2 is None:
+            op("V", lambda: g.vector.tensor_scalar(out, in0, s1, None, o1), r, w)
+        else:
+            op("V", lambda: g.vector.tensor_scalar(out, in0, s1, s2, o1, o2), r, w)
+
+    def tt(out, in0, in1, o, r, w):
+        op("V", lambda: g.vector.tensor_tensor(out, in0, in1, o), r, w)
+
+    def cp(out, in_, r, w):
+        op("V", lambda: g.vector.tensor_copy(out, in_), r, w)
+
+    def fill(ap, c, w):
+        op("V", lambda: g.vector.memset(ap, c), (), w)
+
+    def act(out, in_, r, w, scale=1.0, bias=None, fn=None):
+        if bias is None:
+            op("S", lambda: g.scalar.activation(out, in_, fn or FN.Copy, scale=scale), r, w)
+        else:
+            op("S", lambda: g.scalar.activation(out, in_, fn or FN.Identity, bias=bias, scale=scale), r, w)
+
+    def scan(out, k, d, r, w):
+        op("V", lambda: g.vector.tensor_tensor_scan(out, k, d, 0.0, OP.mult, OP.add), r, w)
+
+    def quant(q, s, a, b, tile, c0, r, w):
+        op("V", lambda: g.vector.quantize_mx(q[:, a:b], s[:, a:b], tile[:, c0:c0 + 4 * (b - a)]), r, w)
+
+    def mm(out, l, ls, la, m, ms, ma, n, r, w, start=True, stop=True):
+        op("T", lambda: g.tensor.matmul_mx(out, l[:, la:la + 128], ls[:, la:la + 128], m[:, ma:ma + n], ms[:, ma:ma + n], start, stop), r, w)
+
+    def evac(e, out, in_, r, w, scale):
+        if e == "S":
+            act(out, in_, r, w, scale=scale)
+        elif scale == 1.0:
+            cp(out, in_, r, w)
+        else:
+            ts(out, in_, scale, OP.mult, r, w)
+
+    ps = [T["ps%d" % b] for b in range(8)]
+    sc = lambda k: T.sc[:, k:k + 1]
+    NSH = len(shifts(0, NC))
+
+    def ring(q, sem, k, p0, p1, q0, tok):
+        dma(q, sem, T.ri[p0:p1, 26 * k:26 * k + 26], T.ring[q0:q0 + p1 - p0, :], (), (tok,))
+    for f in (1, 3, 5, 7):
+        ring("S", "dR", 3, GRP * f, GRP * f + GRP, GRP * f, ("l1", f))
+        e = (f + 1) % 8
+        ring("Y", "dR", 3, GRP * e, GRP * e + GRP, GRP * f, ("l1", e))
+    ring("S", "dR", 4, 0, 128 - GRP, GRP, "l2a")
+    ring("Y", "dR", 4, 128 - GRP, 128, 0, "l2b")
+    dma("Y", "dX", T.win[:, 4 * CEN:4 * (CEN + NC)], T.x[:, :], (), ("xO", "xG"))
+    dma("Y", "dU", T.ut[:, :], T.u[:, :], (), ("ut",))
+    n = 0
+    for k, src in ((0, -1), (1, 1)):
+        for h in range(8):
+            f = (h // 2 * 2 + src) % 8
+            ring("SY"[n % 2], "dQ", k, GRP * h, GRP * h + GRP, GRP * f, ("q", k, h))
+            n += 1
+    ring("S", "dQ", 2, 0, 128 - 2 * GRP, 2 * GRP, "l3a")
+    ring("Y", "dQ", 2, 128 - 2 * GRP, 128, 0, "l3b")
+    qtok = tuple(("q", k, h) for k in range(2) for h in range(8)) + ("l3a", "l3b")
+
+    fl = dict(allow_small_or_imprecise_dtypes=True)
+    op("G", lambda: g.iota(T.pI[:, :], [[0, 8]], 0, 1), (), ("pI",))
+    op("G", lambda: g.iota(T.idt[:, 0:RING], [[1, RING]], 0, 0, **fl), (), ("id0",))
+    op("G", lambda: g.iota(T.j20[:, :], [[16, 20]], 0, 1, **fl), (), ("j20",))
+    op("G", lambda: g.iota(T.jm[:, :], [[0, 40], [1, 16]], 0, 0, **fl), (), ("jm",))
+    op("G", lambda: g.iota(T.jj[:, 0:40], [[1, 5], [1, 8]], 63, 0), (), ("jja",))
+    op("G", lambda: g.iota(T.jj[:, 40:48], [[1, 8]], 64, 0), (), ("jjb",))
+    op("G", lambda: g.iota(T.idt[:, RING:2560], [[1, 2560 - RING]], RING, 0, **fl), (), ("id1",))
+    op("G", lambda: g.iota(T.ew[:, :], [[0, 516]], 32, 0, **fl), (), ("ew",))
+    op("G", lambda: g.affine_select(T.e1[:, :], T.ew[:, :], [[1, 516]], OP.is_equal, 0.0, -3, -4), ("ew",), ("e1",))
+    ts(T.gI[:, :], T.pI[:, :], 4, OP.arith_shift_right, ("pI",), ("gI",))
+    ts(T.kI[:, :], T.pI[:, :], 15, OP.bitwise_and, ("pI",), ("kI",))
+    ts(T.p7[:, :], T.pI[:, :], 7, OP.bitwise_and, ("pI",), ("p7",))
+    ts(T.pr[:, :], T.gI[:, :], 1, OP.bitwise_and, ("gI",), ("pr",))
+    gc, pc = T.gI[:, 0:1], T.pr[:, 0:1]
+    ts(sc(2), gc, -320.0, OP.mult, ("gI",), ("s2",), float(CEN), OP.add)
+    ts(sc(15), gc, 304.0, OP.mult, ("gI",), ("s15",))
+    ts(sc(19), T.kI[:, 0:1], -1.0, OP.mult, ("kI",), ("s19",))
+    ts(sc(20), pc, float(DBL), OP.mult, ("pr",), ("s20",), 320.0, OP.add)
+    ts(sc(21), pc, -float(DBL + 320), OP.mult, ("pr",), ("s21",), float(DBL + 320), OP.add)
+    ts(sc(24), pc, float(INV), OP.mult, ("pr",), ("s24",))
+    ts(T.kl[:, 0:20], T.j20[:, :], sc(15), OP.add, ("j20", "s15"), ("kl0",))
+    tt(sc(14), sc(2), sc(24), OP.add, ("s2", "s24"), ("s14",))
+    tt(sc(16), sc(15), sc(24), OP.add, ("s15", "s24"), ("s16",))
+    ts(sc(7), sc(2), 4.0, OP.mult, ("s2",), ("s7",))
+    ts(T.kl[:, 20:40], T.j20[:, :], sc(16), OP.add, ("j20", "s16"), ("kl1",))
+    cp(sc(0), gc, ("gI",), ("s0",))
+    cp(sc(1), pc, ("pr",), ("s1",))
+    ts(sc(4), gc, -16.0, OP.mult, ("gI",), ("s4",), float(CEN), OP.add)
+    ts(sc(5), gc, 7.0, OP.is_equal, ("gI",), ("s5",), -2560.0, OP.mult)
+    ts(sc(6), pc, float(INV + NC), OP.mult, ("pr",), ("s6",))
+    ts(sc(8), pc, 320.0, OP.mult, ("pr",), ("s8",))
+    tt(sc(9), sc(4), sc(5), OP.add, ("s4", "s5"), ("s9",))
+    ts(sc(12), gc, -16.0, OP.mult, ("gI",), ("s12",), 832.0, OP.add)
+    ts(sc(22), gc, 0.0, OP.is_equal, ("gI",), ("s22",), -2560.0, OP.mult)
+    tt(sc(17), sc(9), sc(6), OP.add, ("s9", "s6"), ("s17",))
+    ts(sc(23), pc, -10000.0, OP.mult, ("pr",), ("s23",), 10001.0, OP.add)
+    ts(sc(25), sc(22), -416.0, OP.add, ("s22",), ("s25",))
+    tt(sc(18), sc(17), sc(8), OP.add, ("s17", "s8"), ("s18",))
+    ts(T.ul[:, :], T.p7[:, :], 16, OP.mult, ("p7",), ("ul",))
+    for h in (0, 2, 4, 6):
+        dma("Y", "dH", T.kl[GRP * h:GRP * h + GRP, 0:26], T.ring[GRP * h:GRP * h + GRP, :], ("kl0", "kl1"), (("kh", h),))
+    klt = ("kl0", "kl1") + tuple(("kh", h) for h in (0, 2, 4, 6))
+    for k, (p0, p1, q0, c, n) in enumerate(shifts(0, NC)):
+        dma("Y", "shG", T.win[p0:p1, c:c + n], T.x[q0:q0 + p1 - p0, :], (), (("shG", k),))
+    dma("Y", "dW", T.wq[:, :].bitcast(dt.uint8), T.wc[:, :], (), ("wq",))
+    dma("Y", "dW", T.wsb[:, :], T.ws[:, :], (), ("wsb",))
+    dma("Y", "dV", T.vt[:, :], T.v[:, :], (), ("vt",))
+    act(T.iv1[:, :], T.idt[:, 0:RING], ("id0", "s20"), ("iv1",), bias=sc(20))
+    act(T.map[:, CEN:CEN + NC], T.idt[:, 0:NC], ("id0",), ("map0",), bias=float(IDB + CEN))
+    for k, c in enumerate((INV + CEN, INV + CEN + 2 * NC, INV + NC)):
+        act(T.map[:, c:c + NC], T.idt[:, 0:NC], ("id0",), ("map%d" % (k + 1),), scale=0.0, bias=float(ABS))
+    act(T.iv2[:, :], T.idt[:, 0:RING], ("id0", "s21"), ("iv2",), bias=sc(21))
+    act(T.jd[:, :], T.jm[:, :], ("jm", "s19"), ("jd",), bias=sc(19), fn=FN.Abs)
+    act(T.mask[:, :], T.jd[:, :], ("jd",), ("mask",), scale=-1.0, bias=1.0, fn=FN.Relu)
+    act(T.keep[:, :], T.jm[:, :], ("jm",), ("keep",), fn=FN.Sign)
+    mapt = tuple("map%d" % k for k in range(4))
+    for k, (p0, p1, t, c) in enumerate(((0, 128, 0, 1.0), (0, 128, 1, 1.0), (0, 64, 2, 0.0), (64, 128, 2, 1.0), (0, 128, 3, 0.0))):
+        act(T.ct[p0:p1, t:512:4], T.idt[p0:p1, 0:128], ("id0",), (("ct", k),), scale=0.0, bias=c)
+    act(T.ft[:, :], T.jm[:, 0:512], ("jm",), ("ft0", "ft1", "ft2"), scale=0.0)
+    fill(T.cst[:, 0:24], -1, ("c0",))
+    fill(T.cst[:, 24:32], 3, ("c1",))
+    fill(T.cst[:, 32:40], 5, ("c2",))
+    fill(T.cst[:, 40:48], 0, ("c3",))
+
+    l1t = tuple(("l1", h) for h in range(8)) + ("l2a", "l2b")
+    ts(T.xu[:, 0:26], T.ri[:, 78:104], sc(2), OP.add, l1t + ("s2",), ("xu0",))
+    ts(T.xu[:, 26:52], T.ri[:, 104:130], sc(14), OP.add, l1t + ("s14",), ("xu1",))
+
+    def scatter(k, nm):
+        op("V", lambda: g.vector.tensor_copy(T.map[:, 0:2 * WINC].indirect(T.xu[:, 26 * k:26 * k + 26]), T[nm][:, :]), (nm, "xu%d" % k), mapt)
+    scatter(0, "iv1")
+    cp(T.eu[:, :], T.ri[:, 0:78], qtok, ("eu",))
+    quant(T.qu, T.su, 0, 128, T.ut, 0, ("ut",), ("qu",))
+    scatter(1, "iv2")
+    quant(T.qx, T.sx, 0, NC, T.win, 4 * CEN, ("xO", "xG"), ("qxO", "qxG"))
+    op("V", lambda: g.vector.tensor_copy(T.qu2[:, 0:128].bitcast(dt.uint32), T.qu[:, 0:128].bitcast(dt.uint32).indirect(T.ul[:, 0:8])), ("qu", "ul"), ("qu2",))
+    op("V", lambda: g.vector.tensor_copy(T.su2[:, 0:128], T.su[:, 0:128].indirect(T.ul[:, 0:8])), ("qu", "ul"), ("su2",))
+    ts(T.xk[:, :], T.kl[:, :], sc(2), OP.add, klt + ("s2",), ("xk",))
+    ts(T.xe[:, 0:20], T.j20[:, :], sc(17), OP.add, ("j20", "s17"), ("xe0",))
+    ts(T.xe[:, 20:40], T.j20[:, :], sc(18), OP.add, ("j20", "s18"), ("xe1",))
+    act(T.src[:, IDB + CEN - NC:IDB + CEN + 2 * NC], T.idt[:, 0:960], ("id0", "id1"), ("src0",), scale=4.0, bias=float(4 * (CEN - NC)))
+    act(T.src[:, IDB:IDB + NC], T.idt[:, 0:NC], ("id0",), ("src1",), scale=4.0)
+    for k in range(3):
+        act(T.src[:, DBL * k:DBL * k + 320], T.idt[:, 0:2560].indirect(T.eu[:, 26 * k + 6:26 * k + 26]), ("id0", "id1", "eu", "s7"), (("sr", k, 0),), scale=4.0, bias=sc(7))
+        act(T.src[:, DBL * k + 320:DBL * k + 736], T.idt[:, 0:2560].indirect(T.eu[:, 26 * k:26 * k + 26]), ("id0", "id1", "eu", "s7"), (("sr", k, 1),), scale=4.0, bias=sc(7))
+    srct = ("src0", "src1") + tuple(("sr", k, i) for k in range(3) for i in range(2))
+
+    def look(k, off, r):
+        m, s = T["hm%d" % k], T["hs%d" % k]
+        tt(m[:, :], T.map[:, 0:2 * WINC].indirect(off), T.mask[:, :], OP.mult, mapt + ("mask",) + r, (("hm", k),))
+        scan(s[:, :], T.keep[:, :], m[:, :], ("keep", ("hm", k)), (("hs", k),))
+
+    def compare(t):
+        ts(T.ft[:, t:192:4], ps[t][:, 0:48], 0.0, OP.is_gt, (("ps", t),), ("ft%d" % t,))
+
+    def counts_a():
+        mm(ps[0][:, 0:128], T.qx, T.sx, 192, T.qu2, T.su2, 0, 128, ("qxO", "qu2", "su2"), (("ps", 0),))
+
+    def counts_b():
+        mm(ps[1][:, 0:128], T.qx, T.sx, 0, T.qu2, T.su2, 0, 128, ("qxG", "qu2", "su2"), (("ps", 1),))
+        mm(ps[2][:, 0:128], T.qx, T.sx, 64, T.qu2, T.su2, 0, 128, ("qxO", "qxG", "qu2", "su2"), (("ps", 2),))
+        for t in range(3):
+            compare(t)
+        quant(T.qf, T.sf, 0, 128, T.ft, 0, ("ft0", "ft1", "ft2"), ("qf",))
+        mm(ps[3][:, 0:128], T.qc, T.sct, 0, T.qf, T.sf, 0, 128, ("qc", "qf"), (("ps", 3),))
+
+    def counts_c():
+        tt(T.cm[:, :], ps[3][:, 0:48], T.mk[:, :], OP.mult, (("ps", 3), "mk"), ("cm",))
+        scan(T.cs[:, :], T.kp8[:, :], T.cm[:, :], ("cm", "kp8"), ("cs",))
+
+    counts_a()
+    look(0, T.xk[:, :], ("xk",))
+    fill(T.kp8[:, :], 1.0, ("kp8",))
+    fill(T.bA[:, :], float(IDB + CEN), ("bA0", "bA1", "bA2", "bA3"))
+    h0 = ("hs", 0)
+    ts(T.w1[:, :], T.hs0[:, 15:RING:16], float(IDB), OP.is_ge, (h0,), ("w1",), -320.0, OP.mult)
+    ts(T.w2[:, :], T.hs0[:, 15:RING:16], float(IDB), OP.is_ge, (h0, "s25"), ("w2",), sc(25), OP.mult)
+    ts(T.w3[:, :], T.hs0[:, 15:RING:16], float(DBL), OP.add, (h0,), ("w3",))
+    tt(T.ph[:, 0:26], T.hs0[:, 15:RING:16], T.w1[:, :], OP.add, (h0, "w1"), ("ph0",))
+    tt(T.ph[:, 26:52], T.w3[:, :], T.w2[:, :], OP.add, ("w3", "w2"), ("ph1",))
+    cp(T.bA[:, 0:20], T.hs0[:, 15:NC:16], (h0,), ("bA0",))
+    cp(T.bA[:, 20:46], T.hs0[:, 15:RING:16], (h0,), ("bA1",))
+    for k, h in enumerate((1, 3, 5, 7)):
+        f = (h + 1) % 8
+        dma("Y", "dL", T.bA[GRP * h:GRP * h + GRP, 20:46], T.ph[GRP * (h - 1):GRP * h, 0:26], ("ph0", "bA1"), (("bh", k),))
+        dma("Y", "dL", T.bA[GRP * h:GRP * h + GRP, 46:72], T.ph[GRP * f:GRP * f + GRP, 26:52], ("ph1", "bA2"), (("bh", 4 + k),))
+    ts(T.rt[:, :], T.hs0[:, NC + 15:640:16], 2.0, OP.mult, (h0, "s23"), ("rt",), sc(23), OP.add)
+    look(1, T.xe[:, :], ("xe0", "xe1"))
+    fill(T.kp8[:, 0:48:8], 0.0, ("kp8",))
+    quant(T.qc, T.sct, 0, 128, T.ct, 0, tuple(("ct", k) for k in range(5)), ("qc",))
+    ts(T.pe[:, :], T.hs1[:, 15:640:16], 2.0, OP.mult, (("hs", 1),), ("pe",))
+    for k, h in enumerate((1, 3, 5, 7)):
+        e, f = (h + 1) % 8, (h + 2) % 8
+        dma("Y", "dE", T.lt[GRP * e:GRP * e + GRP, :], T.pe[GRP * h:GRP * h + GRP, 0:20], ("pe",), (("lt", k),))
+        dma("Y", "dE", T.lt[GRP * f:GRP * f + GRP, :], T.pe[GRP * h:GRP * h + GRP, 20:40], ("pe",), (("lt", 4 + k),))
+    counts_b()
+    ts(T.cst[:, :], T.cst[:, :], sc(1), OP.mult, ("c0", "c1", "c2", "c3", "s1"), ("c0",))
+    ts(T.j832[:, :], T.j20[:, :], sc(12), OP.add, ("j20", "s12"), ("j832",))
+    tt(T.jj[:, :], T.jj[:, :], T.cst[:, :], OP.subtract, ("jja", "jjb", "c0"), ("jja",))
+    tt(T.te[:, :], T.rt[:, :], T.j832[:, :], OP.min, ("rt", "j832"), ("te",))
+    ts(T.jj[:, :], T.jj[:, :], sc(0), OP.subtract, ("jja", "s0"), ("jja",))
+    ts(T.mR[:, 72:92], T.rt[:, :], 832.0, OP.is_lt, ("rt",), ("mE",), 2.0, OP.mult)
+    ts(T.jj[:, :], T.jj[:, :], 7, OP.bitwise_and, ("jja",), ("jja",))
+    for b in range(2):
+        quant(T.qe, T.se, 128 * b, 128 * b + 128, T.e1, 3 - b, ("e1",), (("qe", b),))
+    ts(T.mk[:, :], T.jj[:, :], 0.0, OP.is_equal, ("jja",), ("mk",))
+    for b in range(2, 4):
+        quant(T.qe, T.se, 128 * b, 128 * b + 128, T.e1, 3 - b, ("e1",), (("qe", b),))
+    bAt = ("bA0", "bA1", "bA2") + tuple(("bh", k) for k in range(8))
+    ts(T.g1[:, :], T.bA[:, 0:72], float(DBL), OP.is_ge, bAt, ("g1",))
+    ts(T.g2[:, :], T.bA[:, 0:72], float(2 * DBL), OP.is_ge, bAt, ("g2",))
+    ts(T.g3[:, :], T.bA[:, 0:72], float(3 * DBL), OP.is_ge, bAt, ("g3",))
+    ts(T.mR[:, 20:46], T.bA[:, 20:46], float(DBL), OP.is_lt, bAt, ("mA",))
+    tt(T.mL[:, 0:72], T.g1[:, :], T.g2[:, :], OP.subtract, ("g1", "g2"), ("mB",))
+    tt(T.mR[:, 46:72], T.g2[:, 46:72], T.g3[:, 46:72], OP.subtract, ("g2", "g3"), ("mC",))
+    ltt = tuple(("lt", k) for k in range(8))
+
+    cs = lambda k: T.cs[:, 8 * k + 7:8 * k + 8]
+
+    def lists():
+        ts(T.ta[:, 0:72], T.mL[:, 0:72], cs(0), OP.mult, ("mB", "cs"), ("ta0",))
+        act(T.tb[:, 46:72], T.mR[:, 46:72], ("mC", "cs"), ("tb1",), scale=cs(4))
+        act(T.tb[:, 72:92], T.mR[:, 72:92], ("mE", "cs"), ("tb2",), scale=cs(3))
+        ts(T.ta[:, 72:92], T.mL[:, 72:92], cs(1), OP.mult, ("mD", "cs"), ("ta1",))
+        ts(T.tb[:, 20:46], T.mR[:, 20:46], cs(2), OP.mult, ("mA", "cs"), ("tb0",))
+        tt(T.tq[:, :], T.bA[:, :], T.ta[:, :], OP.subtract, bAt + ("bA3", "ta0", "ta1"), ("tq",))
+        tt(T.tq[:, 20:92], T.tq[:, 20:92], T.tb[:, 20:92], OP.subtract, ("tq", "tb0", "tb1", "tb2"), ("tq",))
+        cp(T.oA[:, :], T.tq[:, 0:72], ("tq",), ("oA",))
+        act(T.tab[:, 0:832:2], T.src[:, :].indirect(T.oA[:, 20:46]), srct + ("oA",), ("tab0",))
+        act(T.tab[:, 1:512:2], T.src[:, :].indirect(T.oA[:, 46:62]), srct + ("oA",), ("tab1",))
+        ts(T.tw[:, :], T.tq[:, 72:92], 0.0, OP.is_lt, ("tq",), ("tw",), 832.0, OP.mult)
+        cp(T.tab[:, 832:1152], T.src[:, :].indirect(T.oA[:, 0:20]), srct + ("oA",), ("tab2",))
+        cp(T.tab[:, 513:832:2], T.src[:, :].indirect(T.oA[:, 62:72]), srct + ("oA",), ("tab3",))
+        tt(T.tw[:, :], T.tq[:, 72:92], T.tw[:, :], OP.add, ("tq", "tw"), ("tw",))
+        cp(T.oB[:, :], T.tw[:, :], ("tw",), ("oB",))
+
+    def pick(h):
+        tt(T.bm[:, HALF * h:HALF * h + HALF], T.tab[:, :].indirect(T.oB[:, 10 * h:10 * h + 10]), T.mask[:, 0:HALF], OP.mult, ("tab0", "tab1", "tab2", "tab3", "oB", "mask"), (("bm", h),))
+
+    def fold(h):
+        scan(T.bs[:, HALF * h:HALF * h + HALF], T.keep[:, 0:HALF], T.bm[:, HALF * h:HALF * h + HALF], ("keep", ("bm", h)), (("bs", h),))
+
+    def offsets(h):
+        for t in (2, 0, 3, 1):
+            c = 40 * h + 10 * t
+            ts(T.l4[:, c:c + 10], T.bs[:, HALF * h + 15:HALF * h + HALF:16], float(t), OP.add, (("bs", h),), (("l4", h, t),))
+
+    def gather(h, tile, tok):
+        wt = ("xO", "xG") + tuple((n, k) for n in ("shO", "shG") for k in range(NSH))
+        for t in (2, 0, 3, 1):
+            c = 40 * h + 10 * t
+            src = T.win[:, :].indirect(T.l4[:, c:c + 10])
+            if t >= 2:
+                act(tile[:, t:4 * HALF:4], src, wt + (("l4", h, t),), ((tok, t),))
+            else:
+                cp(tile[:, t:4 * HALF:4], src, wt + (("l4", h, t),), ((tok, t),))
+
+    def unpack(q, s, qt, base, tile, tok, beside=()):
+        for b in range(4):
+            mm(ps[base + b][:, 0:HALF], T.qe, T.se, 128 * b, q, s, 0, HALF, (("qe", b),) + qt, (("ps", base + b),))
+        for b in range(4):
+            if b % 2 == 0 and beside:
+                beside[b // 2]()
+            evac("VS"[b % 2], tile[:, b:4 * HALF:4], ps[base + b][:, 0:HALF], (("ps", base + b),), ((tok, b),), 2.0 ** -5)
+        if beside:
+            beside[2]()
+
+    def first(base, q, s, qt):
+        for b in range(4):
+            mm(ps[base + b][:, 0:HALF], T.qe, T.se, 128 * b, q, s, 0, HALF, (("qe", b),) + qt, (("ps", base + b),), True, False)
+
+    def layer(base, q, s, qt, c0, tok):
+        for b in range(4):
+            mm(ps[base + b][:, 0:HALF], T.wq, T.wsb, 128 * b, q, s, 0, HALF, ("wq", "wsb") + qt, (("ps", base + b),), False, True)
+        for b in range(4):
+            evac("VS"[b % 2], T.win[:, c0 + b:c0 + 4 * HALF:4], ps[base + b][:, 0:HALF], (("ps", base + b),), ((tok, b),), 2.0 ** -5)
+
+    four = lambda t: tuple((t, b) for b in range(4))
+
+    for rd in range(3):
+        last = rd == 2
+        counts_c()
+        if rd == 0:
+            ts(T.mL[:, 72:92], T.lt[:, :], 832.0, OP.is_lt, ltt, ("mD",), 2.0, OP.mult)
+            tt(T.bA[:, 72:92], T.lt[:, :], T.te[:, :], OP.min, ltt + ("te",), ("bA3",))
+        lists()
+        pick(0)
+        fold(0)
+        offsets(0)
+        gather(0, T.gr, "gr")
+        quant(T.q1, T.s1, 0, HALF, T.gr, 0, four("gr"), ("q1",))
+        unpack(T.q1, T.s1, ("q1",), 4, T.gt, "gt", (lambda: pick(1), lambda: fold(1), lambda: offsets(1)))
+        quant(T.q2, T.s2, 0, HALF, T.gt, 0, four("gt"), ("q2",))
+        dst = T.cores[rank ^ MASKS[rd]]
+        rid, pid = topo.addr(dst)[0], topo.addr(dst)[1]
+        ne, mask = len(topo.engines(core, dst)), topo.mask(core, dst)
+        arr = "arr%d" % rd
+        gate("G", ("q2",), ())
+        g.remote_dma(T["lc%d" % rd][:, :].bitcast(dt.uint8), T.q2[:, :].bitcast(dt.uint8), T.sem[arr], T.sem.sent, pid, rid, mask)
+        g.remote_dma(T["ls%d" % rd][:, :], T.s2[:, :], T.sem[arr], T.sem.sent, pid, rid, mask)
+        total["sent"] += 2 * ne
+        total[arr] += 2 * ne
+        mark("G", "sent", total["sent"], ("q2",), ())
+        land = ("land", rd)
+        writer[land] = [(arr, 2 * ne, {}, "R")]
+        gather(1, T.ow, "ow")
+        quant(T.qo, T.so, 0, HALF, T.ow, 0, four("ow"), ("qo",))
+        unpack(T.qo, T.so, ("qo",), 0, T.zo, "zo")
+        first(0, T.qo, T.so, ("qo",))
+        quant(T.qzo, T.szo, 0, HALF, T.zo, 0, four("zo"), ("qzo",))
+        layer(0, T.qzo, T.szo, ("qzo",), 4 * (CEN + HALF), "xo")
+        writer["xO"], reader["xO"] = sum([writer[("xo", b)] for b in range(4)], []), []
+        if not last:
+            gate("Y", ("xO",), tuple(("shO", k) for k in range(NSH)))
+            for k, (p0, p1, q0, c, n) in enumerate(shifts(HALF, NC)):
+                dma("Y", "shO", T.win[p0:p1, c:c + n], T.win[q0:q0 + p1 - p0, 4 * (CEN + HALF):4 * (CEN + NC)], ("xO",), (("shO", k),))
+        unpack(T["lc%d" % rd], T["ls%d" % rd], (land,), 4, T.zg, "zg")
+        first(4, T["lc%d" % rd], T["ls%d" % rd], (land,))
+        quant(T.qzg, T.szg, 0, HALF, T.zg, 0, four("zg"), ("qzg",))
+        quant(T.qx, T.sx, HALF, NC, T.win, 4 * (CEN + HALF), ("xO",), ("qxO",))
+        act(T.acs[:, rd:rd + 1], cs(5), ("cs",), (("ac", rd),))
+        if rd == 0:
+            quant(T.qv, T.sv, 0, 128, T.vt, 0, ("vt",), ("qv",))
+        layer(4, T.qzg, T.szg, ("qzg",), 4 * CEN, "xg")
+        writer["xG"], reader["xG"] = sum([writer[("xg", b)] for b in range(4)], []), []
+        if last:
+            dma("Y", "dOut", T.oc[:, 4 * HALF:4 * NC], T.qx[:, HALF:NC].bitcast(dt.uint8), ("qxO",), ("oco",))
+            for k in range(4):
+                dma("Y", "dOut", T.osc[4 * k:4 * k + 4, HALF:NC], T.sx[32 * k:32 * k + 4, HALF:NC], ("qxO",), (("oso", k),))
+            dma("Y", "dOut", T.ac[:, :], T.acs[0:128:16, 0:3], (("ac", 0), ("ac", 1), ("ac", 2)), ("aco",))
+            mm(ps[0][:, 0:HALF], T.qv, T.sv, 0, T.qx, T.sx, HALF, HALF, ("qv", "qxO"), (("ps", 0),))
+            act(T.yt[:, HALF:NC], ps[0][:, 0:HALF], (("ps", 0),), ("yO",))
+            dma("Y", "dOut", T.y[:, HALF:NC], T.yt[:, HALF:NC], ("yO",), ("you",))
+        else:
+            counts_a()
+        if not last:
+            gate("Y", ("xG",), tuple(("shG", k) for k in range(NSH)))
+            for k, (p0, p1, q0, c, n) in enumerate(shifts(0, HALF)):
+                dma("Y", "shG", T.win[p0:p1, c:c + n], T.win[q0:q0 + p1 - p0, 4 * CEN:4 * (CEN + HALF)], ("xG",), (("shG", k),))
+        quant(T.qx, T.sx, 0, HALF, T.win, 4 * CEN, ("xG",), ("qxG",))
+        if last:
+            dma("Y", "dOut", T.oc[:, 0:4 * HALF], T.qx[:, 0:HALF].bitcast(dt.uint8), ("qxG",), ("ocg",))
+            for k in range(4):
+                dma("S", "dOut", T.osc[4 * k:4 * k + 4, 0:HALF], T.sx[32 * k:32 * k + 4, 0:HALF], ("qxG",), (("osg", k),))
+            mm(ps[1][:, 0:HALF], T.qv, T.sv, 0, T.qx, T.sx, 0, HALF, ("qv", "qxG"), (("ps", 1),))
+            cp(T.yt[:, 0:HALF], ps[1][:, 0:HALF], (("ps", 1),), ("yG",))
+            dma("Y", "dOut", T.y[:, 0:HALF], T.yt[:, 0:HALF], ("yG",), ("yog",))
+        else:
+            counts_b()
+    for s in SEMAPHORES:
+        if total[s] and known["Y"].get(s, 0) < total[s]:
+            g.sync.wait_ge(T.sem[s], total[s])

@@ -6,60 +6,33 @@ MASKS = (1, 2, 3)
 NC, HALF, GRP, RING, DBL = 320, 160, 16, 416, 736
 CEN = 7 * NC
 WINC = 15 * NC
-IDB = 3 * DBL
-INV = WINC
-ABS = 2500
+OWN = 3 * DBL
+MO = 5 * DBL
+EB, EW = WINC, 1080
+IDB = 4 * DBL
+UI = 1920
+BIG = 1.0e6
+B = 8192.0
+NP = 88
 OP = AluOpType
 FN = ActivationFunctionType
+F32, BF16, I32, U16, U8, X4 = "float32", "bfloat16", "int32", "uint16", "uint8", "float8_e4m3fn_x4"
 
-SCRATCH = {
-    "win": ("sbuf", [128, 4 * WINC], "bfloat16"),
-    "map": ("sbuf", [128, 2 * WINC], "float32"),
-    "src": ("sbuf", [128, IDB + WINC], "float32"),
-    "idt": ("sbuf", [128, 2560], "float32"),
-    "iv1": ("sbuf", [128, RING], "float32"), "iv2": ("sbuf", [128, RING], "float32"),
-    "ri": ("sbuf", [128, 130], "int32"), "eu": ("sbuf", [128, 78], "uint16"), "xu": ("sbuf", [128, 52], "uint16"),
-    "kl": ("sbuf", [128, 40], "int32"), "xk": ("sbuf", [128, 40], "uint16"), "xe": ("sbuf", [128, 40], "uint16"),
-    "pI": ("sbuf", [128, 8], "int32"), "gI": ("sbuf", [128, 8], "int32"), "pr": ("sbuf", [128, 8], "int32"), "p7": ("sbuf", [128, 8], "int32"),
-    "kI": ("sbuf", [128, 8], "int32"), "ul": ("sbuf", [128, 8], "uint16"),
-    "sc": ("sbuf", [128, 32], "float32"),
-    "jj": ("sbuf", [128, 48], "int32"), "cst": ("sbuf", [128, 48], "int32"), "mk": ("sbuf", [128, 48], "float32"), "kp8": ("sbuf", [128, 48], "float32"),
-    "jm": ("sbuf", [128, 640], "float32"), "jd": ("sbuf", [128, 640], "float32"), "mask": ("sbuf", [128, 640], "float32"), "keep": ("sbuf", [128, 640], "float32"),
-    "j20": ("sbuf", [128, 20], "float32"), "j832": ("sbuf", [128, 20], "float32"),
-    "hm0": ("sbuf", [128, 640], "float32"), "hs0": ("sbuf", [128, 640], "float32"),
-    "hm1": ("sbuf", [128, 640], "float32"), "hs1": ("sbuf", [128, 640], "float32"),
-    "ph": ("sbuf", [128, 52], "float32"), "pe": ("sbuf", [128, 40], "float32"), "lt": ("sbuf", [128, 20], "float32"), "rt": ("sbuf", [128, 20], "float32"),
-    "w1": ("sbuf", [128, 26], "float32"), "w2": ("sbuf", [128, 26], "float32"), "w3": ("sbuf", [128, 26], "float32"), "w4": ("sbuf", [128, 26], "float32"),
-    "bA": ("sbuf", [128, 92], "float32"), "mL": ("sbuf", [128, 92], "float32"), "mR": ("sbuf", [128, 92], "float32"),
-    "g1": ("sbuf", [128, 72], "float32"), "g2": ("sbuf", [128, 72], "float32"), "g3": ("sbuf", [128, 72], "float32"),
-    "ta": ("sbuf", [128, 92], "float32"), "tb": ("sbuf", [128, 92], "float32"), "tq": ("sbuf", [128, 92], "float32"), "tw": ("sbuf", [128, 20], "float32"), "te": ("sbuf", [128, 20], "float32"),
-    "oA": ("sbuf", [128, 72], "uint16"), "oB": ("sbuf", [128, 20], "uint16"), "l4": ("sbuf", [128, 80], "uint16"),
-    "tab": ("sbuf", [128, 1152], "float32"),
-    "bm": ("sbuf", [128, 2 * HALF], "float32"), "bs": ("sbuf", [128, 2 * HALF], "float32"),
-    "cm": ("sbuf", [128, 48], "float32"), "cs": ("sbuf", [128, 48], "float32"), "acs": ("sbuf", [128, 4], "float32"),
-    "ew": ("sbuf", [128, 516], "bfloat16"), "e1": ("sbuf", [128, 516], "bfloat16"), "e32": ("sbuf", [128, 516], "bfloat16"),
-    "qe": ("sbuf", [128, 1024], "float8_e4m3fn_x4"), "se": ("sbuf", [128, 1024], "uint8"),
-    "ct": ("sbuf", [128, 512], "bfloat16"), "qc": ("sbuf", [128, 128], "float8_e4m3fn_x4"), "sct": ("sbuf", [128, 128], "uint8"),
-    "ft": ("sbuf", [128, 512], "bfloat16"), "qf": ("sbuf", [128, 128], "float8_e4m3fn_x4"), "sf": ("sbuf", [128, 128], "uint8"),
-    "ut": ("sbuf", [128, 512], "bfloat16"), "qu": ("sbuf", [128, 128], "float8_e4m3fn_x4"), "su": ("sbuf", [128, 128], "uint8"),
-    "qu2": ("sbuf", [128, 128], "float8_e4m3fn_x4"), "su2": ("sbuf", [128, 128], "uint8"),
-    "vt": ("sbuf", [128, 512], "bfloat16"), "qv": ("sbuf", [128, 128], "float8_e4m3fn_x4"), "sv": ("sbuf", [128, 128], "uint8"),
-    "wq": ("sbuf", [128, 512], "float8_e4m3fn_x4"), "wsb": ("sbuf", [128, 512], "uint8"),
-    "qx": ("sbuf", [128, NC], "float8_e4m3fn_x4"), "sx": ("sbuf", [128, NC], "uint8"),
-    "gr": ("sbuf", [128, 4 * HALF], "bfloat16"), "q1": ("sbuf", [128, HALF], "float8_e4m3fn_x4"), "s1": ("sbuf", [128, HALF], "uint8"),
-    "gt": ("sbuf", [128, 4 * HALF], "bfloat16"), "q2": ("sbuf", [128, HALF], "float8_e4m3fn_x4"), "s2": ("sbuf", [128, HALF], "uint8"),
-    "ow": ("sbuf", [128, 4 * HALF], "bfloat16"), "qo": ("sbuf", [128, HALF], "float8_e4m3fn_x4"), "so": ("sbuf", [128, HALF], "uint8"),
-    "zo": ("sbuf", [128, 4 * HALF], "bfloat16"), "zg": ("sbuf", [128, 4 * HALF], "bfloat16"),
-    "qzo": ("sbuf", [128, HALF], "float8_e4m3fn_x4"), "szo": ("sbuf", [128, HALF], "uint8"),
-    "qzg": ("sbuf", [128, HALF], "float8_e4m3fn_x4"), "szg": ("sbuf", [128, HALF], "uint8"),
-    "yt": ("sbuf", [128, NC], "float32"),
+WIDTHS = {
+    BF16: {"win": 4 * WINC, "ew": 516, "e1": 516, "ct": 512, "ft": 512, "ut": 512, "vt": 512, "gr": 4 * HALF, "gt": 4 * HALF, "ow": 4 * HALF, "zo": 4 * HALF},
+    F32: {"mp": MO + EB + EW, "src": IDB + 4 * NC, "idt": UI + 3 * NC, "st": DBL, "iv1": RING, "iv2": RING, "sc": 32, "y5": 130, "s5": 130, "keep": 130,
+          "j20": 20, "j16": HALF, "j4": HALF, "g16": HALF, "g4": HALF, "p16": HALF, "p4": HALF, "t4": 4, "th": 4, "pl": 80, "mt": 80, "nt": 80, "xc": 80, "xs": 80,
+          "cnt": 8, "df": 4, "r1": NC, "f1": NC, "r2": NC, "f2": NC, "z5": 100, "zs": 100, "acs": 24, "yt": NC},
+    I32: {"ri": 78, "qi": 26, "pI": 8, "pJ": 2, "bi": 32},
+    U16: {"x1": 26, "x2": 26, "x3": 26, "ui": 26, "ul": 8, "o1": 20, "o2": 20, "l4": 80},
+    X4: {"qe": 512, "qc": 128, "qf": 128, "qu": 128, "qu2": 128, "qv": 128, "wq": 512, "qx": NC, "q1": HALF, "q2": HALF, "qo": HALF, "qz": HALF, "lc0": HALF, "lc1": HALF, "lc2": HALF},
+    U8: {"se": 512, "sct": 128, "sf": 128, "su": 128, "su2": 128, "sv": 128, "wsb": 512, "sx": NC, "s1": HALF, "s2": HALF, "so": HALF, "sz": HALF, "ls0": HALF, "ls1": HALF, "ls2": HALF},
 }
-for _r in range(3):
-    SCRATCH["lc%d" % _r] = ("sbuf", [128, HALF], "float8_e4m3fn_x4")
-    SCRATCH["ls%d" % _r] = ("sbuf", [128, HALF], "uint8")
+SCRATCH = {name: ("sbuf", [128, n], t) for t, d in WIDTHS.items() for name, n in d.items()}
 for _b in range(8):
     SCRATCH["ps%d" % _b] = ("psum", [128, 512], "float32")
-SEMAPHORES = ["cV", "cS", "cT", "cG", "dX", "dR", "dQ", "dH", "dU", "dV", "dW", "shO", "shG", "dL", "dE", "dOut", "arr0", "arr1", "arr2", "sent"]
+LOCAL = ("d1", "d2", "d3", "dX", "dU", "dV", "dW", "shO", "shG", "dS", "dF", "dC", "dOut")
+SEMAPHORES = ["cV", "cS", "cT", "cG", "arr0", "arr1", "arr2", "sent"] + list(LOCAL)
 
 
 def shifts(lo, hi):
@@ -87,7 +60,6 @@ def rank_program(g, core, T, topo):
     eng = {"V": g.vector, "S": g.scalar, "T": g.tensor, "G": g, "Y": g.sync}
     own_sem = {"V": "cV", "S": "cS", "T": "cT", "G": "cG"}
     total = {s: 0 for s in SEMAPHORES}
-    local = ("dX", "dR", "dQ", "dH", "dU", "dV", "dW", "shO", "shG", "dL", "dE", "dOut")
     known = {e: {} for e in eng}
     writer, reader = {}, {}
 
@@ -100,12 +72,12 @@ def rank_program(g, core, T, topo):
             need += [x for x in reader.get(t, []) if x[3] != e]
         best = {}
         for sem, val, clk, _ in need:
-            v = total[sem] if sem in local else val
+            v = total[sem] if sem in LOCAL else val
             best[sem] = max(best.get(sem, 0), v)
         clks = {}
         for sem, val, clk, _ in need:
             for s, v in clk.items():
-                if s != sem and s not in local:
+                if s != sem and s not in LOCAL:
                     clks.setdefault(s, []).append((sem, v))
         for sem in best:
             v = best[sem]
@@ -120,10 +92,10 @@ def rank_program(g, core, T, topo):
         for sem in best:
             known[e][sem] = max(known[e].get(sem, 0), best[sem])
 
-    def mark(e, sem, val, r, w):
+    def mark(e, sem, val, r, w, who=None):
         clk = dict(known[e])
         clk[sem] = val
-        x = (sem, val, clk, e)
+        x = (sem, val, clk, who or e)
         for t in w:
             writer[t] = [x]
             reader[t] = []
@@ -137,12 +109,16 @@ def rank_program(g, core, T, topo):
         call().then_inc(T.sem[s], 1)
         mark(e, s, total[s], r, w)
 
-    def dma(e, sem, out, in_, r, w):
-        if sem not in ("shO", "shG"):
+    def dmas(sem, copies, r, w):
+        for e in sorted(set(c[0] for c in copies)):
             gate(e, r, w)
-        total[sem] += 16
-        eng[e].dma_start(out, in_).then_inc(T.sem[sem], 16)
-        mark(e, sem, total[sem], r, w)
+        for e, out, in_ in copies:
+            total[sem] += 16
+            eng[e].dma_start(out, in_).then_inc(T.sem[sem], 16)
+        mark(copies[0][0], sem, total[sem], r, w, "DMA")
+
+    def dma(e, sem, out, in_, r, w):
+        dmas(sem, [(e, out, in_)], r, w)
 
     def ts(out, in0, s1, o1, r, w, s2=None, o2=None):
         if o2 is None:
@@ -165,8 +141,14 @@ def rank_program(g, core, T, topo):
         else:
             op("S", lambda: g.scalar.activation(out, in_, fn or FN.Identity, bias=bias, scale=scale), r, w)
 
-    def scan(out, k, d, r, w):
-        op("V", lambda: g.vector.tensor_tensor_scan(out, k, d, 0.0, OP.mult, OP.add), r, w)
+    def iota(out, pattern, base, step, w):
+        if out is T.pI or out is T.pJ:
+            op("G", lambda: g.iota(out[:, :], pattern, base, step), (), w)
+        else:
+            op("G", lambda: g.iota(out, pattern, base, step, allow_small_or_imprecise_dtypes=True), (), w)
+
+    def scan(out, k, d, r, w, o0=OP.mult, o1=OP.add):
+        op("V", lambda: g.vector.tensor_tensor_scan(out, k, d, 0.0, o0, o1), r, w)
 
     def quant(q, s, a, b, tile, c0, r, w):
         op("V", lambda: g.vector.quantize_mx(q[:, a:b], s[:, a:b], tile[:, c0:c0 + 4 * (b - a)]), r, w)
@@ -174,7 +156,7 @@ def rank_program(g, core, T, topo):
     def mm(out, l, ls, la, m, ms, ma, n, r, w, start=True, stop=True):
         op("T", lambda: g.tensor.matmul_mx(out, l[:, la:la + 128], ls[:, la:la + 128], m[:, ma:ma + n], ms[:, ma:ma + n], start, stop), r, w)
 
-    def evac(e, out, in_, r, w, scale):
+    def move(e, out, in_, r, w, scale=1.0):
         if e == "S":
             act(out, in_, r, w, scale=scale)
         elif scale == 1.0:
@@ -183,129 +165,137 @@ def rank_program(g, core, T, topo):
             ts(out, in_, scale, OP.mult, r, w)
 
     ps = [T["ps%d" % b] for b in range(8)]
-    sc = lambda k: T.sc[:, k:k + 1]
-    NSH = len(shifts(0, NC))
+    rows = lambda h, n=1: slice(GRP * h, GRP * (h + n))
+    names = {}
 
-    def ring(q, sem, k, p0, p1, q0, tok):
-        dma(q, sem, T.ri[p0:p1, 26 * k:26 * k + 26], T.ring[q0:q0 + p1 - p0, :], (), (tok,))
-    for f in (1, 3, 5, 7):
-        ring("S", "dR", 3, GRP * f, GRP * f + GRP, GRP * f, ("l1", f))
-        e = (f + 1) % 8
-        ring("Y", "dR", 3, GRP * e, GRP * e + GRP, GRP * f, ("l1", e))
-    ring("S", "dR", 4, 0, 128 - GRP, GRP, "l2a")
-    ring("Y", "dR", 4, 128 - GRP, 128, 0, "l2b")
-    dma("Y", "dX", T.win[:, 4 * CEN:4 * (CEN + NC)], T.x[:, :], (), ("xO", "xG"))
+    def sc(name):
+        k = names.setdefault(name, len(names))
+        return T.sc[:, k:k + 1]
+
+    def scalar(name, in0, r, s1, o1, s2=None, o2=None):
+        ts(sc(name), in0, s1, o1, r, (name,), s2, o2)
+
+    L1, L2, L3 = T.ri[:, 0:26], T.ri[:, 26:52], T.ri[:, 52:78]
+    dmas("d2", [("YS"[h % 2], T.ri[rows(h), 26:52], T.ring[rows(h | 1), :]) for h in range(8)], (), ("L2",))
+    dmas("d1", [("Y", T.ri[rows(1, 7), 0:26], T.ring[rows(0, 7), :]), ("S", T.ri[rows(0), 0:26], T.ring[rows(7), :])], (), ("L1",))
+    dma("S", "d3", L3, T.ring[:, :], (), ("L3",))
     dma("Y", "dU", T.ut[:, :], T.u[:, :], (), ("ut",))
-    n = 0
-    for k, src in ((0, -1), (1, 1)):
-        for h in range(8):
-            f = (h // 2 * 2 + src) % 8
-            ring("SY"[n % 2], "dQ", k, GRP * h, GRP * h + GRP, GRP * f, ("q", k, h))
-            n += 1
-    ring("S", "dQ", 2, 0, 128 - 2 * GRP, 2 * GRP, "l3a")
-    ring("Y", "dQ", 2, 128 - 2 * GRP, 128, 0, "l3b")
-    qtok = tuple(("q", k, h) for k in range(2) for h in range(8)) + ("l3a", "l3b")
+    dma("Y", "dX", T.win[:, 4 * CEN:4 * (CEN + NC)], T.x[:, :], (), ("xO", "xG"))
+    dmas("shG", [("Y", T.win[p0:p1, c:c + n], T.x[q0:q0 + p1 - p0, :]) for p0, p1, q0, c, n in shifts(0, NC)], (), ("shG", "shO"))
 
-    fl = dict(allow_small_or_imprecise_dtypes=True)
-    op("G", lambda: g.iota(T.pI[:, :], [[0, 8]], 0, 1), (), ("pI",))
-    op("G", lambda: g.iota(T.idt[:, 0:RING], [[1, RING]], 0, 0, **fl), (), ("id0",))
-    op("G", lambda: g.iota(T.j20[:, :], [[16, 20]], 0, 1, **fl), (), ("j20",))
-    op("G", lambda: g.iota(T.jm[:, :], [[0, 40], [1, 16]], 0, 0, **fl), (), ("jm",))
-    op("G", lambda: g.iota(T.jj[:, 0:40], [[1, 5], [1, 8]], 63, 0), (), ("jja",))
-    op("G", lambda: g.iota(T.jj[:, 40:48], [[1, 8]], 64, 0), (), ("jjb",))
-    op("G", lambda: g.iota(T.idt[:, RING:2560], [[1, 2560 - RING]], RING, 0, **fl), (), ("id1",))
-    op("G", lambda: g.iota(T.ew[:, :], [[0, 516]], 32, 0, **fl), (), ("ew",))
-    op("G", lambda: g.affine_select(T.e1[:, :], T.ew[:, :], [[1, 516]], OP.is_equal, 0.0, -3, -4), ("ew",), ("e1",))
-    ts(T.gI[:, :], T.pI[:, :], 4, OP.arith_shift_right, ("pI",), ("gI",))
-    ts(T.kI[:, :], T.pI[:, :], 15, OP.bitwise_and, ("pI",), ("kI",))
-    ts(T.p7[:, :], T.pI[:, :], 7, OP.bitwise_and, ("pI",), ("p7",))
-    ts(T.pr[:, :], T.gI[:, :], 1, OP.bitwise_and, ("gI",), ("pr",))
-    gc, pc = T.gI[:, 0:1], T.pr[:, 0:1]
-    ts(sc(2), gc, -320.0, OP.mult, ("gI",), ("s2",), float(CEN), OP.add)
-    ts(sc(15), gc, 304.0, OP.mult, ("gI",), ("s15",))
-    ts(sc(19), T.kI[:, 0:1], -1.0, OP.mult, ("kI",), ("s19",))
-    ts(sc(20), pc, float(DBL), OP.mult, ("pr",), ("s20",), 320.0, OP.add)
-    ts(sc(21), pc, -float(DBL + 320), OP.mult, ("pr",), ("s21",), float(DBL + 320), OP.add)
-    ts(sc(24), pc, float(INV), OP.mult, ("pr",), ("s24",))
-    ts(T.kl[:, 0:20], T.j20[:, :], sc(15), OP.add, ("j20", "s15"), ("kl0",))
-    tt(sc(14), sc(2), sc(24), OP.add, ("s2", "s24"), ("s14",))
-    tt(sc(16), sc(15), sc(24), OP.add, ("s15", "s24"), ("s16",))
-    ts(sc(7), sc(2), 4.0, OP.mult, ("s2",), ("s7",))
-    ts(T.kl[:, 20:40], T.j20[:, :], sc(16), OP.add, ("j20", "s16"), ("kl1",))
-    cp(sc(0), gc, ("gI",), ("s0",))
-    cp(sc(1), pc, ("pr",), ("s1",))
-    ts(sc(4), gc, -16.0, OP.mult, ("gI",), ("s4",), float(CEN), OP.add)
-    ts(sc(5), gc, 7.0, OP.is_equal, ("gI",), ("s5",), -2560.0, OP.mult)
-    ts(sc(6), pc, float(INV + NC), OP.mult, ("pr",), ("s6",))
-    ts(sc(8), pc, 320.0, OP.mult, ("pr",), ("s8",))
-    tt(sc(9), sc(4), sc(5), OP.add, ("s4", "s5"), ("s9",))
-    ts(sc(12), gc, -16.0, OP.mult, ("gI",), ("s12",), 832.0, OP.add)
-    ts(sc(22), gc, 0.0, OP.is_equal, ("gI",), ("s22",), -2560.0, OP.mult)
-    tt(sc(17), sc(9), sc(6), OP.add, ("s9", "s6"), ("s17",))
-    ts(sc(23), pc, -10000.0, OP.mult, ("pr",), ("s23",), 10001.0, OP.add)
-    ts(sc(25), sc(22), -416.0, OP.add, ("s22",), ("s25",))
-    tt(sc(18), sc(17), sc(8), OP.add, ("s17", "s8"), ("s18",))
-    ts(T.ul[:, :], T.p7[:, :], 16, OP.mult, ("p7",), ("ul",))
-    for h in (0, 2, 4, 6):
-        dma("Y", "dH", T.kl[GRP * h:GRP * h + GRP, 0:26], T.ring[GRP * h:GRP * h + GRP, :], ("kl0", "kl1"), (("kh", h),))
-    klt = ("kl0", "kl1") + tuple(("kh", h) for h in (0, 2, 4, 6))
-    for k, (p0, p1, q0, c, n) in enumerate(shifts(0, NC)):
-        dma("Y", "shG", T.win[p0:p1, c:c + n], T.x[q0:q0 + p1 - p0, :], (), (("shG", k),))
-    dma("Y", "dW", T.wq[:, :].bitcast(dt.uint8), T.wc[:, :], (), ("wq",))
-    dma("Y", "dW", T.wsb[:, :], T.ws[:, :], (), ("wsb",))
-    dma("Y", "dV", T.vt[:, :], T.v[:, :], (), ("vt",))
-    act(T.iv1[:, :], T.idt[:, 0:RING], ("id0", "s20"), ("iv1",), bias=sc(20))
-    act(T.map[:, CEN:CEN + NC], T.idt[:, 0:NC], ("id0",), ("map0",), bias=float(IDB + CEN))
-    for k, c in enumerate((INV + CEN, INV + CEN + 2 * NC, INV + NC)):
-        act(T.map[:, c:c + NC], T.idt[:, 0:NC], ("id0",), ("map%d" % (k + 1),), scale=0.0, bias=float(ABS))
-    act(T.iv2[:, :], T.idt[:, 0:RING], ("id0", "s21"), ("iv2",), bias=sc(21))
-    act(T.jd[:, :], T.jm[:, :], ("jm", "s19"), ("jd",), bias=sc(19), fn=FN.Abs)
-    act(T.mask[:, :], T.jd[:, :], ("jd",), ("mask",), scale=-1.0, bias=1.0, fn=FN.Relu)
-    act(T.keep[:, :], T.jm[:, :], ("jm",), ("keep",), fn=FN.Sign)
-    mapt = tuple("map%d" % k for k in range(4))
-    for k, (p0, p1, t, c) in enumerate(((0, 128, 0, 1.0), (0, 128, 1, 1.0), (0, 64, 2, 0.0), (64, 128, 2, 1.0), (0, 128, 3, 0.0))):
-        act(T.ct[p0:p1, t:512:4], T.idt[p0:p1, 0:128], ("id0",), (("ct", k),), scale=0.0, bias=c)
-    act(T.ft[:, :], T.jm[:, 0:512], ("jm",), ("ft0", "ft1", "ft2"), scale=0.0)
-    fill(T.cst[:, 0:24], -1, ("c0",))
-    fill(T.cst[:, 24:32], 3, ("c1",))
-    fill(T.cst[:, 32:40], 5, ("c2",))
-    fill(T.cst[:, 40:48], 0, ("c3",))
+    iota(T.pI, [[0, 8]], 0, 1, ("pI",))
+    iota(T.pJ, [[128 - GRP, 2]], 0, 1, ("pJ",))
+    iota(T.idt[:, 0:RING], [[1, RING]], 0, 0, ("id0",))
+    iota(T.idt[:, UI:UI + 3 * NC], [[1, 3 * NC]], UI, 0, ("id1",))
+    fill(T.ew[:, :], 32.0, ("ew",))
 
-    l1t = tuple(("l1", h) for h in range(8)) + ("l2a", "l2b")
-    ts(T.xu[:, 0:26], T.ri[:, 78:104], sc(2), OP.add, l1t + ("s2",), ("xu0",))
-    ts(T.xu[:, 26:52], T.ri[:, 104:130], sc(14), OP.add, l1t + ("s14",), ("xu1",))
-
-    def scatter(k, nm):
-        op("V", lambda: g.vector.tensor_copy(T.map[:, 0:2 * WINC].indirect(T.xu[:, 26 * k:26 * k + 26]), T[nm][:, :]), (nm, "xu%d" % k), mapt)
-    scatter(0, "iv1")
-    cp(T.eu[:, :], T.ri[:, 0:78], qtok, ("eu",))
-    quant(T.qu, T.su, 0, 128, T.ut, 0, ("ut",), ("qu",))
-    scatter(1, "iv2")
-    quant(T.qx, T.sx, 0, NC, T.win, 4 * CEN, ("xO", "xG"), ("qxO", "qxG"))
-    op("V", lambda: g.vector.tensor_copy(T.qu2[:, 0:128].bitcast(dt.uint32), T.qu[:, 0:128].bitcast(dt.uint32).indirect(T.ul[:, 0:8])), ("qu", "ul"), ("qu2",))
-    op("V", lambda: g.vector.tensor_copy(T.su2[:, 0:128], T.su[:, 0:128].indirect(T.ul[:, 0:8])), ("qu", "ul"), ("su2",))
-    ts(T.xk[:, :], T.kl[:, :], sc(2), OP.add, klt + ("s2",), ("xk",))
-    ts(T.xe[:, 0:20], T.j20[:, :], sc(17), OP.add, ("j20", "s17"), ("xe0",))
-    ts(T.xe[:, 20:40], T.j20[:, :], sc(18), OP.add, ("j20", "s18"), ("xe1",))
-    act(T.src[:, IDB + CEN - NC:IDB + CEN + 2 * NC], T.idt[:, 0:960], ("id0", "id1"), ("src0",), scale=4.0, bias=float(4 * (CEN - NC)))
-    act(T.src[:, IDB:IDB + NC], T.idt[:, 0:NC], ("id0",), ("src1",), scale=4.0)
+    bi = lambda k, n=1: T.bi[:, k:k + n]
+    p0 = T.pI[:, 0:1]
+    ts(bi(0), p0, 4, OP.arith_shift_right, ("pI",), ("g",))
+    ts(bi(1), p0, 4, OP.arith_shift_right, ("pI",), ("par",), 1, OP.bitwise_and)
+    ts(bi(2, 2), T.pJ[:, :], 5, OP.arith_shift_right, ("pJ",), ("kq",), 3, OP.bitwise_and)
+    gI, par, pair = bi(0), bi(1), bi(2)
+    scalar("c2", gI, ("g",), -320.0, OP.mult, float(CEN), OP.add)
+    scalar("df", gI, ("g",), 160.0, OP.mult, float(IDB), OP.add)
+    names["v2"], names["v1"] = len(names), len(names) + 1
+    ts(T.sc[:, names["v2"]:names["v2"] + 2], bi(2, 2), float(DBL), OP.mult, ("kq",), ("v2", "v1"), 320.0, OP.add)
+    scalar("ui", pair, ("kq",), -640.0, OP.mult, float(UI), OP.add)
+    scalar("uv", pair, ("kq",), 640.0, OP.mult, -float(UI), OP.add)
+    scalar("xa", par, ("par",), 300.0, OP.mult, -320.0, OP.add)
+    scalar("xb", par, ("par",), float(EB + 40 - CEN), OP.mult, float(CEN), OP.add)
+    scalar("th2", gI, ("g",), 320.0, OP.mult)
+    scalar("al", par, ("par",), 19.0, OP.mult, 1.0, OP.add)
+    scalar("be", par, ("par",), -319.0, OP.mult)
+    scalar("w", par, ("par",), 300.0, OP.mult)
+    scalar("c0", gI, ("g", "xa", "xb"), sc("xa"), OP.mult, sc("xb"), OP.add)
+    scalar("th1", sc("th2"), ("th2",), -320.0, OP.add, 640.0, OP.max)
+    fill(T.keep[:, :], 1.0, ("keep",))
+    fill(T.y5[:, :], 0.0, ("y0", "y1", "y2", "y3"))
+    fill(T.pl[:, :], BIG, ("pl",))
+    fill(T.keep[:, 0:130:5], 0.0, ("keep",))
+    act(T.mp[:, MO + CEN:MO + CEN + NC], T.idt[:, 0:NC], ("id0", "df"), ("mapO",), bias=sc("df"))
+    act(T.iv2[:, :], T.idt[:, 0:RING], ("id0", "v2"), ("iv2",), bias=sc("v2"))
     for k in range(3):
-        act(T.src[:, DBL * k:DBL * k + 320], T.idt[:, 0:2560].indirect(T.eu[:, 26 * k + 6:26 * k + 26]), ("id0", "id1", "eu", "s7"), (("sr", k, 0),), scale=4.0, bias=sc(7))
-        act(T.src[:, DBL * k + 320:DBL * k + 736], T.idt[:, 0:2560].indirect(T.eu[:, 26 * k:26 * k + 26]), ("id0", "id1", "eu", "s7"), (("sr", k, 1),), scale=4.0, bias=sc(7))
-    srct = ("src0", "src1") + tuple(("sr", k, i) for k in range(3) for i in range(2))
+        act(T.mp[:, MO + EB + 360 * k:MO + EB + 360 * k + 360], T.idt[:, 0:360], ("id0",), (("mapE", k),), scale=0.0, bias=BIG)
+    act(T.iv1[:, :], T.idt[:, 0:RING], ("id0", "v1"), ("iv1",), bias=sc("v1"))
+    mapE = tuple(("mapE", k) for k in range(3))
 
-    def look(k, off, r):
-        m, s = T["hm%d" % k], T["hs%d" % k]
-        tt(m[:, :], T.map[:, 0:2 * WINC].indirect(off), T.mask[:, :], OP.mult, mapt + ("mask",) + r, (("hm", k),))
-        scan(s[:, :], T.keep[:, :], m[:, :], ("keep", ("hm", k)), (("hs", k),))
+    ts(T.x2[:, :], L2, sc("c2"), OP.add, ("L2", "c2"), ("x2",))
+    ts(T.ui[:, :], L2, sc("ui"), OP.add, ("L2", "ui"), ("uil",))
+    ts(T.qi[:, :], L1, 4, OP.arith_shift_right, ("L1",), ("qi",))
+    ts(T.y5[:, 0:130:5], L1, sc("al"), OP.mult, ("L1", "al", "c0"), ("y0",), sc("c0"), OP.add)
+    ts(T.y5[:, 1:130:5], L1, sc("th1"), OP.is_ge, ("L1", "th1", "w"), ("y1",), sc("w"), OP.mult)
+    ts(T.y5[:, 2:130:5], L1, sc("th2"), OP.is_ge, ("L1", "th2", "w"), ("y2",), sc("w"), OP.mult)
+    ts(T.y5[:, 3:130:5], T.qi[:, :], sc("be"), OP.mult, ("qi", "be"), ("y3",))
+    op("V", lambda: g.vector.tensor_copy(T.mp[:, MO:MO + EB].indirect(T.x2[:, :]), T.iv2[:, :]), ("iv2", "x2"), ("mapO",))
+    scan(T.s5[:, :], T.keep[:, :], T.y5[:, :], ("keep", "y0", "y1", "y2", "y3"), ("s5",))
+    ts(T.x3[:, :], L3, sc("c2"), OP.add, ("L3", "c2"), ("x3",))
+    cp(T.x1[:, :], T.s5[:, 4:130:5], ("s5",), ("x1",))
+    quant(T.qu, T.su, 0, 128, T.ut, 0, ("ut",), ("qu",))
+    op("V", lambda: g.vector.tensor_copy(T.mp[:, MO:MO + EB + EW].indirect(T.x1[:, :]), T.iv1[:, :]), ("iv1", "x1"), ("mapO",) + mapE)
+    win_id = T.idt[:, 0:UI + 3 * NC]
+    act(T.st[:, 0:NC], win_id.indirect(T.ui[:, 6:26]), ("id0", "id1", "uil", "uv"), ("st0",), bias=sc("uv"))
+    act(T.st[:, NC:DBL], win_id.indirect(T.ui[:, 0:26]), ("id0", "id1", "uil", "uv"), ("st1",), bias=sc("uv"))
+    copies = []
+    for k in range(4):
+        for first, n in ((2 * k - 1, 1), (2 * k, 2), (2 * k + 2, 2)):
+            copies.append(("Y", T.src[rows(first % 8, n), DBL * k:DBL * k + DBL], T.st[rows(2 * k, n), :]))
+    dmas("dS", copies, ("st0", "st1"), ("src",))
+    win_o = T.mp[:, MO:MO + EB]
+    cp(T.mp[:, OWN:OWN + NC], win_o.indirect(T.x3[:, 6:26]), ("mapO", "x3"), ("ct0",))
+    act(T.mp[:, OWN + NC:OWN + DBL], win_o.indirect(T.x3[:, 0:26]), ("mapO", "x3"), ("ct1",))
+    copies = []
+    for f in (1, 3, 5, 7):
+        for h in ((f - 2) % 8, f - 1, f):
+            a = MO + EB + 40 - 20 * f + 20 * h + 300 * ((NC * h >= max(NC * (f - 1), 640)) + (h >= f))
+            copies.append(("Y", T.pl[rows(h), 20 * (f // 2):20 * (f // 2) + 20], T.mp[GRP * f:GRP * f + 1, a:a + NC]))
+    dmas("dF", copies, mapE, ("pl",))
+    copies = []
+    for e in (0, 2, 4, 6):
+        for h, a in ((e + 1, OWN), ((e - 1) % 8, OWN + DBL if e else 0)):
+            copies.append(("Y", T.mp[rows(h), a:a + DBL], T.mp[rows(e), OWN:OWN + DBL]))
+    dmas("dC", copies, (), ("ct0", "ct1"))
+    dmas("dW", [("Y", T.wq[:, :].bitcast(dt.uint8), T.wc[:, :]), ("Y", T.wsb[:, :], T.ws[:, :])], (), ("wq",))
+    dma("Y", "dV", T.vt[:, :], T.v[:, :], (), ("vt",))
+
+    iota(T.j20[:, :], [[16, 20]], 0, 1, ("j20",))
+    iota(T.t4[:, :], [[DBL, 4]], DBL, 0, ("t4",))
+    op("G", lambda: g.affine_select(T.e1[:, :], T.ew[:, :], [[1, 516]], OP.is_equal, 0.0, -3, -4), ("ew",), ("e1",))
+    iota(T.j16[:, :], [[0, 10], [1, 16]], 0, 0, ("j16",))
+    iota(T.j4[:, :], [[0, 40], [1, 4]], 0, 0, ("j4",))
+    iota(T.src[:, IDB:IDB + 4 * NC], [[640, 4], [1, NC]], 0, 0, ("idr",))
+    ts(bi(8, 5), T.pI[:, 0:5], 3, OP.bitwise_and, ("pI",), ("p3",))
+    ts(bi(13, 3), T.pI[:, 0:3], 7, OP.bitwise_and, ("pI",), ("p7",))
+    ts(bi(4), p0, 15, OP.bitwise_and, ("pI",), ("k16",))
+    ts(bi(5), p0, 2, OP.arith_shift_right, ("pI",), ("kk",), 3, OP.bitwise_and)
+    ts(T.ul[:, 0:5], bi(8, 5), 32.0, OP.mult, ("p3",), ("ul0",))
+    ts(T.ul[:, 5:8], bi(13, 3), 16.0, OP.mult, ("p7",), ("ul1",))
+    quant(T.qx, T.sx, 0, NC, T.win, 4 * CEN, ("xO", "xG"), ("qxO", "qxG"))
+    op("V", lambda: g.vector.tensor_copy(T.qu2[:, 0:128].bitcast(dt.uint32), T.qu[:, 0:128].bitcast(dt.uint32).indirect(T.ul[:, 0:8])), ("qu", "ul0", "ul1"), ("qu2",))
+    op("S", lambda: g.scalar.activation(T.su2[:, 0:128], T.su[:, 0:128].indirect(T.ul[:, 0:8]), FN.Copy), ("qu", "ul0", "ul1"), ("su2",))
+    fill(T.ft[:, :], 0.0, ("ft0", "ft1", "ft2"))
+    fill(T.ct[:, :], 1.0, ("ct",))
+    scalar("p16", bi(4), ("k16",), -1.0, OP.mult, -0.5, OP.add)
+    scalar("p4", bi(5), ("kk",), -1.0, OP.mult, -0.5, OP.add)
+    fill(T.ct[0:64, 2:512:4], 0.0, ("ct",))
+    scalar("f1", bi(4), ("k16",), -B, OP.mult, 15 * B, OP.add)
+    scalar("fa", bi(5), ("kk",), 4 * B, OP.mult, -12 * B, OP.add)
+    fill(T.ct[:, 3:512:4], 0.0, ("ct",))
+    scalar("fb", sc("c2"), ("c2", "fa"), 4.0, OP.mult, sc("fa"), OP.add)
+    scalar("n", gI, ("g",), -16.0, OP.mult, float(MO + CEN), OP.add)
+    quant(T.qc, T.sct, 0, 128, T.ct, 0, ("ct",), ("qc",))
+    for pat, j, sg, nm in ((T.p16, T.j16, T.g16, "16"), (T.p4, T.j4, T.g4, "4")):
+        act(sg[:, :], j[:, :], ("j" + nm, "p" + nm), ("g" + nm,), bias=sc("p" + nm), fn=FN.Sign)
+    for pat, sg, nm in ((T.p16, T.g16, "16"), (T.p4, T.g4, "4")):
+        act(pat[:, :], sg[:, :], ("g" + nm,), ("P" + nm,), scale=8.5 * B, bias=-7.5 * B)
 
     def compare(t):
-        ts(T.ft[:, t:192:4], ps[t][:, 0:48], 0.0, OP.is_gt, (("ps", t),), ("ft%d" % t,))
+        ts(T.ft[:, t:4 * NP:4], ps[t][:, 0:NP], 0.0, OP.is_gt, (("ps", t),), ("ft%d" % t,))
 
     def counts_a():
         mm(ps[0][:, 0:128], T.qx, T.sx, 192, T.qu2, T.su2, 0, 128, ("qxO", "qu2", "su2"), (("ps", 0),))
 
-    def counts_b():
+    def counts_b(beside=None):
         mm(ps[1][:, 0:128], T.qx, T.sx, 0, T.qu2, T.su2, 0, 128, ("qxG", "qu2", "su2"), (("ps", 1),))
         mm(ps[2][:, 0:128], T.qx, T.sx, 64, T.qu2, T.su2, 0, 128, ("qxO", "qxG", "qu2", "su2"), (("ps", 2),))
         for t in range(3):
@@ -313,96 +303,60 @@ def rank_program(g, core, T, topo):
         quant(T.qf, T.sf, 0, 128, T.ft, 0, ("ft0", "ft1", "ft2"), ("qf",))
         mm(ps[3][:, 0:128], T.qc, T.sct, 0, T.qf, T.sf, 0, 128, ("qc", "qf"), (("ps", 3),))
 
-    def counts_c():
-        tt(T.cm[:, :], ps[3][:, 0:48], T.mk[:, :], OP.mult, (("ps", 3), "mk"), ("cm",))
-        scan(T.cs[:, :], T.kp8[:, :], T.cm[:, :], ("cm", "kp8"), ("cs",))
-
     counts_a()
-    look(0, T.xk[:, :], ("xk",))
-    fill(T.kp8[:, :], 1.0, ("kp8",))
-    fill(T.bA[:, :], float(IDB + CEN), ("bA0", "bA1", "bA2", "bA3"))
-    h0 = ("hs", 0)
-    ts(T.w1[:, :], T.hs0[:, 15:RING:16], float(IDB), OP.is_ge, (h0,), ("w1",), -320.0, OP.mult)
-    ts(T.w2[:, :], T.hs0[:, 15:RING:16], float(IDB), OP.is_ge, (h0, "s25"), ("w2",), sc(25), OP.mult)
-    ts(T.w3[:, :], T.hs0[:, 15:RING:16], float(DBL), OP.add, (h0,), ("w3",))
-    tt(T.ph[:, 0:26], T.hs0[:, 15:RING:16], T.w1[:, :], OP.add, (h0, "w1"), ("ph0",))
-    tt(T.ph[:, 26:52], T.w3[:, :], T.w2[:, :], OP.add, ("w3", "w2"), ("ph1",))
-    cp(T.bA[:, 0:20], T.hs0[:, 15:NC:16], (h0,), ("bA0",))
-    cp(T.bA[:, 20:46], T.hs0[:, 15:RING:16], (h0,), ("bA1",))
-    for k, h in enumerate((1, 3, 5, 7)):
-        f = (h + 1) % 8
-        dma("Y", "dL", T.bA[GRP * h:GRP * h + GRP, 20:46], T.ph[GRP * (h - 1):GRP * h, 0:26], ("ph0", "bA1"), (("bh", k),))
-        dma("Y", "dL", T.bA[GRP * h:GRP * h + GRP, 46:72], T.ph[GRP * f:GRP * f + GRP, 26:52], ("ph1", "bA2"), (("bh", 4 + k),))
-    ts(T.rt[:, :], T.hs0[:, NC + 15:640:16], 2.0, OP.mult, (h0, "s23"), ("rt",), sc(23), OP.add)
-    look(1, T.xe[:, :], ("xe0", "xe1"))
-    fill(T.kp8[:, 0:48:8], 0.0, ("kp8",))
-    quant(T.qc, T.sct, 0, 128, T.ct, 0, tuple(("ct", k) for k in range(5)), ("qc",))
-    ts(T.pe[:, :], T.hs1[:, 15:640:16], 2.0, OP.mult, (("hs", 1),), ("pe",))
-    for k, h in enumerate((1, 3, 5, 7)):
-        e, f = (h + 1) % 8, (h + 2) % 8
-        dma("Y", "dE", T.lt[GRP * e:GRP * e + GRP, :], T.pe[GRP * h:GRP * h + GRP, 0:20], ("pe",), (("lt", k),))
-        dma("Y", "dE", T.lt[GRP * f:GRP * f + GRP, :], T.pe[GRP * h:GRP * h + GRP, 20:40], ("pe",), (("lt", 4 + k),))
     counts_b()
-    ts(T.cst[:, :], T.cst[:, :], sc(1), OP.mult, ("c0", "c1", "c2", "c3", "s1"), ("c0",))
-    ts(T.j832[:, :], T.j20[:, :], sc(12), OP.add, ("j20", "s12"), ("j832",))
-    tt(T.jj[:, :], T.jj[:, :], T.cst[:, :], OP.subtract, ("jja", "jjb", "c0"), ("jja",))
-    tt(T.te[:, :], T.rt[:, :], T.j832[:, :], OP.min, ("rt", "j832"), ("te",))
-    ts(T.jj[:, :], T.jj[:, :], sc(0), OP.subtract, ("jja", "s0"), ("jja",))
-    ts(T.mR[:, 72:92], T.rt[:, :], 832.0, OP.is_lt, ("rt",), ("mE",), 2.0, OP.mult)
-    ts(T.jj[:, :], T.jj[:, :], 7, OP.bitwise_and, ("jja",), ("jja",))
-    for b in range(2):
+    scalar("fin", bi(8), ("p3", "fb"), sc("fb"), OP.add)
+    scalar("adj", pair, ("kq",), -float(DBL), OP.mult, float(OWN), OP.add)
+    fill(T.nt[:, :], 0.0, ("nt",))
+    ts(T.th[:, :], T.t4[:, :], sc("f1"), OP.add, ("t4", "f1"), ("th",))
+    ts(T.nt[:, 0:80:4], T.j20[:, :], sc("n"), OP.add, ("j20", "n"), ("nt",))
+    for r in range(4):
+        ts(T.mt[:, r:80:4], T.pl[:, 20 * r:20 * r + 20], sc("adj"), OP.add, ("pl", "adj"), (("mt", r),))
+    four = lambda t: tuple((t, b) for b in range(4))
+
+    def pack_e(b):
         quant(T.qe, T.se, 128 * b, 128 * b + 128, T.e1, 3 - b, ("e1",), (("qe", b),))
-    ts(T.mk[:, :], T.jj[:, :], 0.0, OP.is_equal, ("jja",), ("mk",))
-    for b in range(2, 4):
-        quant(T.qe, T.se, 128 * b, 128 * b + 128, T.e1, 3 - b, ("e1",), (("qe", b),))
-    bAt = ("bA0", "bA1", "bA2") + tuple(("bh", k) for k in range(8))
-    ts(T.g1[:, :], T.bA[:, 0:72], float(DBL), OP.is_ge, bAt, ("g1",))
-    ts(T.g2[:, :], T.bA[:, 0:72], float(2 * DBL), OP.is_ge, bAt, ("g2",))
-    ts(T.g3[:, :], T.bA[:, 0:72], float(3 * DBL), OP.is_ge, bAt, ("g3",))
-    ts(T.mR[:, 20:46], T.bA[:, 20:46], float(DBL), OP.is_lt, bAt, ("mA",))
-    tt(T.mL[:, 0:72], T.g1[:, :], T.g2[:, :], OP.subtract, ("g1", "g2"), ("mB",))
-    tt(T.mR[:, 46:72], T.g2[:, 46:72], T.g3[:, 46:72], OP.subtract, ("g2", "g3"), ("mC",))
-    ltt = tuple(("lt", k) for k in range(8))
 
-    cs = lambda k: T.cs[:, 8 * k + 7:8 * k + 8]
-
-    def lists():
-        ts(T.ta[:, 0:72], T.mL[:, 0:72], cs(0), OP.mult, ("mB", "cs"), ("ta0",))
-        act(T.tb[:, 46:72], T.mR[:, 46:72], ("mC", "cs"), ("tb1",), scale=cs(4))
-        act(T.tb[:, 72:92], T.mR[:, 72:92], ("mE", "cs"), ("tb2",), scale=cs(3))
-        ts(T.ta[:, 72:92], T.mL[:, 72:92], cs(1), OP.mult, ("mD", "cs"), ("ta1",))
-        ts(T.tb[:, 20:46], T.mR[:, 20:46], cs(2), OP.mult, ("mA", "cs"), ("tb0",))
-        tt(T.tq[:, :], T.bA[:, :], T.ta[:, :], OP.subtract, bAt + ("bA3", "ta0", "ta1"), ("tq",))
-        tt(T.tq[:, 20:92], T.tq[:, 20:92], T.tb[:, 20:92], OP.subtract, ("tq", "tb0", "tb1", "tb2"), ("tq",))
-        cp(T.oA[:, :], T.tq[:, 0:72], ("tq",), ("oA",))
-        act(T.tab[:, 0:832:2], T.src[:, :].indirect(T.oA[:, 20:46]), srct + ("oA",), ("tab0",))
-        act(T.tab[:, 1:512:2], T.src[:, :].indirect(T.oA[:, 46:62]), srct + ("oA",), ("tab1",))
-        ts(T.tw[:, :], T.tq[:, 72:92], 0.0, OP.is_lt, ("tq",), ("tw",), 832.0, OP.mult)
-        cp(T.tab[:, 832:1152], T.src[:, :].indirect(T.oA[:, 0:20]), srct + ("oA",), ("tab2",))
-        cp(T.tab[:, 513:832:2], T.src[:, :].indirect(T.oA[:, 62:72]), srct + ("oA",), ("tab3",))
-        tt(T.tw[:, :], T.tq[:, 72:92], T.tw[:, :], OP.add, ("tq", "tw"), ("tw",))
-        cp(T.oB[:, :], T.tw[:, :], ("tw",), ("oB",))
-
-    def pick(h):
-        tt(T.bm[:, HALF * h:HALF * h + HALF], T.tab[:, :].indirect(T.oB[:, 10 * h:10 * h + 10]), T.mask[:, 0:HALF], OP.mult, ("tab0", "tab1", "tab2", "tab3", "oB", "mask"), (("bm", h),))
+    def lists(rd):
+        cn = lambda k: T.cnt[:, k:k + 1]
+        tt(T.xc[:, :], T.mt[:, :], ps[3][:, 0:80], OP.subtract, four("mt") + (("ps", 3),), ("xc",))
+        cp(T.cnt[:, :], ps[3][:, 80:NP], (("ps", 3),), ("cnt",))
+        scan(T.xs[:, :], T.nt[:, :], T.xc[:, :], ("nt", "xc"), ("xs",), OP.max, OP.min)
+        tt(T.df[:, 0:3], T.cnt[:, 1:6:2], T.cnt[:, 3:8:2], OP.subtract, ("cnt",), ("dfc",))
+        cp(T.o1[:, :], T.xs[:, 3:80:4], ("xs",), ("o1",))
+        if rd == 0:
+            pack_e(0)
+        tab = T.mp[:, 0:MO + EB]
+        for h in range(2):
+            move("VS"[h], T.r1[:, HALF * h:HALF * h + HALF], tab.indirect(T.o1[:, 10 * h:10 * h + 10]), ("o1", "mapO", "ct0", "ct1"), (("r1", h),))
+        act(T.acs[:, rd:24:3], T.cnt[:, :], ("cnt",), (("ac", rd),))
+        if rd == 0:
+            pack_e(1)
+        for h in range(2):
+            scan(T.f1[:, HALF * h:HALF * h + HALF], T.p16[:, :], T.r1[:, HALF * h:HALF * h + HALF], ("P16", ("r1", h)), (("f1", h),), OP.add, OP.max)
+        if rd == 0:
+            pack_e(2)
+        x, xt = T.f1[:, 15:NC:16], (("f1", 0), ("f1", 1))
+        ts(T.z5[:, 0:100:5], x, sc("f1"), OP.subtract, xt + ("f1", "cnt"), (("z", 0),), cn(1), OP.subtract)
+        for q in range(4):
+            ts(T.z5[:, q + 1:100:5], x, T.th[:, q:q + 1], OP.is_ge, xt + ("th", "dfc", "cnt"), (("z", q + 1),), T.df[:, q:q + 1] if q < 3 else cn(7), OP.mult)
+        scan(T.zs[:, :], T.keep[:, 0:100], T.z5[:, :], ("keep",) + tuple(("z", q) for q in range(5)), ("zs",))
+        if rd == 0:
+            pack_e(3)
+        cp(T.o2[:, :], T.zs[:, 4:100:5], ("zs",), ("o2",))
+        for h in range(2):
+            move("VS"[h], T.r2[:, HALF * h:HALF * h + HALF], T.src[:, :].indirect(T.o2[:, 10 * h:10 * h + 10]), ("o2", "src", "idr"), (("r2", h),))
 
     def fold(h):
-        scan(T.bs[:, HALF * h:HALF * h + HALF], T.keep[:, 0:HALF], T.bm[:, HALF * h:HALF * h + HALF], ("keep", ("bm", h)), (("bs", h),))
+        scan(T.f2[:, HALF * h:HALF * h + HALF], T.p4[:, :], T.r2[:, HALF * h:HALF * h + HALF], ("P4", ("r2", h)), (("f2", h),), OP.add, OP.max)
 
     def offsets(h):
-        for t in (2, 0, 3, 1):
-            c = 40 * h + 10 * t
-            ts(T.l4[:, c:c + 10], T.bs[:, HALF * h + 15:HALF * h + HALF:16], float(t), OP.add, (("bs", h),), (("l4", h, t),))
+        ts(T.l4[:, 40 * h:40 * h + 40], T.f2[:, HALF * h + 3:HALF * h + HALF:4], 4.0, OP.mult, (("f2", h), "fin"), (("l4", h),), sc("fin"), OP.add)
 
     def gather(h, tile, tok):
-        wt = ("xO", "xG") + tuple((n, k) for n in ("shO", "shG") for k in range(NSH))
-        for t in (2, 0, 3, 1):
-            c = 40 * h + 10 * t
-            src = T.win[:, :].indirect(T.l4[:, c:c + 10])
-            if t >= 2:
-                act(tile[:, t:4 * HALF:4], src, wt + (("l4", h, t),), ((tok, t),))
-            else:
-                cp(tile[:, t:4 * HALF:4], src, wt + (("l4", h, t),), ((tok, t),))
+        for k in range(2):
+            c = 40 * h + 20 * k
+            move("VS"[k], tile[:, NC * k:NC * k + NC], T.win[:, :].indirect(T.l4[:, c:c + 20]), ("xO", "xG", "shO", "shG", ("l4", h)), ((tok, k),))
 
     def unpack(q, s, qt, base, tile, tok, beside=()):
         for b in range(4):
@@ -410,90 +364,84 @@ def rank_program(g, core, T, topo):
         for b in range(4):
             if b % 2 == 0 and beside:
                 beside[b // 2]()
-            evac("VS"[b % 2], tile[:, b:4 * HALF:4], ps[base + b][:, 0:HALF], (("ps", base + b),), ((tok, b),), 2.0 ** -5)
-        if beside:
-            beside[2]()
+            move("VS"[b % 2], tile[:, b:4 * HALF:4], ps[base + b][:, 0:HALF], (("ps", base + b),), ((tok, b),), 2.0 ** -5)
 
-    def first(base, q, s, qt):
+    def first(base, b, q, s, qt):
+        mm(ps[base + b][:, 0:HALF], T.qe, T.se, 128 * b, q, s, 0, HALF, (("qe", b),) + qt, (("ps", base + b),), True, False)
+
+    def layer(base, b, q, s, qt):
+        tok = ("ps", base + b)
+        writer[tok] = [x for x in writer[tok] if x[0] != "cT"]
+        mm(ps[base + b][:, 0:HALF], T.wq, T.wsb, 128 * b, q, s, 0, HALF, ("wq",) + qt, (tok,), False, True)
+
+    def state(base, c0, tok):
+        gate("V", (), (tok,))
+        gate("S", (), (tok,))
         for b in range(4):
-            mm(ps[base + b][:, 0:HALF], T.qe, T.se, 128 * b, q, s, 0, HALF, (("qe", b),) + qt, (("ps", base + b),), True, False)
+            move("VS"[b % 2], T.win[:, c0 + b:c0 + 4 * HALF:4], ps[base + b][:, 0:HALF], (("ps", base + b),), ((tok + "b", b),), 2.0 ** -5)
+        writer[tok], reader[tok] = sum([writer[(tok + "b", b)] for b in range(4)], []), []
 
-    def layer(base, q, s, qt, c0, tok):
-        for b in range(4):
-            mm(ps[base + b][:, 0:HALF], T.wq, T.wsb, 128 * b, q, s, 0, HALF, ("wq", "wsb") + qt, (("ps", base + b),), False, True)
-        for b in range(4):
-            evac("VS"[b % 2], T.win[:, c0 + b:c0 + 4 * HALF:4], ps[base + b][:, 0:HALF], (("ps", base + b),), ((tok, b),), 2.0 ** -5)
+    def spread(lo, hi, sem, tok):
+        dmas(sem, [("Y", T.win[p0:p1, c:c + n], T.win[q0:q0 + p1 - p0, 4 * (CEN + lo):4 * (CEN + hi)]) for p0, p1, q0, c, n in shifts(lo, hi)], (tok,), (sem,))
 
-    four = lambda t: tuple((t, b) for b in range(4))
+    def store(lo, tok, bank, e):
+        dma("Y", "dOut", T.oc[:, 4 * lo:4 * (lo + HALF)], T.qx[:, lo:lo + HALF].bitcast(dt.uint8), (tok,), ())
+        mm(ps[bank][:, 0:HALF], T.qv, T.sv, 0, T.qx, T.sx, lo, HALF, ("qv", tok), (("ps", bank),))
+        dmas("dOut", [(e, T.osc[4 * k:4 * k + 4, lo:lo + HALF], T.sx[32 * k:32 * k + 4, lo:lo + HALF]) for k in range(4)], (tok,), ())
+        move("VS"[e == "Y"], T.yt[:, lo:lo + HALF], ps[bank][:, 0:HALF], (("ps", bank),), (("y", lo),))
+        dma("Y", "dOut", T.y[:, lo:lo + HALF], T.yt[:, lo:lo + HALF], (("y", lo),), ())
 
+    two = lambda t: ((t, 0), (t, 1))
     for rd in range(3):
         last = rd == 2
-        counts_c()
-        if rd == 0:
-            ts(T.mL[:, 72:92], T.lt[:, :], 832.0, OP.is_lt, ltt, ("mD",), 2.0, OP.mult)
-            tt(T.bA[:, 72:92], T.lt[:, :], T.te[:, :], OP.min, ltt + ("te",), ("bA3",))
-        lists()
-        pick(0)
+        lists(rd)
         fold(0)
         offsets(0)
         gather(0, T.gr, "gr")
-        quant(T.q1, T.s1, 0, HALF, T.gr, 0, four("gr"), ("q1",))
-        unpack(T.q1, T.s1, ("q1",), 4, T.gt, "gt", (lambda: pick(1), lambda: fold(1), lambda: offsets(1)))
+        quant(T.q1, T.s1, 0, HALF, T.gr, 0, two("gr"), ("q1",))
+        unpack(T.q1, T.s1, ("q1",), 4, T.gt, "gt", (lambda: fold(1), lambda: offsets(1)))
         quant(T.q2, T.s2, 0, HALF, T.gt, 0, four("gt"), ("q2",))
         dst = T.cores[rank ^ MASKS[rd]]
         rid, pid = topo.addr(dst)[0], topo.addr(dst)[1]
         ne, mask = len(topo.engines(core, dst)), topo.mask(core, dst)
         arr = "arr%d" % rd
+        lc, ls = T["lc%d" % rd], T["ls%d" % rd]
         gate("G", ("q2",), ())
-        g.remote_dma(T["lc%d" % rd][:, :].bitcast(dt.uint8), T.q2[:, :].bitcast(dt.uint8), T.sem[arr], T.sem.sent, pid, rid, mask)
-        g.remote_dma(T["ls%d" % rd][:, :], T.s2[:, :], T.sem[arr], T.sem.sent, pid, rid, mask)
+        g.remote_dma(lc[:, :].bitcast(dt.uint8), T.q2[:, :].bitcast(dt.uint8), T.sem[arr], T.sem.sent, pid, rid, mask)
+        g.remote_dma(ls[:, :], T.s2[:, :], T.sem[arr], T.sem.sent, pid, rid, mask)
         total["sent"] += 2 * ne
         total[arr] += 2 * ne
         mark("G", "sent", total["sent"], ("q2",), ())
         land = ("land", rd)
         writer[land] = [(arr, 2 * ne, {}, "R")]
         gather(1, T.ow, "ow")
-        quant(T.qo, T.so, 0, HALF, T.ow, 0, four("ow"), ("qo",))
+        quant(T.qo, T.so, 0, HALF, T.ow, 0, two("ow"), ("qo",))
         unpack(T.qo, T.so, ("qo",), 0, T.zo, "zo")
-        first(0, T.qo, T.so, ("qo",))
-        quant(T.qzo, T.szo, 0, HALF, T.zo, 0, four("zo"), ("qzo",))
-        layer(0, T.qzo, T.szo, ("qzo",), 4 * (CEN + HALF), "xo")
-        writer["xO"], reader["xO"] = sum([writer[("xo", b)] for b in range(4)], []), []
-        if not last:
-            gate("Y", ("xO",), tuple(("shO", k) for k in range(NSH)))
-            for k, (p0, p1, q0, c, n) in enumerate(shifts(HALF, NC)):
-                dma("Y", "shO", T.win[p0:p1, c:c + n], T.win[q0:q0 + p1 - p0, 4 * (CEN + HALF):4 * (CEN + NC)], ("xO",), (("shO", k),))
-        unpack(T["lc%d" % rd], T["ls%d" % rd], (land,), 4, T.zg, "zg")
-        first(4, T["lc%d" % rd], T["ls%d" % rd], (land,))
-        quant(T.qzg, T.szg, 0, HALF, T.zg, 0, four("zg"), ("qzg",))
-        quant(T.qx, T.sx, HALF, NC, T.win, 4 * (CEN + HALF), ("xO",), ("qxO",))
-        act(T.acs[:, rd:rd + 1], cs(5), ("cs",), (("ac", rd),))
+        for b in range(4):
+            first(0, b, T.qo, T.so, ("qo",))
+        quant(T.qz, T.sz, 0, HALF, T.zo, 0, four("zo"), ("qz",))
         if rd == 0:
             quant(T.qv, T.sv, 0, 128, T.vt, 0, ("vt",), ("qv",))
-        layer(4, T.qzg, T.szg, ("qzg",), 4 * CEN, "xg")
-        writer["xG"], reader["xG"] = sum([writer[("xg", b)] for b in range(4)], []), []
+        for b in range(4):
+            layer(0, b, T.qz, T.sz, ("qz",))
+        state(0, 4 * (CEN + HALF), "xO")
+        if not last:
+            spread(HALF, NC, "shO", "xO")
+        quant(T.qx, T.sx, HALF, NC, T.win, 4 * (CEN + HALF), ("xO",), ("qxO",))
+        for b in range(4):
+            first(4, b, lc, ls, (land,))
+            layer(4, b, lc, ls, (land,))
         if last:
-            dma("Y", "dOut", T.oc[:, 4 * HALF:4 * NC], T.qx[:, HALF:NC].bitcast(dt.uint8), ("qxO",), ("oco",))
-            for k in range(4):
-                dma("Y", "dOut", T.osc[4 * k:4 * k + 4, HALF:NC], T.sx[32 * k:32 * k + 4, HALF:NC], ("qxO",), (("oso", k),))
-            dma("Y", "dOut", T.ac[:, :], T.acs[0:128:16, 0:3], (("ac", 0), ("ac", 1), ("ac", 2)), ("aco",))
-            mm(ps[0][:, 0:HALF], T.qv, T.sv, 0, T.qx, T.sx, HALF, HALF, ("qv", "qxO"), (("ps", 0),))
-            act(T.yt[:, HALF:NC], ps[0][:, 0:HALF], (("ps", 0),), ("yO",))
-            dma("Y", "dOut", T.y[:, HALF:NC], T.yt[:, HALF:NC], ("yO",), ("you",))
+            dma("Y", "dOut", T.ac[:, :], T.acs[0:1, 0:24], (("ac", 0), ("ac", 1), ("ac", 2)), ())
+            store(HALF, "qxO", 0, "Y")
         else:
             counts_a()
+        state(4, 4 * CEN, "xG")
         if not last:
-            gate("Y", ("xG",), tuple(("shG", k) for k in range(NSH)))
-            for k, (p0, p1, q0, c, n) in enumerate(shifts(0, HALF)):
-                dma("Y", "shG", T.win[p0:p1, c:c + n], T.win[q0:q0 + p1 - p0, 4 * CEN:4 * (CEN + HALF)], ("xG",), (("shG", k),))
+            spread(0, HALF, "shG", "xG")
         quant(T.qx, T.sx, 0, HALF, T.win, 4 * CEN, ("xG",), ("qxG",))
         if last:
-            dma("Y", "dOut", T.oc[:, 0:4 * HALF], T.qx[:, 0:HALF].bitcast(dt.uint8), ("qxG",), ("ocg",))
-            for k in range(4):
-                dma("S", "dOut", T.osc[4 * k:4 * k + 4, 0:HALF], T.sx[32 * k:32 * k + 4, 0:HALF], ("qxG",), (("osg", k),))
-            mm(ps[1][:, 0:HALF], T.qv, T.sv, 0, T.qx, T.sx, 0, HALF, ("qv", "qxG"), (("ps", 1),))
-            cp(T.yt[:, 0:HALF], ps[1][:, 0:HALF], (("ps", 1),), ("yG",))
-            dma("Y", "dOut", T.y[:, 0:HALF], T.yt[:, 0:HALF], ("yG",), ("yog",))
+            store(0, "qxG", 1, "S")
         else:
             counts_b()
     for s in SEMAPHORES:

@@ -8,7 +8,7 @@ CEN = 7 * NC
 WINC = 15 * NC
 OWN = 3 * DBL
 MO = 5 * DBL
-EB, EW = WINC, 1080
+EW = 1080
 IDB = 4 * DBL
 UI = 1920
 BIG = 1.0e6
@@ -19,19 +19,19 @@ FN = ActivationFunctionType
 F32, BF16, I32, U16, U8, X4 = "float32", "bfloat16", "int32", "uint16", "uint8", "float8_e4m3fn_x4"
 
 WIDTHS = {
-    BF16: {"win": 4 * WINC, "ew": 516, "e1": 516, "ct": 512, "ft": 512, "ut": 512, "vt": 512, "gr": 4 * HALF, "gt": 4 * HALF, "ow": 4 * HALF, "zo": 4 * HALF},
-    F32: {"mp": MO + EB + EW, "src": IDB + 4 * NC, "idt": UI + 3 * NC, "st": DBL, "iv1": RING, "iv2": RING, "sc": 32, "y5": 130, "s5": 130, "keep": 130,
+    BF16: {"win": 4 * WINC, "xt": 4 * NC, "ew": 516, "e1": 516, "ct": 512, "ft": 512, "ut": 512, "vt": 512, "gt": 4 * HALF, "zo": 4 * HALF, "z32": 4 * HALF},
+    F32: {"mp": MO + WINC, "src": IDB + 4 * NC, "idt": UI + 3 * NC, "st": DBL, "iv": RING, "sc": 32, "bf": 8, "y5": 130, "s5": 130, "keep": 130,
           "j20": 20, "j16": HALF, "j4": HALF, "g16": HALF, "g4": HALF, "p16": HALF, "p4": HALF, "t4": 4, "th": 4, "pl": 80, "mt": 80, "nt": 80, "xc": 80, "xs": 80,
-          "cnt": 8, "df": 4, "r1": NC, "f1": NC, "r2": NC, "f2": NC, "z5": 100, "zs": 100, "acs": 24, "yt": NC},
-    I32: {"ri": 78, "qi": 26, "pI": 8, "pJ": 2, "bi": 32},
-    U16: {"x1": 26, "x2": 26, "x3": 26, "ui": 26, "ul": 8, "o1": 20, "o2": 20, "l4": 80},
-    X4: {"qe": 512, "qc": 128, "qf": 128, "qu": 128, "qu2": 128, "qv": 128, "wq": 512, "qx": NC, "q1": HALF, "q2": HALF, "qo": HALF, "qz": HALF, "lc0": HALF, "lc1": HALF, "lc2": HALF},
-    U8: {"se": 512, "sct": 128, "sf": 128, "su": 128, "su2": 128, "sv": 128, "wsb": 512, "sx": NC, "s1": HALF, "s2": HALF, "so": HALF, "sz": HALF, "ls0": HALF, "ls1": HALF, "ls2": HALF},
+          "cnt": 8, "df": 4, "r1": NC, "f1": NC, "r2": NC, "f2": NC, "z5": 100, "zs": 100, "acs": 24, "sm": 4 * HALF, "yt": NC},
+    I32: {"ri": 56, "qi": 26, "pI": 8, "bi": 32},
+    U16: {"x1": 26, "x3": 26, "ui": 26, "ul": 8, "o1": 20, "o2": 20, "l4": 80},
+    X4: {"qe": 512, "qc": 128, "qf": 128, "qu": 128, "qu2": 128, "qv": 128, "wq": 512, "qx": NC, "q2": HALF, "qz": HALF, "lc0": HALF, "lc1": HALF, "lc2": HALF},
+    U8: {"se": 512, "sct": 128, "sf": 128, "su": 128, "su2": 128, "sv": 128, "wsb": 512, "sx": NC, "s2": HALF, "sz": HALF, "ls0": HALF, "ls1": HALF, "ls2": HALF},
 }
 SCRATCH = {name: ("sbuf", [128, n], t) for t, d in WIDTHS.items() for name, n in d.items()}
 for _b in range(8):
     SCRATCH["ps%d" % _b] = ("psum", [128, 512], "float32")
-LOCAL = ("d1", "d2", "d3", "dX", "dU", "dV", "dW", "shO", "shG", "dS", "dF", "dC", "dOut")
+LOCAL = ("d2", "d3", "dB", "dX", "dU", "dV", "dW", "shO", "shG", "dS", "dM", "dF", "dC", "dOut")
 SEMAPHORES = ["cV", "cS", "cT", "cG", "arr0", "arr1", "arr2", "sent"] + list(LOCAL)
 
 
@@ -142,10 +142,7 @@ def rank_program(g, core, T, topo):
             op("S", lambda: g.scalar.activation(out, in_, fn or FN.Identity, bias=bias, scale=scale), r, w)
 
     def iota(out, pattern, base, step, w):
-        if out is T.pI or out is T.pJ:
-            op("G", lambda: g.iota(out[:, :], pattern, base, step), (), w)
-        else:
-            op("G", lambda: g.iota(out, pattern, base, step, allow_small_or_imprecise_dtypes=True), (), w)
+        op("G", lambda: g.iota(out, pattern, base, step, allow_small_or_imprecise_dtypes=True), (), w)
 
     def scan(out, k, d, r, w, o0=OP.mult, o1=OP.add):
         op("V", lambda: g.vector.tensor_tensor_scan(out, k, d, 0.0, o0, o1), r, w)
@@ -166,6 +163,9 @@ def rank_program(g, core, T, topo):
 
     ps = [T["ps%d" % b] for b in range(8)]
     rows = lambda h, n=1: slice(GRP * h, GRP * (h + n))
+    slot = lambda k, n=1: slice(MO + NC * k, MO + NC * (k + n))
+    four = lambda t: tuple((t, b) for b in range(4))
+    two = lambda t: ((t, 0), (t, 1))
     names = {}
 
     def sc(name):
@@ -175,147 +175,171 @@ def rank_program(g, core, T, topo):
     def scalar(name, in0, r, s1, o1, s2=None, o2=None):
         ts(sc(name), in0, s1, o1, r, (name,), s2, o2)
 
-    L1, L2, L3 = T.ri[:, 0:26], T.ri[:, 26:52], T.ri[:, 52:78]
-    dmas("d2", [("YS"[h % 2], T.ri[rows(h), 26:52], T.ring[rows(h | 1), :]) for h in range(8)], (), ("L2",))
-    dmas("d1", [("Y", T.ri[rows(1, 7), 0:26], T.ring[rows(0, 7), :]), ("S", T.ri[rows(0), 0:26], T.ring[rows(7), :])], (), ("L1",))
-    dma("S", "d3", L3, T.ring[:, :], (), ("L3",))
+    def line(name, in0, r, scale, bias):
+        act(sc(name), in0, r, (name,), scale=scale, bias=bias)
+
+    def join(tok, parts):
+        writer[tok], reader[tok] = sum([writer[t] for t in parts], []), []
+
+    def unpack(lo, hi, toks, base):
+        for b in range(4):
+            mm(ps[base + b][:, 0:hi - lo], T.qe, T.se, 128 * b, T.qx, T.sx, lo, hi - lo, (("qe", b),) + toks, (("ps", base + b),))
+
+    def window(lo, hi, base, who, toks, between=()):
+        for e in set(who):
+            gate(e, (), toks)
+        for b in range(4):
+            move(who[b], T.win[:, 4 * (CEN + lo) + b:4 * (CEN + hi):4], ps[base + b][:, 0:hi - lo], (("ps", base + b),), (("w", lo, b),), 2.0 ** -5)
+        for t in toks:
+            join(t, [("w", lo, b) for b in range(4)])
+
+    def spread(lo, hi, sem, r, w):
+        dmas(sem, [("Y", T.win[p0:p1, c:c + n], T.win[q0:q0 + p1 - p0, 4 * (CEN + lo):4 * (CEN + hi)]) for p0, p1, q0, c, n in shifts(lo, hi)], r, w)
+
+    L3, L2 = T.ri[:, 0:26], T.ri[:, 28:54]
+    dma("Y", "d3", L3, T.ring[:, :], (), ("L3",))
+    dmas("d2", [("Y", T.ri[rows(h), 28:54], T.ring[rows(h | 1), :]) for h in range(8)], (), ("L2",))
+    dma("Y", "dX", T.xt[:, :], T.x[:, :], (), ("xO", "xG"))
     dma("Y", "dU", T.ut[:, :], T.u[:, :], (), ("ut",))
-    dma("Y", "dX", T.win[:, 4 * CEN:4 * (CEN + NC)], T.x[:, :], (), ("xO", "xG"))
-    dmas("shG", [("Y", T.win[p0:p1, c:c + n], T.x[q0:q0 + p1 - p0, :]) for p0, p1, q0, c, n in shifts(0, NC)], (), ("shG", "shO"))
 
-    iota(T.pI, [[0, 8]], 0, 1, ("pI",))
-    iota(T.pJ, [[128 - GRP, 2]], 0, 1, ("pJ",))
+    op("G", lambda: g.iota(T.pI[:, :], [[0, 8]], 0, 1), (), ("pI",))
     iota(T.idt[:, 0:RING], [[1, RING]], 0, 0, ("id0",))
-    iota(T.idt[:, UI:UI + 3 * NC], [[1, 3 * NC]], UI, 0, ("id1",))
     fill(T.ew[:, :], 32.0, ("ew",))
-
     bi = lambda k, n=1: T.bi[:, k:k + n]
     p0 = T.pI[:, 0:1]
-    ts(bi(0), p0, 4, OP.arith_shift_right, ("pI",), ("g",))
-    ts(bi(1), p0, 4, OP.arith_shift_right, ("pI",), ("par",), 1, OP.bitwise_and)
-    ts(bi(2, 2), T.pJ[:, :], 5, OP.arith_shift_right, ("pJ",), ("kq",), 3, OP.bitwise_and)
     gI, par, pair = bi(0), bi(1), bi(2)
-    scalar("c2", gI, ("g",), -320.0, OP.mult, float(CEN), OP.add)
-    scalar("df", gI, ("g",), 160.0, OP.mult, float(IDB), OP.add)
-    names["v2"], names["v1"] = len(names), len(names) + 1
-    ts(T.sc[:, names["v2"]:names["v2"] + 2], bi(2, 2), float(DBL), OP.mult, ("kq",), ("v2", "v1"), 320.0, OP.add)
-    scalar("ui", pair, ("kq",), -640.0, OP.mult, float(UI), OP.add)
-    scalar("uv", pair, ("kq",), 640.0, OP.mult, -float(UI), OP.add)
-    scalar("xa", par, ("par",), 300.0, OP.mult, -320.0, OP.add)
-    scalar("xb", par, ("par",), float(EB + 40 - CEN), OP.mult, float(CEN), OP.add)
-    scalar("th2", gI, ("g",), 320.0, OP.mult)
-    scalar("al", par, ("par",), 19.0, OP.mult, 1.0, OP.add)
-    scalar("be", par, ("par",), -319.0, OP.mult)
-    scalar("w", par, ("par",), 300.0, OP.mult)
+    ts(gI, p0, 4, OP.arith_shift_right, ("pI",), ("g",))
+    ts(par, p0, 4, OP.arith_shift_right, ("pI",), ("par",), 1, OP.bitwise_and)
+    ts(pair, p0, 5, OP.arith_shift_right, ("pI",), ("pair",))
+    scalar("df", gI, ("g",), 160.0, OP.mult, float(IDB - 160), OP.add)
+    scalar("xa", par, ("par",), -300.0, OP.mult, -20.0, OP.add)
+    scalar("xb", par, ("par",), float(CEN - 20), OP.mult, 20.0, OP.add)
+    scalar("v", pair, ("pair",), float(DBL), OP.mult, 320.0, OP.add)
+    scalar("th1", gI, ("g",), 320.0, OP.mult, 640.0, OP.max)
+    scalar("th2", gI, ("g",), 320.0, OP.mult, 320.0, OP.add)
+    scalar("al", par, ("par",), -19.0, OP.mult, 20.0, OP.add)
+    scalar("be", par, ("par",), 319.0, OP.mult, -319.0, OP.add)
+    scalar("w", par, ("par",), -300.0, OP.mult, 300.0, OP.add)
     scalar("c0", gI, ("g", "xa", "xb"), sc("xa"), OP.mult, sc("xb"), OP.add)
-    scalar("th1", sc("th2"), ("th2",), -320.0, OP.add, 640.0, OP.max)
     fill(T.keep[:, :], 1.0, ("keep",))
-    fill(T.y5[:, :], 0.0, ("y0", "y1", "y2", "y3"))
-    fill(T.pl[:, :], BIG, ("pl",))
+    fill(T.y5[:, 4:130:5], 0.0, ("y4",))
     fill(T.keep[:, 0:130:5], 0.0, ("keep",))
-    act(T.mp[:, MO + CEN:MO + CEN + NC], T.idt[:, 0:NC], ("id0", "df"), ("mapO",), bias=sc("df"))
-    act(T.iv2[:, :], T.idt[:, 0:RING], ("id0", "v2"), ("iv2",), bias=sc("v2"))
+    act(T.mp[:, MO:MO + 512], T.ew[:, 0:512], ("ew",), ("big0",), scale=0.0, bias=BIG)
+    act(T.mp[:, slot(8)], T.ew[:, 0:NC], ("ew",), ("big1",), scale=0.0, bias=BIG)
+    fill(T.mp[:, MO + 512:MO + 800], BIG, ("big3",))
+    act(T.mp[:, slot(6)], T.idt[:, 0:NC], ("id0", "df"), ("big2",), bias=sc("df"))
+    act(T.iv[:, :], T.idt[:, 0:RING], ("id0", "v"), ("iv",), bias=sc("v"))
+    act(T.mp[:, MO + 800:MO + EW], T.ew[:, 0:EW - 800], ("ew",), ("big4",), scale=0.0, bias=BIG)
     for k in range(3):
-        act(T.mp[:, MO + EB + 360 * k:MO + EB + 360 * k + 360], T.idt[:, 0:360], ("id0",), (("mapE", k),), scale=0.0, bias=BIG)
-    act(T.iv1[:, :], T.idt[:, 0:RING], ("id0", "v1"), ("iv1",), bias=sc("v1"))
-    mapE = tuple(("mapE", k) for k in range(3))
+        act(T.idt[:, UI + NC * k:UI + NC * k + NC], T.idt[:, 0:NC], ("id0",), (("id1", k),), bias=float(UI + NC * k))
+    op("G", lambda: g.affine_select(T.e1[:, :], T.ew[:, :], [[1, 516]], OP.is_equal, 0.0, -3, -4), ("ew",), ("e1",))
+    iota(T.j20[:, :], [[16, 20]], 0, 1, ("j20",))
+    iota(T.t4[:, :], [[DBL, 4]], DBL, 0, ("t4",))
+    iota(T.j16[:, :], [[0, 10], [1, 16]], 0, 0, ("j16",))
+    iota(T.j4[:, :], [[0, 40], [1, 4]], 0, 0, ("j4",))
+    iota(T.ft[:, :], [[0, 512]], 0, 0, ("ft0", "ft1", "ft2"))
+    iota(T.src[:, IDB:IDB + 4 * NC], [[640, 4], [1, NC]], 0, 0, ("idr",))
 
-    ts(T.x2[:, :], L2, sc("c2"), OP.add, ("L2", "c2"), ("x2",))
-    ts(T.ui[:, :], L2, sc("ui"), OP.add, ("L2", "ui"), ("uil",))
-    ts(T.qi[:, :], L1, 4, OP.arith_shift_right, ("L1",), ("qi",))
-    ts(T.y5[:, 0:130:5], L1, sc("al"), OP.mult, ("L1", "al", "c0"), ("y0",), sc("c0"), OP.add)
-    ts(T.y5[:, 1:130:5], L1, sc("th1"), OP.is_ge, ("L1", "th1", "w"), ("y1",), sc("w"), OP.mult)
-    ts(T.y5[:, 2:130:5], L1, sc("th2"), OP.is_ge, ("L1", "th2", "w"), ("y2",), sc("w"), OP.mult)
+    ts(T.qi[:, :], L3, 4, OP.arith_shift_right, ("L3",), ("qi",))
+    ts(T.y5[:, 0:130:5], L3, sc("al"), OP.mult, ("L3", "al", "c0"), ("y0",), sc("c0"), OP.add)
+    ts(T.y5[:, 1:130:5], L3, sc("th1"), OP.is_ge, ("L3", "th1", "w"), ("y1",), sc("w"), OP.mult)
+    ts(T.y5[:, 2:130:5], L3, sc("th2"), OP.is_ge, ("L3", "th2", "w"), ("y2",), sc("w"), OP.mult)
     ts(T.y5[:, 3:130:5], T.qi[:, :], sc("be"), OP.mult, ("qi", "be"), ("y3",))
-    op("V", lambda: g.vector.tensor_copy(T.mp[:, MO:MO + EB].indirect(T.x2[:, :]), T.iv2[:, :]), ("iv2", "x2"), ("mapO",))
-    scan(T.s5[:, :], T.keep[:, :], T.y5[:, :], ("keep", "y0", "y1", "y2", "y3"), ("s5",))
-    ts(T.x3[:, :], L3, sc("c2"), OP.add, ("L3", "c2"), ("x3",))
+    scalar("ui", pair, ("pair",), -640.0, OP.mult, float(UI), OP.add)
+    scan(T.s5[:, :], T.keep[:, :], T.y5[:, :], ("keep", "y0", "y1", "y2", "y3", "y4"), ("s5",))
+    ts(T.ui[:, :], L2, sc("ui"), OP.add, ("L2", "ui"), ("uil",))
     cp(T.x1[:, :], T.s5[:, 4:130:5], ("s5",), ("x1",))
-    quant(T.qu, T.su, 0, 128, T.ut, 0, ("ut",), ("qu",))
-    op("V", lambda: g.vector.tensor_copy(T.mp[:, MO:MO + EB + EW].indirect(T.x1[:, :]), T.iv1[:, :]), ("iv1", "x1"), ("mapO",) + mapE)
-    win_id = T.idt[:, 0:UI + 3 * NC]
-    act(T.st[:, 0:NC], win_id.indirect(T.ui[:, 6:26]), ("id0", "id1", "uil", "uv"), ("st0",), bias=sc("uv"))
-    act(T.st[:, NC:DBL], win_id.indirect(T.ui[:, 0:26]), ("id0", "id1", "uil", "uv"), ("st1",), bias=sc("uv"))
+    scalar("uv", pair, ("pair",), 640.0, OP.mult, -float(UI), OP.add)
+    fill(T.pl[:, :], BIG, ("pl",))
+    op("V", lambda: g.vector.tensor_copy(T.mp[:, slot(0, 15)].indirect(T.x1[:, :]), T.iv[:, :]), ("iv", "x1"), ("big0", "big1", "big2", "big3", "big4", "inv"))
+    copies = []
+    for e in (0, 2, 4, 6):
+        f = (e - 1) % 8
+        copies.append(("Y", T.mp[rows(e), slot(6, 2)], T.mp[rows(e + 1), slot(6, 2)]))
+        copies.append(("Y", T.mp[rows(e), slot(5 if e else 13)], T.mp[rows(f), slot(7)]))
+        copies.append(("Y", T.mp[rows(e), slot(8)], T.mp[rows(f), slot(8 if e else 0)]))
+    dmas("dM", copies, ("inv",), ("near",))
+    copies = []
+    for e in (0, 2, 4, 6):
+        for h in ((e - 1) % 8, e, e + 1):
+            a = MO + 20 - 20 * e + 20 * h + 300 * ((NC * h >= max(NC * e, 640)) + (h > e))
+            copies.append(("Y", T.pl[rows(h), 10 * e:10 * e + 20], T.mp[GRP * e:GRP * e + 1, a:a + NC]))
+    dmas("dF", copies, ("inv",), ("pl",))
+    idt = ("id0", ("id1", 0), ("id1", 1), ("id1", 2), "uil", "uv")
+    act(T.st[:, 0:NC], T.idt[:, :].indirect(T.ui[:, 6:26]), idt, ("st0",), bias=sc("uv"))
+    act(T.st[:, NC:DBL], T.idt[:, :].indirect(T.ui[:, 0:26]), idt, ("st1",), bias=sc("uv"))
     copies = []
     for k in range(4):
-        for first, n in ((2 * k - 1, 1), (2 * k, 2), (2 * k + 2, 2)):
-            copies.append(("Y", T.src[rows(first % 8, n), DBL * k:DBL * k + DBL], T.st[rows(2 * k, n), :]))
+        for first_, n in ((2 * k - 1, 1), (2 * k, 2), (2 * k + 2, 2)):
+            copies.append(("Y", T.src[rows(first_ % 8, n), DBL * k:DBL * k + DBL], T.st[rows(2 * k, n), :]))
+    quant(T.qx, T.sx, 0, NC, T.xt, 0, ("xO", "xG"), ("qxO", "qxG"))
+    for b in range(4):
+        quant(T.qe, T.se, 128 * b, 128 * b + 128, T.e1, 3 - b, ("e1",), (("qe", b),))
+    unpack(0, NC, ("qxO", "qxG"), 4)
+    ts(bi(3), p0, 15, OP.bitwise_and, ("pI",), ("k16",))
+    ts(bi(4), p0, 2, OP.arith_shift_right, ("pI",), ("kk",), 3, OP.bitwise_and)
+    ts(bi(5, 5), T.pI[:, 0:5], 3, OP.bitwise_and, ("pI",), ("p3",))
+    ts(bi(10, 3), T.pI[:, 0:3], 7, OP.bitwise_and, ("pI",), ("p7",))
+    scalar("x3a", par, ("par",), 320.0, OP.mult, float(CEN - NC), OP.add)
+    cp(T.bf[:, 0:6], bi(0, 6), ("g", "par", "pair", "k16", "kk", "p3"), ("bf",))
+    scalar("c3", gI, ("g", "x3a"), -320.0, OP.mult, sc("x3a"), OP.add)
+    ts(T.ul[:, 0:5], bi(5, 5), 32.0, OP.mult, ("p3",), ("ul0",))
+    ts(T.ul[:, 5:8], bi(10, 3), 16.0, OP.mult, ("p7",), ("ul1",))
+    ts(T.x3[:, :], L3, sc("c3"), OP.add, ("L3", "c3"), ("x3",))
+    quant(T.qu, T.su, 0, 128, T.ut, 0, ("ut",), ("qu",))
+    fill(T.ct[:, :], 1.0, ("ct",))
     dmas("dS", copies, ("st0", "st1"), ("src",))
-    win_o = T.mp[:, MO:MO + EB]
-    cp(T.mp[:, OWN:OWN + NC], win_o.indirect(T.x3[:, 6:26]), ("mapO", "x3"), ("ct0",))
-    act(T.mp[:, OWN + NC:OWN + DBL], win_o.indirect(T.x3[:, 0:26]), ("mapO", "x3"), ("ct1",))
-    copies = []
-    for f in (1, 3, 5, 7):
-        for h in ((f - 2) % 8, f - 1, f):
-            a = MO + EB + 40 - 20 * f + 20 * h + 300 * ((NC * h >= max(NC * (f - 1), 640)) + (h >= f))
-            copies.append(("Y", T.pl[rows(h), 20 * (f // 2):20 * (f // 2) + 20], T.mp[GRP * f:GRP * f + 1, a:a + NC]))
-    dmas("dF", copies, mapE, ("pl",))
+    window(0, NC, 4, "SSSS", ("wO", "wG"))
+    tt(T.mp[:, slot(6)], T.mp[:, slot(6)], T.mp[:, slot(8)], OP.min, (), ("near",))
+    inv = T.mp[:, slot(0, 15)]
+    cp(T.mp[:, OWN:OWN + NC], inv.indirect(T.x3[:, 6:26]), ("near", "inv", "x3"), ("ct0",))
+    act(T.mp[:, OWN + NC:OWN + DBL], inv.indirect(T.x3[:, 0:26]), ("near", "inv", "x3"), ("ct1",))
     copies = []
     for e in (0, 2, 4, 6):
         for h, a in ((e + 1, OWN), ((e - 1) % 8, OWN + DBL if e else 0)):
             copies.append(("Y", T.mp[rows(h), a:a + DBL], T.mp[rows(e), OWN:OWN + DBL]))
     dmas("dC", copies, (), ("ct0", "ct1"))
+    spread(0, NC, "shG", ("wO", "wG"), ("shO", "shG"))
     dmas("dW", [("Y", T.wq[:, :].bitcast(dt.uint8), T.wc[:, :]), ("Y", T.wsb[:, :], T.ws[:, :])], (), ("wq",))
     dma("Y", "dV", T.vt[:, :], T.v[:, :], (), ("vt",))
 
-    iota(T.j20[:, :], [[16, 20]], 0, 1, ("j20",))
-    iota(T.t4[:, :], [[DBL, 4]], DBL, 0, ("t4",))
-    op("G", lambda: g.affine_select(T.e1[:, :], T.ew[:, :], [[1, 516]], OP.is_equal, 0.0, -3, -4), ("ew",), ("e1",))
-    iota(T.j16[:, :], [[0, 10], [1, 16]], 0, 0, ("j16",))
-    iota(T.j4[:, :], [[0, 40], [1, 4]], 0, 0, ("j4",))
-    iota(T.src[:, IDB:IDB + 4 * NC], [[640, 4], [1, NC]], 0, 0, ("idr",))
-    ts(bi(8, 5), T.pI[:, 0:5], 3, OP.bitwise_and, ("pI",), ("p3",))
-    ts(bi(13, 3), T.pI[:, 0:3], 7, OP.bitwise_and, ("pI",), ("p7",))
-    ts(bi(4), p0, 15, OP.bitwise_and, ("pI",), ("k16",))
-    ts(bi(5), p0, 2, OP.arith_shift_right, ("pI",), ("kk",), 3, OP.bitwise_and)
-    ts(T.ul[:, 0:5], bi(8, 5), 32.0, OP.mult, ("p3",), ("ul0",))
-    ts(T.ul[:, 5:8], bi(13, 3), 16.0, OP.mult, ("p7",), ("ul1",))
-    quant(T.qx, T.sx, 0, NC, T.win, 4 * CEN, ("xO", "xG"), ("qxO", "qxG"))
     op("V", lambda: g.vector.tensor_copy(T.qu2[:, 0:128].bitcast(dt.uint32), T.qu[:, 0:128].bitcast(dt.uint32).indirect(T.ul[:, 0:8])), ("qu", "ul0", "ul1"), ("qu2",))
     op("S", lambda: g.scalar.activation(T.su2[:, 0:128], T.su[:, 0:128].indirect(T.ul[:, 0:8]), FN.Copy), ("qu", "ul0", "ul1"), ("su2",))
-    fill(T.ft[:, :], 0.0, ("ft0", "ft1", "ft2"))
-    fill(T.ct[:, :], 1.0, ("ct",))
-    scalar("p16", bi(4), ("k16",), -1.0, OP.mult, -0.5, OP.add)
-    scalar("p4", bi(5), ("kk",), -1.0, OP.mult, -0.5, OP.add)
     fill(T.ct[0:64, 2:512:4], 0.0, ("ct",))
-    scalar("f1", bi(4), ("k16",), -B, OP.mult, 15 * B, OP.add)
-    scalar("fa", bi(5), ("kk",), 4 * B, OP.mult, -12 * B, OP.add)
+    fill(T.nt[:, :], 0.0, ("nt",))
     fill(T.ct[:, 3:512:4], 0.0, ("ct",))
-    scalar("fb", sc("c2"), ("c2", "fa"), 4.0, OP.mult, sc("fa"), OP.add)
-    scalar("n", gI, ("g",), -16.0, OP.mult, float(MO + CEN), OP.add)
-    quant(T.qc, T.sct, 0, 128, T.ct, 0, ("ct",), ("qc",))
-    for pat, j, sg, nm in ((T.p16, T.j16, T.g16, "16"), (T.p4, T.j4, T.g4, "4")):
+    bf = lambda k: T.bf[:, k:k + 1]
+    line("adj", bf(2), ("bf",), -float(DBL), float(OWN))
+    line("n", bf(0), ("bf",), -16.0, float(MO + CEN))
+    line("p16", bf(3), ("bf",), -1.0, -0.5)
+    line("p4", bf(4), ("bf",), -1.0, -0.5)
+    line("f1", bf(3), ("bf",), -B, 15 * B)
+    line("fa", bf(4), ("bf",), 4 * B, 4.0 * CEN - 12 * B)
+    line("fb", bf(0), ("bf", "fa"), -1280.0, sc("fa"))
+    for r in range(4):
+        act(T.mt[:, r:80:4], T.pl[:, 20 * r:20 * r + 20], ("pl", "adj"), (("mt", r),), bias=sc("adj"))
+    act(T.nt[:, 0:80:4], T.j20[:, :], ("j20", "n"), ("nt",), bias=sc("n"))
+    for j, sg, nm in ((T.j16, T.g16, "16"), (T.j4, T.g4, "4")):
         act(sg[:, :], j[:, :], ("j" + nm, "p" + nm), ("g" + nm,), bias=sc("p" + nm), fn=FN.Sign)
+    act(T.th[:, :], T.t4[:, :], ("t4", "f1"), ("th",), bias=sc("f1"))
+    line("fin", bf(5), ("bf", "fb"), 1.0, sc("fb"))
     for pat, sg, nm in ((T.p16, T.g16, "16"), (T.p4, T.g4, "4")):
         act(pat[:, :], sg[:, :], ("g" + nm,), ("P" + nm,), scale=8.5 * B, bias=-7.5 * B)
+    quant(T.qc, T.sct, 0, 128, T.ct, 0, ("ct",), ("qc",))
 
-    def compare(t):
-        ts(T.ft[:, t:4 * NP:4], ps[t][:, 0:NP], 0.0, OP.is_gt, (("ps", t),), ("ft%d" % t,))
+    def score(t):
+        a, toks = ((192, ("qxO",)), (0, ("qxG",)), (64, ("qxO", "qxG")))[t]
+        mm(ps[t][:, 0:128], T.qx, T.sx, a, T.qu2, T.su2, 0, 128, toks + ("qu2", "su2"), (("ps", t),))
 
-    def counts_a():
-        mm(ps[0][:, 0:128], T.qx, T.sx, 192, T.qu2, T.su2, 0, 128, ("qxO", "qu2", "su2"), (("ps", 0),))
-
-    def counts_b(beside=None):
-        mm(ps[1][:, 0:128], T.qx, T.sx, 0, T.qu2, T.su2, 0, 128, ("qxG", "qu2", "su2"), (("ps", 1),))
-        mm(ps[2][:, 0:128], T.qx, T.sx, 64, T.qu2, T.su2, 0, 128, ("qxO", "qxG", "qu2", "su2"), (("ps", 2),))
+    def counts():
         for t in range(3):
-            compare(t)
+            ts(T.ft[:, t:4 * NP:4], ps[t][:, 0:NP], 0.0, OP.is_gt, (("ps", t),), ("ft%d" % t,))
         quant(T.qf, T.sf, 0, 128, T.ft, 0, ("ft0", "ft1", "ft2"), ("qf",))
         mm(ps[3][:, 0:128], T.qc, T.sct, 0, T.qf, T.sf, 0, 128, ("qc", "qf"), (("ps", 3),))
 
-    counts_a()
-    counts_b()
-    scalar("fin", bi(8), ("p3", "fb"), sc("fb"), OP.add)
-    scalar("adj", pair, ("kq",), -float(DBL), OP.mult, float(OWN), OP.add)
-    fill(T.nt[:, :], 0.0, ("nt",))
-    ts(T.th[:, :], T.t4[:, :], sc("f1"), OP.add, ("t4", "f1"), ("th",))
-    ts(T.nt[:, 0:80:4], T.j20[:, :], sc("n"), OP.add, ("j20", "n"), ("nt",))
-    for r in range(4):
-        ts(T.mt[:, r:80:4], T.pl[:, 20 * r:20 * r + 20], sc("adj"), OP.add, ("pl", "adj"), (("mt", r),))
-    four = lambda t: tuple((t, b) for b in range(4))
-
-    def pack_e(b):
-        quant(T.qe, T.se, 128 * b, 128 * b + 128, T.e1, 3 - b, ("e1",), (("qe", b),))
+    for t in range(3):
+        score(t)
+    counts()
 
     def lists(rd):
         cn = lambda k: T.cnt[:, k:k + 1]
@@ -324,25 +348,17 @@ def rank_program(g, core, T, topo):
         scan(T.xs[:, :], T.nt[:, :], T.xc[:, :], ("nt", "xc"), ("xs",), OP.max, OP.min)
         tt(T.df[:, 0:3], T.cnt[:, 1:6:2], T.cnt[:, 3:8:2], OP.subtract, ("cnt",), ("dfc",))
         cp(T.o1[:, :], T.xs[:, 3:80:4], ("xs",), ("o1",))
-        if rd == 0:
-            pack_e(0)
-        tab = T.mp[:, 0:MO + EB]
+        tab = T.mp[:, 0:MO + WINC]
         for h in range(2):
-            move("VS"[h], T.r1[:, HALF * h:HALF * h + HALF], tab.indirect(T.o1[:, 10 * h:10 * h + 10]), ("o1", "mapO", "ct0", "ct1"), (("r1", h),))
+            move("VS"[h], T.r1[:, HALF * h:HALF * h + HALF], tab.indirect(T.o1[:, 10 * h:10 * h + 10]), ("o1", "near", "inv", "ct0", "ct1"), (("r1", h),))
         act(T.acs[:, rd:24:3], T.cnt[:, :], ("cnt",), (("ac", rd),))
-        if rd == 0:
-            pack_e(1)
         for h in range(2):
             scan(T.f1[:, HALF * h:HALF * h + HALF], T.p16[:, :], T.r1[:, HALF * h:HALF * h + HALF], ("P16", ("r1", h)), (("f1", h),), OP.add, OP.max)
-        if rd == 0:
-            pack_e(2)
         x, xt = T.f1[:, 15:NC:16], (("f1", 0), ("f1", 1))
         ts(T.z5[:, 0:100:5], x, sc("f1"), OP.subtract, xt + ("f1", "cnt"), (("z", 0),), cn(1), OP.subtract)
         for q in range(4):
             ts(T.z5[:, q + 1:100:5], x, T.th[:, q:q + 1], OP.is_ge, xt + ("th", "dfc", "cnt"), (("z", q + 1),), T.df[:, q:q + 1] if q < 3 else cn(7), OP.mult)
         scan(T.zs[:, :], T.keep[:, 0:100], T.z5[:, :], ("keep",) + tuple(("z", q) for q in range(5)), ("zs",))
-        if rd == 0:
-            pack_e(3)
         cp(T.o2[:, :], T.zs[:, 4:100:5], ("zs",), ("o2",))
         for h in range(2):
             move("VS"[h], T.r2[:, HALF * h:HALF * h + HALF], T.src[:, :].indirect(T.o2[:, 10 * h:10 * h + 10]), ("o2", "src", "idr"), (("r2", h),))
@@ -356,33 +372,13 @@ def rank_program(g, core, T, topo):
     def gather(h, tile, tok):
         for k in range(2):
             c = 40 * h + 20 * k
-            move("VS"[k], tile[:, NC * k:NC * k + NC], T.win[:, :].indirect(T.l4[:, c:c + 20]), ("xO", "xG", "shO", "shG", ("l4", h)), ((tok, k),))
+            move("VS"[k], tile[:, NC * k:NC * k + NC], T.win[:, :].indirect(T.l4[:, c:c + 20]), ("wO", "wG", "shO", "shG", ("l4", h)), ((tok, k),))
 
-    def unpack(q, s, qt, base, tile, tok, beside=()):
-        for b in range(4):
-            mm(ps[base + b][:, 0:HALF], T.qe, T.se, 128 * b, q, s, 0, HALF, (("qe", b),) + qt, (("ps", base + b),))
-        for b in range(4):
-            if b % 2 == 0 and beside:
-                beside[b // 2]()
-            move("VS"[b % 2], tile[:, b:4 * HALF:4], ps[base + b][:, 0:HALF], (("ps", base + b),), ((tok, b),), 2.0 ** -5)
-
-    def first(base, b, q, s, qt):
-        mm(ps[base + b][:, 0:HALF], T.qe, T.se, 128 * b, q, s, 0, HALF, (("qe", b),) + qt, (("ps", base + b),), True, False)
-
-    def layer(base, b, q, s, qt):
+    def layer(base, b, q, s, qt, start):
         tok = ("ps", base + b)
-        writer[tok] = [x for x in writer[tok] if x[0] != "cT"]
-        mm(ps[base + b][:, 0:HALF], T.wq, T.wsb, 128 * b, q, s, 0, HALF, ("wq",) + qt, (tok,), False, True)
-
-    def state(base, c0, tok):
-        gate("V", (), (tok,))
-        gate("S", (), (tok,))
-        for b in range(4):
-            move("VS"[b % 2], T.win[:, c0 + b:c0 + 4 * HALF:4], ps[base + b][:, 0:HALF], (("ps", base + b),), ((tok + "b", b),), 2.0 ** -5)
-        writer[tok], reader[tok] = sum([writer[(tok + "b", b)] for b in range(4)], []), []
-
-    def spread(lo, hi, sem, tok):
-        dmas(sem, [("Y", T.win[p0:p1, c:c + n], T.win[q0:q0 + p1 - p0, 4 * (CEN + lo):4 * (CEN + hi)]) for p0, p1, q0, c, n in shifts(lo, hi)], (tok,), (sem,))
+        if not start:
+            writer[tok] = [x for x in writer[tok] if x[0] != "cT"]
+        mm(ps[base + b][:, 0:HALF], T.wq, T.wsb, 128 * b, q, s, 0, HALF, ("wq",) + qt, (tok,), start, True)
 
     def store(lo, tok, bank, e):
         dma("Y", "dOut", T.oc[:, 4 * lo:4 * (lo + HALF)], T.qx[:, lo:lo + HALF].bitcast(dt.uint8), (tok,), ())
@@ -391,16 +387,15 @@ def rank_program(g, core, T, topo):
         move("VS"[e == "Y"], T.yt[:, lo:lo + HALF], ps[bank][:, 0:HALF], (("ps", bank),), (("y", lo),))
         dma("Y", "dOut", T.y[:, lo:lo + HALF], T.yt[:, lo:lo + HALF], (("y", lo),), ())
 
-    two = lambda t: ((t, 0), (t, 1))
     for rd in range(3):
         last = rd == 2
         lists(rd)
         fold(0)
         offsets(0)
-        gather(0, T.gr, "gr")
-        quant(T.q1, T.s1, 0, HALF, T.gr, 0, two("gr"), ("q1",))
-        unpack(T.q1, T.s1, ("q1",), 4, T.gt, "gt", (lambda: fold(1), lambda: offsets(1)))
-        quant(T.q2, T.s2, 0, HALF, T.gt, 0, four("gt"), ("q2",))
+        fold(1)
+        gather(0, T.gt, "gt")
+        offsets(1)
+        quant(T.q2, T.s2, 0, HALF, T.gt, 0, two("gt"), ("q2",))
         dst = T.cores[rank ^ MASKS[rd]]
         rid, pid = topo.addr(dst)[0], topo.addr(dst)[1]
         ne, mask = len(topo.engines(core, dst)), topo.mask(core, dst)
@@ -414,36 +409,48 @@ def rank_program(g, core, T, topo):
         mark("G", "sent", total["sent"], ("q2",), ())
         land = ("land", rd)
         writer[land] = [(arr, 2 * ne, {}, "R")]
-        gather(1, T.ow, "ow")
-        quant(T.qo, T.so, 0, HALF, T.ow, 0, two("ow"), ("qo",))
-        unpack(T.qo, T.so, ("qo",), 0, T.zo, "zo")
+        gather(1, T.zo, "zo")
+        quant(T.qz, T.sz, 0, HALF, T.zo, 0, two("zo"), ("qz",))
         for b in range(4):
-            first(0, b, T.qo, T.so, ("qo",))
-        quant(T.qz, T.sz, 0, HALF, T.zo, 0, four("zo"), ("qz",))
+            act(T.z32[:, HALF * b:HALF * b + HALF], T.zo[:, b:4 * HALF:4], two("zo"), (("z32", b),), scale=32.0)
         if rd == 0:
             quant(T.qv, T.sv, 0, 128, T.vt, 0, ("vt",), ("qv",))
         for b in range(4):
-            layer(0, b, T.qz, T.sz, ("qz",))
-        state(0, 4 * (CEN + HALF), "xO")
-        if not last:
-            spread(HALF, NC, "shO", "xO")
-        quant(T.qx, T.sx, HALF, NC, T.win, 4 * (CEN + HALF), ("xO",), ("qxO",))
+            layer(0, b, T.qz, T.sz, ("qz",), True)
+        gate("S", (), ("xO",))
         for b in range(4):
-            first(4, b, lc, ls, (land,))
-            layer(4, b, lc, ls, (land,))
-        if last:
+            part = T.sm[:, HALF * b:HALF * b + HALF]
+            tt(part, ps[b][:, 0:HALF], T.z32[:, HALF * b:HALF * b + HALF], OP.add, (("ps", b), ("z32", b)), (("sm", b),))
+            act(T.xt[:, 4 * HALF + b:4 * NC:4], part, (("sm", b),), (("xo", b),), scale=2.0 ** -5)
+        join("xO", four("xo"))
+        quant(T.qx, T.sx, HALF, NC, T.xt, 4 * HALF, ("xO",), ("qxO",))
+        if not last:
+            unpack(HALF, NC, ("qxO",), 0)
+            window(HALF, NC, 0, "SSSS", ("wO",))
+            spread(HALF, NC, "shO", ("wO",), ("shO",))
+        else:
             dma("Y", "dOut", T.ac[:, :], T.acs[0:1, 0:24], (("ac", 0), ("ac", 1), ("ac", 2)), ())
             store(HALF, "qxO", 0, "Y")
-        else:
-            counts_a()
-        state(4, 4 * CEN, "xG")
+        for b in range(4):
+            mm(ps[4 + b][:, 0:HALF], T.qe, T.se, 128 * b, lc, ls, 0, HALF, (("qe", b), land), (("ps", 4 + b),), True, False)
+            layer(4, b, lc, ls, (land,), False)
         if not last:
-            spread(0, HALF, "shG", "xG")
-        quant(T.qx, T.sx, 0, HALF, T.win, 4 * CEN, ("xG",), ("qxG",))
+            score(0)
+        for e in "VS":
+            gate(e, (), ("xG",))
+        for b in range(4):
+            move("VS"[b % 2], T.xt[:, b:4 * HALF:4], ps[4 + b][:, 0:HALF], (("ps", 4 + b),), (("xg", b),), 2.0 ** -5)
+        join("xG", four("xg"))
+        quant(T.qx, T.sx, 0, HALF, T.xt, 0, ("xG",), ("qxG",))
         if last:
             store(0, "qxG", 1, "S")
         else:
-            counts_b()
+            score(1)
+            score(2)
+            unpack(0, HALF, ("qxG",), 4)
+            window(0, HALF, 4, "SSSS", ("wG",))
+            spread(0, HALF, "shG", ("wG",), ("shG",))
+            counts()
     for s in SEMAPHORES:
         if total[s] and known["Y"].get(s, 0) < total[s]:
             g.sync.wait_ge(T.sem[s], total[s])

@@ -7,10 +7,10 @@ NC, HALF, GRP, RING, DBL = 320, 160, 16, 416, 736
 CEN = 7 * NC
 WINC = 15 * NC
 OWN = 3 * DBL
-MO = 5 * DBL
-EW = 1080
+MO = 6 * DBL
+EB, EW = 7 * NC, 1060
 IDB = 4 * DBL
-UI = 1920
+UI = 6 * NC
 BIG = 1.0e6
 B = 8192.0
 NP = 88
@@ -20,10 +20,10 @@ F32, BF16, I32, U16, U8, X4 = "float32", "bfloat16", "int32", "uint16", "uint8",
 
 WIDTHS = {
     BF16: {"win": 4 * WINC, "xt": 4 * NC, "ew": 516, "e1": 516, "ct": 512, "ft": 512, "ut": 512, "vt": 512, "gt": 4 * HALF, "zo": 4 * HALF, "z32": 4 * HALF},
-    F32: {"mp": MO + WINC, "src": IDB + 4 * NC, "idt": UI + 3 * NC, "st": DBL, "iv": RING, "sc": 32, "bf": 8, "y5": 130, "s5": 130, "keep": 130,
+    F32: {"mp": MO + 20 * NC, "src": IDB + UI + 3 * NC, "iv": RING, "sc": 32, "bf": 12, "y5": 130, "s5": 130, "keep": 130,
           "j20": 20, "j16": HALF, "j4": HALF, "g16": HALF, "g4": HALF, "p16": HALF, "p4": HALF, "t4": 4, "th": 4, "pl": 80, "mt": 80, "nt": 80, "xc": 80, "xs": 80,
-          "cnt": 8, "df": 4, "r1": NC, "f1": NC, "r2": NC, "f2": NC, "z5": 100, "zs": 100, "acs": 24, "sm": 4 * HALF, "yt": NC},
-    I32: {"ri": 56, "qi": 26, "pI": 8, "bi": 32},
+          "rel": 8, "cnt": 4, "df": 4, "r1": NC, "f1": NC, "r2": NC, "f2": NC, "z5": 100, "zs": 100, "acs": 24, "sm": 4 * HALF, "yt": NC},
+    I32: {"ri": 84, "qi": 26, "pI": 24, "bi": 32},
     U16: {"x1": 26, "x3": 26, "ui": 26, "ul": 8, "o1": 20, "o2": 20, "l4": 80},
     X4: {"qe": 512, "qc": 128, "qf": 128, "qu": 128, "qu2": 128, "qv": 128, "wq": 512, "qx": NC, "q2": HALF, "qz": HALF, "lc0": HALF, "lc1": HALF, "lc2": HALF},
     U8: {"se": 512, "sct": 128, "sf": 128, "su": 128, "su2": 128, "sv": 128, "wsb": 512, "sx": NC, "s2": HALF, "sz": HALF, "ls0": HALF, "ls1": HALF, "ls2": HALF},
@@ -31,25 +31,17 @@ WIDTHS = {
 SCRATCH = {name: ("sbuf", [128, n], t) for t, d in WIDTHS.items() for name, n in d.items()}
 for _b in range(8):
     SCRATCH["ps%d" % _b] = ("psum", [128, 512], "float32")
-LOCAL = ("d2", "d3", "dB", "dX", "dU", "dV", "dW", "shO", "shG", "dS", "dM", "dF", "dC", "dOut")
+LOCAL = ("dM", "dN", "d2", "d3", "dX", "dU", "dV", "dW", "sh", "shO", "shG", "dS", "dF", "dC", "dOut")
 SEMAPHORES = ["cV", "cS", "cT", "cG", "arr0", "arr1", "arr2", "sent"] + list(LOCAL)
 
 
-def shifts(lo, hi):
+def shifts():
     out = []
-
-    def piece(p0, p1, q0):
-        slot = q0 // GRP - p0 // GRP + 7
-        out.append((p0, p1, q0, 4 * (NC * slot + lo), 4 * (hi - lo)))
-    for m in (1, 2):
-        k = GRP * m
-        piece(0, 128 - k, k)
-        piece(128 - k, 128, 0)
-        piece(k, 128, 0)
-        piece(0, k, 128 - k)
-    for grp in (1, 3, 5, 7):
-        for d in (3, -3):
-            piece(GRP * grp, GRP * grp + GRP, GRP * ((grp + d) % 8))
+    for d in (1, -1, 2, -2):
+        k = GRP * (d % 8)
+        out += [(0, 128 - k, k, 7 + d % 8), (128 - k, 128, 0, d % 8 - 1)]
+    for h in (1, 3, 5, 7):
+        out += [(GRP * h, GRP * h + GRP, GRP * ((h + d) % 8), (h + d) % 8 - h + 7) for d in (3, -3)]
     return out
 
 
@@ -69,13 +61,13 @@ def rank_program(g, core, T, topo):
             need += writer.get(t, [])
         for t in w:
             need += writer.get(t, [])
-            need += [x for x in reader.get(t, []) if x[3] != e]
+            need += reader.get(t, [])
         best = {}
-        for sem, val, clk, _ in need:
+        for sem, val, clk in need:
             v = total[sem] if sem in LOCAL else val
             best[sem] = max(best.get(sem, 0), v)
         clks = {}
-        for sem, val, clk, _ in need:
+        for sem, val, clk in need:
             for s, v in clk.items():
                 if s != sem and s not in LOCAL:
                     clks.setdefault(s, []).append((sem, v))
@@ -86,16 +78,16 @@ def rank_program(g, core, T, topo):
             if any(o != sem and o in best and x >= v for o, x in clks.get(sem, [])):
                 continue
             eng[e].wait_ge(T.sem[sem], v)
-        for sem, val, clk, _ in need:
+        for sem, val, clk in need:
             for s, v in clk.items():
                 known[e][s] = max(known[e].get(s, 0), v)
         for sem in best:
             known[e][sem] = max(known[e].get(sem, 0), best[sem])
 
-    def mark(e, sem, val, r, w, who=None):
+    def mark(e, sem, val, r, w):
         clk = dict(known[e])
         clk[sem] = val
-        x = (sem, val, clk, who or e)
+        x = (sem, val, clk)
         for t in w:
             writer[t] = [x]
             reader[t] = []
@@ -115,7 +107,7 @@ def rank_program(g, core, T, topo):
         for e, out, in_ in copies:
             total[sem] += 16
             eng[e].dma_start(out, in_).then_inc(T.sem[sem], 16)
-        mark(copies[0][0], sem, total[sem], r, w, "DMA")
+        mark(copies[0][0], sem, total[sem], r, w)
 
     def dma(e, sem, out, in_, r, w):
         dmas(sem, [(e, out, in_)], r, w)
@@ -181,187 +173,192 @@ def rank_program(g, core, T, topo):
     def join(tok, parts):
         writer[tok], reader[tok] = sum([writer[t] for t in parts], []), []
 
-    def unpack(lo, hi, toks, base):
-        for b in range(4):
-            mm(ps[base + b][:, 0:hi - lo], T.qe, T.se, 128 * b, T.qx, T.sx, lo, hi - lo, (("qe", b),) + toks, (("ps", base + b),))
+    SB, HI, LO = (0, 4, 5), (1, 2, 3, 0), (6, 1, 2, 3)
 
-    def window(lo, hi, base, who, toks, between=()):
-        for e in set(who):
+    def unpack(lo, hi, toks, banks):
+        for b, k in enumerate(banks):
+            mm(ps[k][:, 0:hi - lo], T.qe, T.se, 128 * b, T.qx, T.sx, lo, hi - lo, (("qe", b),) + toks, (("ps", k),))
+
+    def window(lo, hi, banks, who, toks):
+        for e in sorted(set(who) - {" "}):
             gate(e, (), toks)
-        for b in range(4):
-            move(who[b], T.win[:, 4 * (CEN + lo) + b:4 * (CEN + hi):4], ps[base + b][:, 0:hi - lo], (("ps", base + b),), (("w", lo, b),), 2.0 ** -5)
+        for b, k in enumerate(banks):
+            if who[b] != " ":
+                move(who[b], T.win[:, 4 * (CEN + lo) + b:4 * (CEN + hi):4], ps[k][:, 0:hi - lo], (("ps", k),), (("w", lo, b),), 2.0 ** -5)
         for t in toks:
             join(t, [("w", lo, b) for b in range(4)])
 
-    def spread(lo, hi, sem, r, w):
-        dmas(sem, [("Y", T.win[p0:p1, c:c + n], T.win[q0:q0 + p1 - p0, 4 * (CEN + lo):4 * (CEN + hi)]) for p0, p1, q0, c, n in shifts(lo, hi)], r, w)
+    def spread(lo, hi, a, b, r, sem):
+        dmas(sem, [("Y", T.win[p0:p1, 4 * (NC * k + lo):4 * (NC * k + hi)], T.win[q0:q0 + p1 - p0, 4 * (CEN + lo):4 * (CEN + hi)])
+                   for p0, p1, q0, k in shifts()[a:b]], r, (sem,))
 
     L3, L2 = T.ri[:, 0:26], T.ri[:, 28:54]
     dma("Y", "d3", L3, T.ring[:, :], (), ("L3",))
-    dmas("d2", [("Y", T.ri[rows(h), 28:54], T.ring[rows(h | 1), :]) for h in range(8)], (), ("L2",))
+    dmas("d2", [("YS"[h % 2], T.ri[rows(h), 28:54], T.ring[rows(h | 1), :]) for h in range(8)], (), ("L2",))
     dma("Y", "dX", T.xt[:, :], T.x[:, :], (), ("xO", "xG"))
     dma("Y", "dU", T.ut[:, :], T.u[:, :], (), ("ut",))
-
-    op("G", lambda: g.iota(T.pI[:, :], [[0, 8]], 0, 1), (), ("pI",))
-    iota(T.idt[:, 0:RING], [[1, RING]], 0, 0, ("id0",))
-    fill(T.ew[:, :], 32.0, ("ew",))
-    bi = lambda k, n=1: T.bi[:, k:k + n]
-    p0 = T.pI[:, 0:1]
-    gI, par, pair = bi(0), bi(1), bi(2)
-    ts(gI, p0, 4, OP.arith_shift_right, ("pI",), ("g",))
-    ts(par, p0, 4, OP.arith_shift_right, ("pI",), ("par",), 1, OP.bitwise_and)
-    ts(pair, p0, 5, OP.arith_shift_right, ("pI",), ("pair",))
-    scalar("df", gI, ("g",), 160.0, OP.mult, float(IDB - 160), OP.add)
-    scalar("xa", par, ("par",), -300.0, OP.mult, -20.0, OP.add)
-    scalar("xb", par, ("par",), float(CEN - 20), OP.mult, 20.0, OP.add)
-    scalar("v", pair, ("pair",), float(DBL), OP.mult, 320.0, OP.add)
-    scalar("th1", gI, ("g",), 320.0, OP.mult, 640.0, OP.max)
-    scalar("th2", gI, ("g",), 320.0, OP.mult, 320.0, OP.add)
-    scalar("al", par, ("par",), -19.0, OP.mult, 20.0, OP.add)
-    scalar("be", par, ("par",), 319.0, OP.mult, -319.0, OP.add)
-    scalar("w", par, ("par",), -300.0, OP.mult, 300.0, OP.add)
-    scalar("c0", gI, ("g", "xa", "xb"), sc("xa"), OP.mult, sc("xb"), OP.add)
-    fill(T.keep[:, :], 1.0, ("keep",))
-    fill(T.y5[:, 4:130:5], 0.0, ("y4",))
-    fill(T.keep[:, 0:130:5], 0.0, ("keep",))
-    act(T.mp[:, MO:MO + 512], T.ew[:, 0:512], ("ew",), ("big0",), scale=0.0, bias=BIG)
-    act(T.mp[:, slot(8)], T.ew[:, 0:NC], ("ew",), ("big1",), scale=0.0, bias=BIG)
-    fill(T.mp[:, MO + 512:MO + 800], BIG, ("big3",))
-    act(T.mp[:, slot(6)], T.idt[:, 0:NC], ("id0", "df"), ("big2",), bias=sc("df"))
-    act(T.iv[:, :], T.idt[:, 0:RING], ("id0", "v"), ("iv",), bias=sc("v"))
-    act(T.mp[:, MO + 800:MO + EW], T.ew[:, 0:EW - 800], ("ew",), ("big4",), scale=0.0, bias=BIG)
-    for k in range(3):
-        act(T.idt[:, UI + NC * k:UI + NC * k + NC], T.idt[:, 0:NC], ("id0",), (("id1", k),), bias=float(UI + NC * k))
-    op("G", lambda: g.affine_select(T.e1[:, :], T.ew[:, :], [[1, 516]], OP.is_equal, 0.0, -3, -4), ("ew",), ("e1",))
-    iota(T.j20[:, :], [[16, 20]], 0, 1, ("j20",))
-    iota(T.t4[:, :], [[DBL, 4]], DBL, 0, ("t4",))
-    iota(T.j16[:, :], [[0, 10], [1, 16]], 0, 0, ("j16",))
-    iota(T.j4[:, :], [[0, 40], [1, 4]], 0, 0, ("j4",))
-    iota(T.ft[:, :], [[0, 512]], 0, 0, ("ft0", "ft1", "ft2"))
-    iota(T.src[:, IDB:IDB + 4 * NC], [[640, 4], [1, NC]], 0, 0, ("idr",))
-
-    ts(T.qi[:, :], L3, 4, OP.arith_shift_right, ("L3",), ("qi",))
-    ts(T.y5[:, 0:130:5], L3, sc("al"), OP.mult, ("L3", "al", "c0"), ("y0",), sc("c0"), OP.add)
-    ts(T.y5[:, 1:130:5], L3, sc("th1"), OP.is_ge, ("L3", "th1", "w"), ("y1",), sc("w"), OP.mult)
-    ts(T.y5[:, 2:130:5], L3, sc("th2"), OP.is_ge, ("L3", "th2", "w"), ("y2",), sc("w"), OP.mult)
-    ts(T.y5[:, 3:130:5], T.qi[:, :], sc("be"), OP.mult, ("qi", "be"), ("y3",))
-    scalar("ui", pair, ("pair",), -640.0, OP.mult, float(UI), OP.add)
-    scan(T.s5[:, :], T.keep[:, :], T.y5[:, :], ("keep", "y0", "y1", "y2", "y3", "y4"), ("s5",))
-    ts(T.ui[:, :], L2, sc("ui"), OP.add, ("L2", "ui"), ("uil",))
-    cp(T.x1[:, :], T.s5[:, 4:130:5], ("s5",), ("x1",))
-    scalar("uv", pair, ("pair",), 640.0, OP.mult, -float(UI), OP.add)
-    fill(T.pl[:, :], BIG, ("pl",))
-    op("V", lambda: g.vector.tensor_copy(T.mp[:, slot(0, 15)].indirect(T.x1[:, :]), T.iv[:, :]), ("iv", "x1"), ("big0", "big1", "big2", "big3", "big4", "inv"))
-    copies = []
-    for e in (0, 2, 4, 6):
-        f = (e - 1) % 8
-        copies.append(("Y", T.mp[rows(e), slot(6, 2)], T.mp[rows(e + 1), slot(6, 2)]))
-        copies.append(("Y", T.mp[rows(e), slot(5 if e else 13)], T.mp[rows(f), slot(7)]))
-        copies.append(("Y", T.mp[rows(e), slot(8)], T.mp[rows(f), slot(8 if e else 0)]))
-    dmas("dM", copies, ("inv",), ("near",))
-    copies = []
-    for e in (0, 2, 4, 6):
-        for h in ((e - 1) % 8, e, e + 1):
-            a = MO + 20 - 20 * e + 20 * h + 300 * ((NC * h >= max(NC * e, 640)) + (h > e))
-            copies.append(("Y", T.pl[rows(h), 10 * e:10 * e + 20], T.mp[GRP * e:GRP * e + 1, a:a + NC]))
-    dmas("dF", copies, ("inv",), ("pl",))
-    idt = ("id0", ("id1", 0), ("id1", 1), ("id1", 2), "uil", "uv")
-    act(T.st[:, 0:NC], T.idt[:, :].indirect(T.ui[:, 6:26]), idt, ("st0",), bias=sc("uv"))
-    act(T.st[:, NC:DBL], T.idt[:, :].indirect(T.ui[:, 0:26]), idt, ("st1",), bias=sc("uv"))
-    copies = []
-    for k in range(4):
-        for first_, n in ((2 * k - 1, 1), (2 * k, 2), (2 * k + 2, 2)):
-            copies.append(("Y", T.src[rows(first_ % 8, n), DBL * k:DBL * k + DBL], T.st[rows(2 * k, n), :]))
-    quant(T.qx, T.sx, 0, NC, T.xt, 0, ("xO", "xG"), ("qxO", "qxG"))
-    for b in range(4):
-        quant(T.qe, T.se, 128 * b, 128 * b + 128, T.e1, 3 - b, ("e1",), (("qe", b),))
-    unpack(0, NC, ("qxO", "qxG"), 4)
-    ts(bi(3), p0, 15, OP.bitwise_and, ("pI",), ("k16",))
-    ts(bi(4), p0, 2, OP.arith_shift_right, ("pI",), ("kk",), 3, OP.bitwise_and)
-    ts(bi(5, 5), T.pI[:, 0:5], 3, OP.bitwise_and, ("pI",), ("p3",))
-    ts(bi(10, 3), T.pI[:, 0:3], 7, OP.bitwise_and, ("pI",), ("p7",))
-    scalar("x3a", par, ("par",), 320.0, OP.mult, float(CEN - NC), OP.add)
-    cp(T.bf[:, 0:6], bi(0, 6), ("g", "par", "pair", "k16", "kk", "p3"), ("bf",))
-    scalar("c3", gI, ("g", "x3a"), -320.0, OP.mult, sc("x3a"), OP.add)
-    ts(T.ul[:, 0:5], bi(5, 5), 32.0, OP.mult, ("p3",), ("ul0",))
-    ts(T.ul[:, 5:8], bi(10, 3), 16.0, OP.mult, ("p7",), ("ul1",))
-    ts(T.x3[:, :], L3, sc("c3"), OP.add, ("L3", "c3"), ("x3",))
-    quant(T.qu, T.su, 0, 128, T.ut, 0, ("ut",), ("qu",))
-    fill(T.ct[:, :], 1.0, ("ct",))
-    dmas("dS", copies, ("st0", "st1"), ("src",))
-    window(0, NC, 4, "SSSS", ("wO", "wG"))
-    tt(T.mp[:, slot(6)], T.mp[:, slot(6)], T.mp[:, slot(8)], OP.min, (), ("near",))
-    inv = T.mp[:, slot(0, 15)]
-    cp(T.mp[:, OWN:OWN + NC], inv.indirect(T.x3[:, 6:26]), ("near", "inv", "x3"), ("ct0",))
-    act(T.mp[:, OWN + NC:OWN + DBL], inv.indirect(T.x3[:, 0:26]), ("near", "inv", "x3"), ("ct1",))
-    copies = []
-    for e in (0, 2, 4, 6):
-        for h, a in ((e + 1, OWN), ((e - 1) % 8, OWN + DBL if e else 0)):
-            copies.append(("Y", T.mp[rows(h), a:a + DBL], T.mp[rows(e), OWN:OWN + DBL]))
-    dmas("dC", copies, (), ("ct0", "ct1"))
-    spread(0, NC, "shG", ("wO", "wG"), ("shO", "shG"))
     dmas("dW", [("Y", T.wq[:, :].bitcast(dt.uint8), T.wc[:, :]), ("Y", T.wsb[:, :], T.ws[:, :])], (), ("wq",))
     dma("Y", "dV", T.vt[:, :], T.v[:, :], (), ("vt",))
 
-    op("V", lambda: g.vector.tensor_copy(T.qu2[:, 0:128].bitcast(dt.uint32), T.qu[:, 0:128].bitcast(dt.uint32).indirect(T.ul[:, 0:8])), ("qu", "ul0", "ul1"), ("qu2",))
-    op("S", lambda: g.scalar.activation(T.su2[:, 0:128], T.su[:, 0:128].indirect(T.ul[:, 0:8]), FN.Copy), ("qu", "ul0", "ul1"), ("su2",))
-    fill(T.ct[0:64, 2:512:4], 0.0, ("ct",))
-    fill(T.nt[:, :], 0.0, ("nt",))
-    fill(T.ct[:, 3:512:4], 0.0, ("ct",))
+    ids = lambda a, n: T.src[:, IDB + a:IDB + a + n]
+    op("G", lambda: g.iota(T.pI[:, 0:2], [[GRP, 2]], 0, 1), (), ("pI",))
+    iota(ids(0, RING), [[1, RING]], 0, 0, ("id0",))
+    fill(T.ew[:, :], 32.0, ("ew",))
+    bi = lambda k, n=1: T.bi[:, k:k + n]
+    gI, pair, par, even = bi(0), bi(1), bi(12), bi(13)
+    ts(gI, T.pI[:, 0:1], 4, OP.arith_shift_right, ("pI",), ("g",))
+    ts(bi(1, 2), T.pI[:, 0:2], 5, OP.arith_shift_right, ("pI",), ("pair",))
+    ts(bi(12, 2), T.pI[:, 0:2], 4, OP.arith_shift_right, ("pI",), ("par",), 1, OP.bitwise_and)
+    scalar("df", gI, ("g",), 320.0, OP.mult, float(IDB - NC), OP.add)
+    scalar("v", pair, ("pair",), float(DBL), OP.mult, 320.0, OP.add)
+    scalar("um", pair, ("pair",), -640.0, OP.mult, float(UI - EB), OP.add)
+    scalar("th1", gI, ("g",), 320.0, OP.mult, 640.0, OP.max)
+    scalar("th2", gI, ("g",), 320.0, OP.mult, 320.0, OP.add)
+    scalar("al", par, ("par",), -19.0, OP.mult, 20.0, OP.add)
+    scalar("c0", par, ("par", "um"), sc("um"), OP.mult, float(EB), OP.add)
+    scalar("w", par, ("par",), -300.0, OP.mult, 300.0, OP.add)
+    scalar("be", par, ("par",), 319.0, OP.mult, -319.0, OP.add)
+    scalar("ui", pair, ("pair",), -640.0, OP.mult, float(UI), OP.add)
+    fill(T.keep[:, :], 1.0, ("keep",))
+    fill(T.y5[:, 4:130:5], 0.0, ("y4",))
+    fill(T.keep[:, 0:130:5], 0.0, ("keep",))
+    scalar("uv", pair, ("pair",), 640.0, OP.mult, -float(UI), OP.add)
+    scalar("u3", even, ("par", "ui"), 6.0 * NC, OP.mult, sc("ui"), OP.add)
+    act(T.mp[:, MO + EB:MO + EB + 512], T.ew[:, 0:512], ("ew",), ("big0",), scale=0.0, bias=BIG)
+    act(T.mp[:, slot(0)], T.ew[:, 0:NC], ("ew",), ("big1",), scale=0.0, bias=BIG)
+    iota(T.mp[:, MO + EB + 512:MO + EB + 800], [[0, 288]], int(BIG), 0, ("big3",))
+    act(T.mp[:, slot(6)], ids(0, NC), ("id0", "df"), ("big2",), bias=sc("df"))
+    act(T.iv[:, :], ids(0, RING), ("id0", "v"), ("iv",), bias=sc("v"))
+    act(T.mp[:, MO + EB + 800:MO + EB + EW], T.ew[:, 0:EW - 800], ("ew",), ("big4",), scale=0.0, bias=BIG)
+    for k in range(3):
+        act(ids(UI + NC * k, NC), ids(0, NC), ("id0",), (("id1", k),), bias=float(UI + NC * k))
+    op("G", lambda: g.affine_select(T.e1[:, :], T.ew[:, :], [[1, 516]], OP.is_equal, 0.0, -3, -4), ("ew",), ("e1",))
+    for a, n, step in ((8, 5, 32), (13, 3, 16), (16, 1, 8)):
+        op("G", lambda: g.iota(T.pI[:, a:a + n], [[0, n]], 0, step), (), (("pJ", a),))
+    op("G", lambda: g.iota(T.pI[:, 20:24], [[32, 4]], 128 + 63, -1), (), ("pQ",))
+    iota(T.t4[:, :], [[DBL, 4]], DBL, 0, ("t4",))
+    iota(T.ct[:, :], [[0, 512]], 1, 0, ("ct",))
+    iota(T.ct[0:64, 2:512:4], [[0, 128]], 0, 0, ("ct",))
+    iota(T.ct[:, 3:512:4], [[0, 128]], 0, 0, ("ct",))
+    iota(T.j20[:, :], [[16, 20]], 0, 1, ("j20",))
+    iota(T.nt[:, :], [[0, 80]], 0, 0, ("nt",))
+    iota(T.j16[:, :], [[0, 10], [1, 16]], 0, 0, ("j16",))
+    iota(T.j4[:, :], [[0, 40], [1, 4]], 0, 0, ("j4",))
+
+    y = lambda k: T.y5[:, k:130:5]
+    ts(T.qi[:, :], L3, 4, OP.arith_shift_right, ("L3",), ("qi",))
+    ts(y(0), L3, sc("al"), OP.mult, ("L3", "al", "c0"), ("y0",), sc("c0"), OP.add)
+    ts(y(1), L3, sc("th1"), OP.is_ge, ("L3", "th1", "w"), ("y1",), sc("w"), OP.mult)
+    ts(y(3), T.qi[:, :], sc("be"), OP.mult, ("qi", "be"), ("y3",))
+    ts(y(2), L3, sc("th2"), OP.is_ge, ("L3", "th2", "w"), ("y2",), sc("w"), OP.mult)
+    ts(T.ui[:, :], L2, sc("ui"), OP.add, ("L2", "ui"), ("uil",))
+    scan(T.s5[:, :], T.keep[:, :], T.y5[:, :], ("keep", "y0", "y1", "y2", "y3", "y4"), ("s5",))
+    fill(T.pl[:, :], BIG, ("pl",))
+    cp(T.x1[:, :], T.s5[:, 4:130:5], ("s5",), ("x1",))
+    ts(T.x3[:, :], L3, sc("u3"), OP.add, ("L3", "u3"), ("x3",))
+    op("V", lambda: g.vector.tensor_copy(T.mp[:, slot(0, 11)].indirect(T.x1[:, :]), T.iv[:, :]), ("iv", "x1"), ("big0", "big1", "big2", "big3", "big4", "inv"))
+    for sem, tok, parts in (("dM", "mid", ((0, 7, 1, 12, 6), (1, 7, 0, 14, 8), (0, 1, 7, 14, 0))), ("dN", "odd", ((0, 7, 1, 13, 7), (1, 7, 0, 11, 7), (0, 1, 7, 19, 7)))):
+        dmas(sem, [("Y", T.mp[rows(a, n), slot(c)], T.mp[rows(b, n), slot(d)]) for a, n, b, c, d in parts], ("inv",), (tok,))
+    copies = []
+    for e, h, n in ((0, 7, 1), (0, 0, 2), (2, 1, 3), (4, 3, 3), (6, 5, 3)):
+        a = MO + EB + 20 * h + 300 * ((NC * h >= max(NC * e, 640)) + (h > e))
+        copies.append(("Y", T.pl[rows(h, n), 10 * e:10 * e + 20], T.mp[GRP * e:GRP * e + 1, a:a + NC * n]))
+    dmas("dF", copies, ("inv",), ("pl",))
+    idt = ("id0", ("id1", 0), ("id1", 1), ("id1", 2), "uil", "uv")
+    act(T.src[:, DBL:DBL + NC], ids(0, UI + 3 * NC).indirect(T.ui[:, 6:26]), idt, ("st0",), bias=sc("uv"))
+    act(T.src[:, DBL + NC:2 * DBL], ids(0, UI + 3 * NC).indirect(T.ui[:, 0:26]), idt, ("st1",), bias=sc("uv"))
+    dmas("dS", [("Y", T.src[rows(a, n), c:c + DBL], T.src[rows(b, n), DBL:2 * DBL]) for a, n, b, c in ((2, 6, 0, 0), (0, 2, 6, 0), (0, 6, 2, 2 * DBL), (6, 2, 0, 2 * DBL))],
+         ("st0", "st1"), ("src",))
+    gate("G", ("st0", "st1"), ())
+    for k in (1, 2):
+        iota(ids(2 * NC * k, NC), [[1, NC]], 2 * NC * k, 0, (("id2", k),))
+    ts(bi(3, 9), T.pI[:, 8:17], 127, OP.bitwise_and, (("pJ", 8), ("pJ", 13), ("pJ", 16)), ("pK",))
+    quant(T.qx, T.sx, 0, NC, T.xt, 0, ("xO", "xG"), ("qxO", "qxG"))
+    cp(T.bf[:, :], bi(0, 12), ("g", "pair", "pK"), ("bf",))
+    cp(T.ul[:, :], bi(3, 8), ("pK",), ("ul",))
+    quant(T.qu, T.su, 0, 128, T.ut, 0, ("ut",), ("qu",))
+    for b in range(4):
+        quant(T.qe, T.se, 128 * b, 128 * b + 128, T.e1, 3 - b, ("e1",), (("qe", b),))
+    unpack(0, NC, ("qxO", "qxG"), LO)
+    op("V", lambda: g.vector.tensor_copy(T.qu2[:, 0:128].bitcast(dt.uint32), T.qu[:, 0:128].bitcast(dt.uint32).indirect(T.ul[:, 0:8])), ("qu", "ul"), ("qu2",))
+    op("S", lambda: g.scalar.activation(T.su2[:, 0:128], T.su[:, 0:128].indirect(T.ul[:, 0:8]), FN.Copy), ("qu", "ul"), ("su2",))
     bf = lambda k: T.bf[:, k:k + 1]
-    line("adj", bf(2), ("bf",), -float(DBL), float(OWN))
+    line("a0", bf(1), ("bf",), -3.0 * DBL, float(OWN))
     line("n", bf(0), ("bf",), -16.0, float(MO + CEN))
-    line("p16", bf(3), ("bf",), -1.0, -0.5)
-    line("p4", bf(4), ("bf",), -1.0, -0.5)
-    line("f1", bf(3), ("bf",), -B, 15 * B)
-    line("fa", bf(4), ("bf",), 4 * B, 4.0 * CEN - 12 * B)
-    line("fb", bf(0), ("bf", "fa"), -1280.0, sc("fa"))
+    line("adj", bf(0), ("bf", "a0"), float(DBL), sc("a0"))
+    ts(bi(20, 4), T.pI[:, 20:24], 5, OP.arith_shift_right, ("pQ",), ("rq",), 3, OP.bitwise_and)
+    fill(T.ft[:, 4 * NP:512], 0.0, ("ftz",))
+    ts(T.rel[:, 4:8], bi(20, 4), -float(DBL), OP.mult, ("rq",), ("rl",), -float(DBL), OP.add)
+    fill(T.ft[:, 3:4 * NP:4], 0.0, ("ft3",))
+    tt(T.rel[:, 0:4], T.rel[:, 4:8], T.t4[:, :], OP.add, ("rl", "t4"), ("rel",))
+    window(0, NC, LO, "SSSS", ("wO", "wG"))
+    tt(T.mp[0:112, slot(12)], T.mp[0:112, slot(12)], T.mp[0:112, slot(14)], OP.min, (), ("mid",))
+    inv = T.mp[:, slot(0, 20)]
+    for e, c, a, b in (("V", 0, 6, 26), ("S", NC, 0, 24), ("V", NC + 16 * 24, 24, 26)):
+        move(e, T.mp[:, OWN + c:OWN + c + 16 * (b - a)], inv.indirect(T.x3[:, a:b]), ("inv", "mid", "odd", "x3"), (("ct", a),))
+    cts = (("ct", 6), ("ct", 0), ("ct", 24))
+    dmas("dC", [("YS"[e // 4], T.mp[rows(h), c:c + DBL], T.mp[rows(e), OWN:OWN + DBL])
+                for e in (0, 2, 4, 6) for h, c in ((e + 1, OWN + DBL), ((e - 1) % 8, OWN + 2 * DBL if e else DBL))], cts, ("near",))
+    spread(0, NC, 0, 16, ("wO", "wG"), "sh")
+    quant(T.qc, T.sct, 0, 128, T.ct, 0, ("ct",), ("qc",))
     for r in range(4):
         act(T.mt[:, r:80:4], T.pl[:, 20 * r:20 * r + 20], ("pl", "adj"), (("mt", r),), bias=sc("adj"))
     act(T.nt[:, 0:80:4], T.j20[:, :], ("j20", "n"), ("nt",), bias=sc("n"))
-    for j, sg, nm in ((T.j16, T.g16, "16"), (T.j4, T.g4, "4")):
+    line("p16", bf(11), ("bf",), -0.125, -0.5)
+    line("k4", bf(3), ("bf",), 1.0 / 128, -0.5)
+    line("f1", bf(11), ("bf",), -B / 8, 15 * B)
+    line("nf1", bf(11), ("bf",), B / 8, -15 * B)
+    line("p4", bf(11), ("bf", "k4"), -1.0 / 32, sc("k4"))
+
+    def pattern(pat, j, sg, nm, beside):
         act(sg[:, :], j[:, :], ("j" + nm, "p" + nm), ("g" + nm,), bias=sc("p" + nm), fn=FN.Sign)
-    act(T.th[:, :], T.t4[:, :], ("t4", "f1"), ("th",), bias=sc("f1"))
-    line("fin", bf(5), ("bf", "fb"), 1.0, sc("fb"))
-    for pat, sg, nm in ((T.p16, T.g16, "16"), (T.p4, T.g4, "4")):
+        line(*beside)
         act(pat[:, :], sg[:, :], ("g" + nm,), ("P" + nm,), scale=8.5 * B, bias=-7.5 * B)
-    quant(T.qc, T.sct, 0, 128, T.ct, 0, ("ct",), ("qc",))
+    pattern(T.p16, T.j16, T.g16, "16", ("fa", sc("p4"), ("p4",), -4 * B, 4.0 * CEN - 14 * B))
+    act(T.th[:, :], T.t4[:, :], ("t4", "f1"), ("th",), bias=sc("f1"))
 
     def score(t):
         a, toks = ((192, ("qxO",)), (0, ("qxG",)), (64, ("qxO", "qxG")))[t]
-        mm(ps[t][:, 0:128], T.qx, T.sx, a, T.qu2, T.su2, 0, 128, toks + ("qu2", "su2"), (("ps", t),))
+        mm(ps[SB[t]][:, 0:128], T.qx, T.sx, a, T.qu2, T.su2, 0, 128, toks + ("qu2", "su2"), (("ps", SB[t]),))
+
+    def compare(t):
+        ts(T.ft[:, t:4 * NP:4], ps[SB[t]][:, 0:NP], 0.0, OP.is_gt, (("ps", SB[t]),), ("ft%d" % t,))
 
     def counts():
-        for t in range(3):
-            ts(T.ft[:, t:4 * NP:4], ps[t][:, 0:NP], 0.0, OP.is_gt, (("ps", t),), ("ft%d" % t,))
-        quant(T.qf, T.sf, 0, 128, T.ft, 0, ("ft0", "ft1", "ft2"), ("qf",))
-        mm(ps[3][:, 0:128], T.qc, T.sct, 0, T.qf, T.sf, 0, 128, ("qc", "qf"), (("ps", 3),))
+        quant(T.qf, T.sf, 0, 128, T.ft, 0, ("ft0", "ft1", "ft2", "ft3", "ftz"), ("qf",))
+        mm(ps[7][:, 0:128], T.qc, T.sct, 0, T.qf, T.sf, 0, 128, ("qc", "qf"), (("ps", 7),))
 
     for t in range(3):
         score(t)
+    for t in range(3):
+        compare(t)
     counts()
 
     def lists(rd):
         cn = lambda k: T.cnt[:, k:k + 1]
-        tt(T.xc[:, :], T.mt[:, :], ps[3][:, 0:80], OP.subtract, four("mt") + (("ps", 3),), ("xc",))
-        cp(T.cnt[:, :], ps[3][:, 80:NP], (("ps", 3),), ("cnt",))
+        tt(T.xc[:, :], T.mt[:, :], ps[7][:, 0:80], OP.subtract, four("mt") + (("ps", 7),), ("xc",))
+        tt(T.cnt[:, :], ps[7][:, 81:NP:2], T.rel[:, 0:4], OP.add, (("ps", 7), "rel"), ("cnt",))
         scan(T.xs[:, :], T.nt[:, :], T.xc[:, :], ("nt", "xc"), ("xs",), OP.max, OP.min)
-        tt(T.df[:, 0:3], T.cnt[:, 1:6:2], T.cnt[:, 3:8:2], OP.subtract, ("cnt",), ("dfc",))
+        tt(T.df[:, 0:3], T.cnt[:, 0:3], T.cnt[:, 1:4], OP.subtract, ("cnt",), ("dfc",))
         cp(T.o1[:, :], T.xs[:, 3:80:4], ("xs",), ("o1",))
-        tab = T.mp[:, 0:MO + WINC]
+        act(T.acs[:, rd:24:3], ps[7][:, 80:NP], (("ps", 7), "cnt"), (("ac", rd),))
+        line("zb", cn(0), ("cnt", "nf1"), -1.0, sc("nf1"))
+        tab = T.mp[:, 0:MO + 8 * NC]
         for h in range(2):
-            move("VS"[h], T.r1[:, HALF * h:HALF * h + HALF], tab.indirect(T.o1[:, 10 * h:10 * h + 10]), ("o1", "near", "inv", "ct0", "ct1"), (("r1", h),))
-        act(T.acs[:, rd:24:3], T.cnt[:, :], ("cnt",), (("ac", rd),))
+            move("VS"[h], T.r1[:, HALF * h:HALF * h + HALF], tab.indirect(T.o1[:, 10 * h:10 * h + 10]), ("o1", "near", "inv") + cts, (("r1", h),))
+        if rd == 0:
+            pattern(T.p4, T.j4, T.g4, "4", ("fb", bf(0), ("bf", "fa"), -1280.0, sc("fa")))
+            line("fin", bf(3), ("bf", "fb"), 1.0 / 32, sc("fb"))
         for h in range(2):
             scan(T.f1[:, HALF * h:HALF * h + HALF], T.p16[:, :], T.r1[:, HALF * h:HALF * h + HALF], ("P16", ("r1", h)), (("f1", h),), OP.add, OP.max)
         x, xt = T.f1[:, 15:NC:16], (("f1", 0), ("f1", 1))
-        ts(T.z5[:, 0:100:5], x, sc("f1"), OP.subtract, xt + ("f1", "cnt"), (("z", 0),), cn(1), OP.subtract)
+        act(T.z5[:, 0:100:5], x, xt + ("zb",), (("z", 0),), bias=sc("zb"))
         for q in range(4):
-            ts(T.z5[:, q + 1:100:5], x, T.th[:, q:q + 1], OP.is_ge, xt + ("th", "dfc", "cnt"), (("z", q + 1),), T.df[:, q:q + 1] if q < 3 else cn(7), OP.mult)
+            ts(T.z5[:, q + 1:100:5], x, T.th[:, q:q + 1], OP.is_ge, xt + ("th", "dfc", "cnt"), (("z", q + 1),), T.df[:, q:q + 1] if q < 3 else cn(3), OP.mult)
         scan(T.zs[:, :], T.keep[:, 0:100], T.z5[:, :], ("keep",) + tuple(("z", q) for q in range(5)), ("zs",))
         cp(T.o2[:, :], T.zs[:, 4:100:5], ("zs",), ("o2",))
         for h in range(2):
-            move("VS"[h], T.r2[:, HALF * h:HALF * h + HALF], T.src[:, :].indirect(T.o2[:, 10 * h:10 * h + 10]), ("o2", "src", "idr"), (("r2", h),))
+            move("VS"[h], T.r2[:, HALF * h:HALF * h + HALF], T.src[:, :].indirect(T.o2[:, 10 * h:10 * h + 10]), ("o2", "src", "st0", "st1", ("id2", 1), ("id2", 2)) + idt, (("r2", h),))
 
     def fold(h):
         scan(T.f2[:, HALF * h:HALF * h + HALF], T.p4[:, :], T.r2[:, HALF * h:HALF * h + HALF], ("P4", ("r2", h)), (("f2", h),), OP.add, OP.max)
@@ -372,7 +369,7 @@ def rank_program(g, core, T, topo):
     def gather(h, tile, tok):
         for k in range(2):
             c = 40 * h + 20 * k
-            move("VS"[k], tile[:, NC * k:NC * k + NC], T.win[:, :].indirect(T.l4[:, c:c + 20]), ("wO", "wG", "shO", "shG", ("l4", h)), ((tok, k),))
+            move("VS"[k], tile[:, NC * k:NC * k + NC], T.win[:, :].indirect(T.l4[:, c:c + 20]), ("wO", "wG", "sh", "shO", "shG", ("l4", h)), ((tok, k),))
 
     def layer(base, b, q, s, qt, start):
         tok = ("ps", base + b)
@@ -380,21 +377,22 @@ def rank_program(g, core, T, topo):
             writer[tok] = [x for x in writer[tok] if x[0] != "cT"]
         mm(ps[base + b][:, 0:HALF], T.wq, T.wsb, 128 * b, q, s, 0, HALF, ("wq",) + qt, (tok,), start, True)
 
-    def store(lo, tok, bank, e):
-        dma("Y", "dOut", T.oc[:, 4 * lo:4 * (lo + HALF)], T.qx[:, lo:lo + HALF].bitcast(dt.uint8), (tok,), ())
-        mm(ps[bank][:, 0:HALF], T.qv, T.sv, 0, T.qx, T.sx, lo, HALF, ("qv", tok), (("ps", bank),))
-        dmas("dOut", [(e, T.osc[4 * k:4 * k + 4, lo:lo + HALF], T.sx[32 * k:32 * k + 4, lo:lo + HALF]) for k in range(4)], (tok,), ())
-        move("VS"[e == "Y"], T.yt[:, lo:lo + HALF], ps[bank][:, 0:HALF], (("ps", bank),), (("y", lo),))
-        dma("Y", "dOut", T.y[:, lo:lo + HALF], T.yt[:, lo:lo + HALF], (("y", lo),), ())
+    def packed(lo, tok, e):
+        dmas("dOut", [(e, T.oc[:, 4 * lo:4 * (lo + HALF)], T.qx[:, lo:lo + HALF].bitcast(dt.uint8))]
+             + [(e, T.osc[4 * k:4 * k + 4, lo:lo + HALF], T.sx[32 * k:32 * k + 4, lo:lo + HALF]) for k in range(4)], (tok,), ())
+
+    def result(lo, bank, e):
+        move(e, T.yt[:, lo:lo + HALF], ps[bank][:, 0:HALF], (("ps", bank),), (("y", lo),))
+        dma("S", "dOut", T.y[:, lo:lo + HALF], T.yt[:, lo:lo + HALF], (("y", lo),), ())
 
     for rd in range(3):
         last = rd == 2
         lists(rd)
         fold(0)
-        offsets(0)
         fold(1)
-        gather(0, T.gt, "gt")
+        offsets(0)
         offsets(1)
+        gather(0, T.gt, "gt")
         quant(T.q2, T.s2, 0, HALF, T.gt, 0, two("gt"), ("q2",))
         dst = T.cores[rank ^ MASKS[rd]]
         rid, pid = topo.addr(dst)[0], topo.addr(dst)[1]
@@ -408,7 +406,7 @@ def rank_program(g, core, T, topo):
         total[arr] += 2 * ne
         mark("G", "sent", total["sent"], ("q2",), ())
         land = ("land", rd)
-        writer[land] = [(arr, 2 * ne, {}, "R")]
+        writer[land] = [(arr, 2 * ne, {})]
         gather(1, T.zo, "zo")
         quant(T.qz, T.sz, 0, HALF, T.zo, 0, two("zo"), ("qz",))
         for b in range(4):
@@ -424,33 +422,42 @@ def rank_program(g, core, T, topo):
             act(T.xt[:, 4 * HALF + b:4 * NC:4], part, (("sm", b),), (("xo", b),), scale=2.0 ** -5)
         join("xO", four("xo"))
         quant(T.qx, T.sx, HALF, NC, T.xt, 4 * HALF, ("xO",), ("qxO",))
-        if not last:
-            unpack(HALF, NC, ("qxO",), 0)
-            window(HALF, NC, 0, "SSSS", ("wO",))
-            spread(HALF, NC, "shO", ("wO",), ("shO",))
-        else:
-            dma("Y", "dOut", T.ac[:, :], T.acs[0:1, 0:24], (("ac", 0), ("ac", 1), ("ac", 2)), ())
-            store(HALF, "qxO", 0, "Y")
         for b in range(4):
             mm(ps[4 + b][:, 0:HALF], T.qe, T.se, 128 * b, lc, ls, 0, HALF, (("qe", b), land), (("ps", 4 + b),), True, False)
             layer(4, b, lc, ls, (land,), False)
-        if not last:
+        if last:
+            dma("Y", "dOut", T.ac[:, :], T.acs[0:1, 0:24], (("ac", 0), ("ac", 1), ("ac", 2)), ())
+            packed(HALF, "qxO", "Y")
+            mm(ps[0][:, 0:HALF], T.qv, T.sv, 0, T.qx, T.sx, HALF, HALF, ("qv", "qxO"), (("ps", 0),))
+        else:
             score(0)
         for e in "VS":
             gate(e, (), ("xG",))
         for b in range(4):
             move("VS"[b % 2], T.xt[:, b:4 * HALF:4], ps[4 + b][:, 0:HALF], (("ps", 4 + b),), (("xg", b),), 2.0 ** -5)
         join("xG", four("xg"))
+        if not last:
+            compare(0)
+            unpack(HALF, NC, ("qxO",), HI)
         quant(T.qx, T.sx, 0, HALF, T.xt, 0, ("xG",), ("qxG",))
         if last:
-            store(0, "qxG", 1, "S")
+            result(HALF, 0, "S")
+            mm(ps[1][:, 0:HALF], T.qv, T.sv, 0, T.qx, T.sx, 0, HALF, ("qv", "qxG"), (("ps", 1),))
+            packed(0, "qxG", "Y")
+            result(0, 1, "V")
         else:
+            gate("Y", (), ("sh",))
+            window(HALF, NC, HI, "VSSS", ("wO",))
+            spread(HALF, NC, 0, 8, ("wO",), "shO")
             score(1)
             score(2)
-            unpack(0, HALF, ("qxG",), 4)
-            window(0, HALF, 4, "SSSS", ("wG",))
-            spread(0, HALF, "shG", ("wG",), ("shG",))
+            unpack(0, HALF, ("qxG",), LO)
+            compare(1)
+            compare(2)
             counts()
+            window(0, HALF, LO, "SSSV", ("wG",))
+            spread(0, HALF, 0, 8, ("wG",), "shG")
+            spread(0, NC, 8, 16, ("wO", "wG"), "sh")
     for s in SEMAPHORES:
         if total[s] and known["Y"].get(s, 0) < total[s]:
             g.sync.wait_ge(T.sem[s], total[s])

@@ -6,33 +6,39 @@ MASKS = (1, 2, 3)
 NC, HALF, GRP, RING, DBL = 320, 160, 16, 416, 736
 CEN = 7 * NC
 WINC = 15 * NC
-OWN = 3 * DBL
-MO = 6 * DBL
-EB, EW = 7 * NC, 1060
+OWN = 0
+MO = OWN + 3 * DBL
 IDB = 4 * DBL
 UI = 6 * NC
 BIG = 1.0e6
 B = 8192.0
-NP = 88
+TINY = 2.0 ** -100
 OP = AluOpType
 FN = ActivationFunctionType
 F32, BF16, I32, U16, U8, X4 = "float32", "bfloat16", "int32", "uint16", "uint8", "float8_e4m3fn_x4"
 
 WIDTHS = {
-    BF16: {"win": 4 * WINC, "xt": 4 * NC, "ew": 516, "e1": 516, "ct": 512, "ft": 512, "ut": 512, "vt": 512, "gt": 4 * HALF, "zo": 4 * HALF, "z32": 4 * HALF},
+    BF16: {"win": 4 * WINC, "sg": 2 * NC, "xt": 4 * NC, "ew": 516, "e1": 516, "ft": 512, "ut": 512, "vt": 512,
+           "gt": 4 * HALF, "zo": 4 * HALF, "z32": 4 * HALF},
     F32: {"mp": MO + 20 * NC, "src": IDB + UI + 3 * NC, "iv": RING, "sc": 32, "bf": 12, "y5": 130, "s5": 130, "keep": 130,
-          "j20": 20, "j16": HALF, "j4": HALF, "g16": HALF, "g4": HALF, "p16": HALF, "p4": HALF, "t4": 4, "th": 4, "pl": 80, "mt": 80, "nt": 80, "xc": 80, "xs": 80,
-          "rel": 8, "cnt": 4, "df": 4, "r1": NC, "f1": NC, "r2": NC, "f2": NC, "z5": 100, "zs": 100, "acs": 24, "sm": 4 * HALF, "yt": NC},
+          "j16": HALF, "j4": HALF, "g16": HALF, "tg": 2, "g4": HALF, "p16": HALF, "xc": 60, "xs": 60, "lo": 60, "p4": HALF, "t4": 4, "th": 4, "pl": 40,
+          "ca": 40, "rel": 8, "cn": 8, "no": 2, "df": 4, "r1": NC, "f1": NC, "r2": NC, "f2": NC,
+          "z5": 100, "zs": 100, "acs": 24, "sm": 4 * HALF, "yt": NC},
     I32: {"ri": 84, "qi": 26, "pI": 24, "bi": 32},
-    U16: {"x1": 26, "x3": 26, "ui": 26, "ul": 8, "o1": 20, "o2": 20, "l4": 80},
-    X4: {"qe": 512, "qc": 128, "qf": 128, "qu": 128, "qu2": 128, "qv": 128, "wq": 512, "qx": NC, "q2": HALF, "qz": HALF, "lc0": HALF, "lc1": HALF, "lc2": HALF},
-    U8: {"se": 512, "sct": 128, "sf": 128, "su": 128, "su2": 128, "sv": 128, "wsb": 512, "sx": NC, "s2": HALF, "sz": HALF, "ls0": HALF, "ls1": HALF, "ls2": HALF},
+    U16: {"x1": 26, "x3": 26, "ui": 26, "ul": 12, "o1": 20, "o2": 20, "l4": 80},
+    X4: {"qe": 512, "qc": 128, "qf": 128, "qu": 128, "qu2": 176, "qv": 128, "wq": 512, "qx": NC, "q2": HALF, "qz": HALF, "lc0": HALF, "lc1": HALF, "lc2": HALF},
+    U8: {"se": 512, "sct": 128, "sf": 128, "su": 128, "su2": 176, "sv": 128, "wsb": 512, "sx": NC, "s2": HALF, "sz": HALF, "ls0": HALF, "ls1": HALF, "ls2": HALF},
 }
 SCRATCH = {name: ("sbuf", [128, n], t) for t, d in WIDTHS.items() for name, n in d.items()}
 for _b in range(8):
     SCRATCH["ps%d" % _b] = ("psum", [128, 512], "float32")
 LOCAL = ("dM", "dN", "d2", "d3", "dX", "dU", "dV", "dW", "sh", "shO", "shG", "dS", "dF", "dC", "dOut")
-SEMAPHORES = ["cV", "cS", "cT", "cG", "arr0", "arr1", "arr2", "sent"] + list(LOCAL)
+SEMAPHORES = ["cV", "cS", "cT", "cG", "arr0", "arr1", "arr2", "sent0", "sent1", "sent2"] + list(LOCAL)
+
+CYCLE, CALL, WAKE, PE = 0.92e-3, 0.0, 0.21, 0.7e-3
+ISSUE, START, ROW, BYTE = 0.05, 0.8, 0.015, 1 / 45.0e3
+RISSUE, RFIRST, RSTART, RBYTE = 0.1, 0.65, 0.8, 1 / 45.0e3
+SLACK = 0.03
 
 
 def shifts():
@@ -45,119 +51,125 @@ def shifts():
     return out
 
 
+def fit(busy, t, d):
+    for a, b in busy:
+        if t + d <= a + SLACK:
+            break
+        t = max(t, b)
+    return t
+
+
+def plan(nodes):
+    busy = {e: [] for e in "VSTGYW"}
+    for x in nodes:
+        t = max([nodes[d]["done"] + (0.0 if d in x["loose"] else WAKE) for d in x["deps"]] + [0.0])
+        if x["wire"]:
+            e = list(x["cost"])[0]
+            if e == "G":
+                t = fit(busy[e], t, x["cost"][e])
+                busy[e] = sorted(busy[e] + [(t, t + x["cost"][e])])
+            lead = x["lead"] + x["late"] / 2
+            w = fit(busy["W"], t + lead, x["wire"])
+            busy["W"] = sorted(busy["W"] + [(w, w + x["wire"])])
+            x["start"], x["done"] = t if e == "G" else w - lead, w + max(x["wire"], x["cost"][e] - x["lead"]) + x["late"] / 2
+        else:
+            x["done"], e = min((fit(busy[e], t, d) + d, e) for e, d in x["cost"].items())
+            x["start"] = x["done"] - x["cost"][e]
+            busy[e] = sorted(busy[e] + [(x["start"], x["done"])])
+        x["on"] = e
+    return [(i, nodes[i]["on"]) for i in sorted(range(len(nodes)), key=lambda i: (nodes[i]["start"], i))]
+
+
 def rank_program(g, core, T, topo):
     rank = T.rank_of(core)
     if rank is None:
         return
     eng = {"V": g.vector, "S": g.scalar, "T": g.tensor, "G": g, "Y": g.sync}
-    own_sem = {"V": "cV", "S": "cS", "T": "cT", "G": "cG"}
-    total = {s: 0 for s in SEMAPHORES}
-    known = {e: {} for e in eng}
-    writer, reader = {}, {}
+    nodes, writer, reader = [], {}, {}
 
-    def gate(e, r, w):
-        need = []
-        for t in r:
-            need += writer.get(t, [])
+    def node(cost, call, r, w, late=0.0, wire=0.0, sem=None, lead=0.0):
+        r, w = tuple(r), tuple(w)
+        w += tuple(t for t in r if t[0] == "ps")
+        deps = set()
+        for t in r + w:
+            deps.update(writer.get(t, ()))
         for t in w:
-            need += writer.get(t, [])
-            need += reader.get(t, [])
-        best = {}
-        for sem, val, clk in need:
-            v = total[sem] if sem in LOCAL else val
-            best[sem] = max(best.get(sem, 0), v)
-        clks = {}
-        for sem, val, clk in need:
-            for s, v in clk.items():
-                if s != sem and s not in LOCAL:
-                    clks.setdefault(s, []).append((sem, v))
-        for sem in best:
-            v = best[sem]
-            if known[e].get(sem, 0) >= v:
-                continue
-            if any(o != sem and o in best and x >= v for o, x in clks.get(sem, [])):
-                continue
-            eng[e].wait_ge(T.sem[sem], v)
-        for sem, val, clk in need:
-            for s, v in clk.items():
-                known[e][s] = max(known[e].get(s, 0), v)
-        for sem in best:
-            known[e][sem] = max(known[e].get(sem, 0), best[sem])
-
-    def mark(e, sem, val, r, w):
-        clk = dict(known[e])
-        clk[sem] = val
-        x = (sem, val, clk)
-        for t in w:
-            writer[t] = [x]
-            reader[t] = []
+            deps.update(reader.get(t, ()))
+        i = len(nodes)
+        loose = set(d for d in deps if "T" in cost and "T" in nodes[d]["cost"])
+        nodes.append({"cost": cost, "call": call, "deps": deps, "loose": loose, "late": late, "wire": wire, "sem": sem, "toks": r + w, "lead": lead})
         for t in r:
-            reader.setdefault(t, []).append(x)
+            reader.setdefault(t, []).append(i)
+        for t in w:
+            writer[t], reader[t] = [i], []
 
-    def op(e, call, r, w):
-        gate(e, r, w)
-        s = own_sem[e]
-        total[s] += 1
-        call().then_inc(T.sem[s], 1)
-        mark(e, s, total[s], r, w)
+    def width(ap):
+        return int(ap.shape[1])
 
-    def dmas(sem, copies, r, w):
-        for e in sorted(set(c[0] for c in copies)):
-            gate(e, r, w)
-        for e, out, in_ in copies:
-            total[sem] += 16
-            eng[e].dma_start(out, in_).then_inc(T.sem[sem], 16)
-        mark(copies[0][0], sem, total[sem], r, w)
+    def span(n):
+        return CALL + CYCLE * max(n, 64)
 
-    def dma(e, sem, out, in_, r, w):
-        dmas(sem, [(e, out, in_)], r, w)
+    def picked(e, n):
+        return CALL + {"V": 0.06, "S": 0.08}[e] + 1.5 * CYCLE * n
+
+    def dmas(sem, copies, r, w, size):
+        wire = sum((int(o.shape[0]) + 15) // 16 * (ROW + BYTE * size * width(o)) for o, i in copies)
+        node({"Y": ISSUE * len(copies)}, lambda e: [g.sync.dma_start(o, i) for o, i in copies], r, w, START, wire, sem)
+
+    def send(rd, pairs, r, land):
+        dst = T.cores[rank ^ MASKS[rd]]
+        rid, pid = topo.addr(dst)[0], topo.addr(dst)[1]
+        ne, arr, sent, lead = len(topo.engines(core, dst)), "arr%d" % rd, "sent%d" % rd, 0.0 if rd else RFIRST
+        call = lambda e: [g.remote_dma(o, i, T.sem[arr], T.sem[sent], pid, rid, topo.mask(core, dst)) for o, i, n in pairs]
+        node({"G": RISSUE * len(pairs) + lead}, call, r, (land,), RSTART, sum(128 // ne * (ROW + RBYTE * n) for o, i, n in pairs), (arr, sent, ne * len(pairs), land), lead)
 
     def ts(out, in0, s1, o1, r, w, s2=None, o2=None):
         if o2 is None:
-            op("V", lambda: g.vector.tensor_scalar(out, in0, s1, None, o1), r, w)
+            node({"V": span(width(out))}, lambda e: g.vector.tensor_scalar(out, in0, s1, None, o1), r, w)
         else:
-            op("V", lambda: g.vector.tensor_scalar(out, in0, s1, s2, o1, o2), r, w)
+            node({"V": span(width(out))}, lambda e: g.vector.tensor_scalar(out, in0, s1, s2, o1, o2), r, w)
 
-    def tt(out, in0, in1, o, r, w):
-        op("V", lambda: g.vector.tensor_tensor(out, in0, in1, o), r, w)
+    def tt(out, in0, in1, o, r, w, both=2):
+        node({"V": span(both * width(out))}, lambda e: g.vector.tensor_tensor(out, in0, in1, o), r, w)
 
     def cp(out, in_, r, w):
-        op("V", lambda: g.vector.tensor_copy(out, in_), r, w)
+        node({"V": span(width(out))}, lambda e: g.vector.tensor_copy(out, in_), r, w)
 
-    def fill(ap, c, w):
-        op("V", lambda: g.vector.memset(ap, c), (), w)
+    def affine(out, in_, r, w, scale=1.0, bias=0.0, who="VS", pick=False):
+        def call(e):
+            plain = isinstance(bias, float) and bias == 0.0
+            if e == "S":
+                return g.scalar.activation(out, in_, FN.Copy, scale=scale) if plain else g.scalar.activation(out, in_, FN.Identity, bias=bias, scale=scale)
+            if isinstance(scale, float) and scale == 1.0:
+                return g.vector.tensor_copy(out, in_) if plain else g.vector.tensor_scalar(out, in_, bias, None, OP.add)
+            return g.vector.tensor_scalar(out, in_, scale, None, OP.mult) if plain else g.vector.tensor_scalar(out, in_, scale, bias, OP.mult, OP.add)
+        node({e: picked(e, width(out)) if pick else span(width(out)) for e in who}, call, r, w)
 
-    def act(out, in_, r, w, scale=1.0, bias=None, fn=None):
-        if bias is None:
-            op("S", lambda: g.scalar.activation(out, in_, fn or FN.Copy, scale=scale), r, w)
+    def fill(ap, c, w, e, half=False):
+        n = width(ap)
+        if e == "V":
+            node({e: span(n // 2 if half else n)}, lambda e: g.vector.memset(ap, c), (), w)
         else:
-            op("S", lambda: g.scalar.activation(out, in_, fn or FN.Identity, bias=bias, scale=scale), r, w)
+            affine(ap, T.ew[:, 0:n], ("ew",), w, 0.0, c, e)
 
-    def iota(out, pattern, base, step, w):
-        op("G", lambda: g.iota(out, pattern, base, step, allow_small_or_imprecise_dtypes=True), (), w)
+    def iota(out, pattern, base, step, w, whole=False):
+        call = lambda e: g.iota(out, pattern, base, step) if whole else g.iota(out, pattern, base, step, allow_small_or_imprecise_dtypes=True)
+        node({"G": 0.16 + 2 * CYCLE * width(out)}, call, (), w)
 
     def scan(out, k, d, r, w, o0=OP.mult, o1=OP.add):
-        op("V", lambda: g.vector.tensor_tensor_scan(out, k, d, 0.0, o0, o1), r, w)
+        node({"V": span(width(out))}, lambda e: g.vector.tensor_tensor_scan(out, k, d, 0.0, o0, o1), r, w)
 
     def quant(q, s, a, b, tile, c0, r, w):
-        op("V", lambda: g.vector.quantize_mx(q[:, a:b], s[:, a:b], tile[:, c0:c0 + 4 * (b - a)]), r, w)
+        node({"V": CALL + 0.014 + 1.06 * CYCLE * (b - a)}, lambda e: g.vector.quantize_mx(q[:, a:b], s[:, a:b], tile[:, c0:c0 + 4 * (b - a)]), r, w)
 
-    def mm(out, l, ls, la, m, ms, ma, n, r, w, start=True, stop=True):
-        op("T", lambda: g.tensor.matmul_mx(out, l[:, la:la + 128], ls[:, la:la + 128], m[:, ma:ma + n], ms[:, ma:ma + n], start, stop), r, w)
-
-    def move(e, out, in_, r, w, scale=1.0):
-        if e == "S":
-            act(out, in_, r, w, scale=scale)
-        elif scale == 1.0:
-            cp(out, in_, r, w)
-        else:
-            ts(out, in_, scale, OP.mult, r, w)
+    def mm(bank, l, ls, la, m, ms, ma, n, r, start=True, stop=True, w=()):
+        node({"T": PE * (n + 16)}, lambda e: g.tensor.matmul_mx(ps[bank][:, 0:n], l[:, la:la + 128], ls[:, la:la + 128], m[:, ma:ma + n], ms[:, ma:ma + n], start, stop),
+             r, (("ps", bank),) + w)
 
     ps = [T["ps%d" % b] for b in range(8)]
     rows = lambda h, n=1: slice(GRP * h, GRP * (h + n))
     slot = lambda k, n=1: slice(MO + NC * k, MO + NC * (k + n))
     four = lambda t: tuple((t, b) for b in range(4))
-    two = lambda t: ((t, 0), (t, 1))
     names = {}
 
     def sc(name):
@@ -167,297 +179,313 @@ def rank_program(g, core, T, topo):
     def scalar(name, in0, r, s1, o1, s2=None, o2=None):
         ts(sc(name), in0, s1, o1, r, (name,), s2, o2)
 
-    def line(name, in0, r, scale, bias):
-        act(sc(name), in0, r, (name,), scale=scale, bias=bias)
+    def line(name, in0, r, scale, bias, who="VS"):
+        affine(sc(name), in0, r, (name,), scale, bias, who)
 
-    def join(tok, parts):
-        writer[tok], reader[tok] = sum([writer[t] for t in parts], []), []
-
-    SB, HI, LO = (0, 4, 5), (1, 2, 3, 0), (6, 1, 2, 3)
-
-    def unpack(lo, hi, toks, banks):
+    def unpack(q, s, lo, hi, toks, banks):
         for b, k in enumerate(banks):
-            mm(ps[k][:, 0:hi - lo], T.qe, T.se, 128 * b, T.qx, T.sx, lo, hi - lo, (("qe", b),) + toks, (("ps", k),))
+            mm(k, T.qe, T.se, 128 * b, q, s, lo, hi - lo, (("qe", b),) + toks)
 
-    def window(lo, hi, banks, who, toks):
-        for e in sorted(set(who) - {" "}):
-            gate(e, (), toks)
+    def out_of(banks, n, tile, c0, toks):
         for b, k in enumerate(banks):
-            if who[b] != " ":
-                move(who[b], T.win[:, 4 * (CEN + lo) + b:4 * (CEN + hi):4], ps[k][:, 0:hi - lo], (("ps", k),), (("w", lo, b),), 2.0 ** -5)
-        for t in toks:
-            join(t, [("w", lo, b) for b in range(4)])
+            affine(tile[:, c0 + b:c0 + 4 * n:4], ps[k][:, 0:n], (("ps", k),), [(t, b) for t in toks], 2.0 ** -5)
 
     def spread(lo, hi, a, b, r, sem):
-        dmas(sem, [("Y", T.win[p0:p1, 4 * (NC * k + lo):4 * (NC * k + hi)], T.win[q0:q0 + p1 - p0, 4 * (CEN + lo):4 * (CEN + hi)])
-                   for p0, p1, q0, k in shifts()[a:b]], r, (sem,))
+        dmas(sem, [(T.win[p0:p1, 4 * (NC * k + lo):4 * (NC * k + hi)], T.win[q0:q0 + p1 - p0, 4 * (CEN + lo):4 * (CEN + hi)])
+                   for p0, p1, q0, k in shifts()[a:b]], r, (sem,), 2)
 
     L3, L2 = T.ri[:, 0:26], T.ri[:, 28:54]
-    dma("Y", "d3", L3, T.ring[:, :], (), ("L3",))
-    dmas("d2", [("YS"[h % 2], T.ri[rows(h), 28:54], T.ring[rows(h | 1), :]) for h in range(8)], (), ("L2",))
-    dma("Y", "dX", T.xt[:, :], T.x[:, :], (), ("xO", "xG"))
-    dma("Y", "dU", T.ut[:, :], T.u[:, :], (), ("ut",))
-    dmas("dW", [("Y", T.wq[:, :].bitcast(dt.uint8), T.wc[:, :]), ("Y", T.wsb[:, :], T.ws[:, :])], (), ("wq",))
-    dma("Y", "dV", T.vt[:, :], T.v[:, :], (), ("vt",))
+    dmas("d3", [(L3, T.ring[:, :])], (), ("L3",), 4)
+    dmas("dX", [(T.xt[:, :], T.x[:, :])], (), four("xO") + four("xG"), 2)
+    dmas("dU", [(T.ut[:, :], T.u[:, :])], (), ("ut",), 2)
+    dmas("d2", [(T.ri[rows(h), 28:54], T.ring[rows(h | 1), :]) for h in range(8)], (), ("L2",), 4)
+    dmas("dW", [(T.wq[:, :].bitcast(dt.uint8), T.wc[:, :]), (T.wsb[:, :], T.ws[:, :])], (), ("wq",), 1)
+    dmas("dV", [(T.vt[:, :], T.v[:, :])], (), ("vt",), 2)
 
     ids = lambda a, n: T.src[:, IDB + a:IDB + a + n]
-    op("G", lambda: g.iota(T.pI[:, 0:2], [[GRP, 2]], 0, 1), (), ("pI",))
-    iota(ids(0, RING), [[1, RING]], 0, 0, ("id0",))
-    fill(T.ew[:, :], 32.0, ("ew",))
     bi = lambda k, n=1: T.bi[:, k:k + n]
-    gI, pair, par, even = bi(0), bi(1), bi(12), bi(13)
-    ts(gI, T.pI[:, 0:1], 4, OP.arith_shift_right, ("pI",), ("g",))
-    ts(bi(1, 2), T.pI[:, 0:2], 5, OP.arith_shift_right, ("pI",), ("pair",))
-    ts(bi(12, 2), T.pI[:, 0:2], 4, OP.arith_shift_right, ("pI",), ("par",), 1, OP.bitwise_and)
-    scalar("df", gI, ("g",), 320.0, OP.mult, float(IDB - NC), OP.add)
-    scalar("v", pair, ("pair",), float(DBL), OP.mult, 320.0, OP.add)
-    scalar("um", pair, ("pair",), -640.0, OP.mult, float(UI - EB), OP.add)
-    scalar("th1", gI, ("g",), 320.0, OP.mult, 640.0, OP.max)
-    scalar("th2", gI, ("g",), 320.0, OP.mult, 320.0, OP.add)
-    scalar("al", par, ("par",), -19.0, OP.mult, 20.0, OP.add)
-    scalar("c0", par, ("par", "um"), sc("um"), OP.mult, float(EB), OP.add)
-    scalar("w", par, ("par",), -300.0, OP.mult, 300.0, OP.add)
-    scalar("be", par, ("par",), 319.0, OP.mult, -319.0, OP.add)
-    scalar("ui", pair, ("pair",), -640.0, OP.mult, float(UI), OP.add)
-    fill(T.keep[:, :], 1.0, ("keep",))
-    fill(T.y5[:, 4:130:5], 0.0, ("y4",))
-    fill(T.keep[:, 0:130:5], 0.0, ("keep",))
-    scalar("uv", pair, ("pair",), 640.0, OP.mult, -float(UI), OP.add)
-    scalar("u3", even, ("par", "ui"), 6.0 * NC, OP.mult, sc("ui"), OP.add)
-    act(T.mp[:, MO + EB:MO + EB + 512], T.ew[:, 0:512], ("ew",), ("big0",), scale=0.0, bias=BIG)
-    act(T.mp[:, slot(0)], T.ew[:, 0:NC], ("ew",), ("big1",), scale=0.0, bias=BIG)
-    iota(T.mp[:, MO + EB + 512:MO + EB + 800], [[0, 288]], int(BIG), 0, ("big3",))
-    act(T.mp[:, slot(6)], ids(0, NC), ("id0", "df"), ("big2",), bias=sc("df"))
-    act(T.iv[:, :], ids(0, RING), ("id0", "v"), ("iv",), bias=sc("v"))
-    act(T.mp[:, MO + EB + 800:MO + EB + EW], T.ew[:, 0:EW - 800], ("ew",), ("big4",), scale=0.0, bias=BIG)
-    for k in range(3):
-        act(ids(UI + NC * k, NC), ids(0, NC), ("id0",), (("id1", k),), bias=float(UI + NC * k))
-    op("G", lambda: g.affine_select(T.e1[:, :], T.ew[:, :], [[1, 516]], OP.is_equal, 0.0, -3, -4), ("ew",), ("e1",))
-    for a, n, step in ((8, 5, 32), (13, 3, 16), (16, 1, 8)):
-        op("G", lambda: g.iota(T.pI[:, a:a + n], [[0, n]], 0, step), (), (("pJ", a),))
-    op("G", lambda: g.iota(T.pI[:, 20:24], [[32, 4]], 128 + 63, -1), (), ("pQ",))
-    iota(T.t4[:, :], [[DBL, 4]], DBL, 0, ("t4",))
-    iota(T.ct[:, :], [[0, 512]], 1, 0, ("ct",))
-    iota(T.ct[0:64, 2:512:4], [[0, 128]], 0, 0, ("ct",))
-    iota(T.ct[:, 3:512:4], [[0, 128]], 0, 0, ("ct",))
-    iota(T.j20[:, :], [[16, 20]], 0, 1, ("j20",))
-    iota(T.nt[:, :], [[0, 80]], 0, 0, ("nt",))
-    iota(T.j16[:, :], [[0, 10], [1, 16]], 0, 0, ("j16",))
-    iota(T.j4[:, :], [[0, 40], [1, 4]], 0, 0, ("j4",))
+    bf = lambda k: T.bf[:, k:k + 1]
+    GR, PAIR, PAR, EVEN, P16, Q4 = 0, 2, 4, 5, 6, 7
+    part = T.pI[:, 0:1]
+    iota(T.pI[:, 0:2], [[GRP, 2]], 0, 1, ("pI",), True)
+    iota(ids(0, RING), [[1, RING]], 0, 0, ("id0",))
+    fill(T.ew[:, :], 32.0, ("ew",), "V", True)
+    ts(bi(GR, 2), T.pI[:, 0:2], 4, OP.arith_shift_right, ("pI",), ("g",))
+    ts(bi(PAR, 2), T.pI[:, 0:2], 4, OP.arith_shift_right, ("pI",), ("par",), 1, OP.bitwise_and)
+    ts(bi(PAIR, 2), T.pI[:, 0:2], 5, OP.arith_shift_right, ("pI",), ("pair",))
+    fill(T.mp[:, slot(8)], BIG, ("big0",), "S")
+    fill(T.mp[:, slot(0)], BIG, ("big1",), "S")
+    scalar("w", bi(EVEN), ("par",), 300.0, OP.mult)
+    cp(T.bf[:, 0:6], bi(0, 6), ("g", "pair", "par"), ("bf",))
+    scalar("al", bi(EVEN), ("par",), 19.0, OP.mult, 1.0, OP.add)
+    scalar("c0", bi(GR), ("g", "w"), -1.0, OP.add, sc("w"), OP.mult)
+    ts(T.tg[:, :], bi(GR, 2), 320.0, OP.mult, ("g",), ("tg",))
+    scalar("be", bi(EVEN), ("par",), -319.0, OP.mult)
+    scalar("w3", bi(GR), ("g",), 0.0, OP.is_equal, -2680.0, OP.mult)
+    line("a6", bf(GR), ("bf",), 320.0, IDB - NC - BIG, "S")
+    line("vv", bf(PAIR), ("bf",), float(DBL), 0.0, "S")
+    line("c1", bf(GR), ("bf",), -320.0, float(CEN), "S")
+    line("d6", sc("a6"), ("a6", "bf"), bf(PAR), BIG, "S")
+    line("v", sc("vv"), ("vv", "bf"), bf(PAR), 320.0, "S")
+    affine(T.mp[:, slot(6)], ids(0, NC), ("id0", "d6", "bf"), ("big2",), bf(PAR), sc("d6"), "S")
+    affine(T.iv[:, :], ids(0, RING), ("id0", "v"), ("iv",), 1.0, sc("v"), "S")
 
     y = lambda k: T.y5[:, k:130:5]
     ts(T.qi[:, :], L3, 4, OP.arith_shift_right, ("L3",), ("qi",))
     ts(y(0), L3, sc("al"), OP.mult, ("L3", "al", "c0"), ("y0",), sc("c0"), OP.add)
-    ts(y(1), L3, sc("th1"), OP.is_ge, ("L3", "th1", "w"), ("y1",), sc("w"), OP.mult)
+    fill(T.keep[:, :], 1.0, ("keep",), "V")
+    for k in range(2):
+        ts(y(1 + k), L3, T.tg[:, k:k + 1], OP.is_ge, ("L3", "tg", "w"), ("y%d" % (1 + k),), sc("w"), OP.mult)
+    fill(T.keep[:, 0:130:5], 0.0, ("keep",), "V")
+    ts(y(4), L3, 2.0 * NC, OP.is_ge, ("L3", "w3"), ("y4",), sc("w3"), OP.mult)
     ts(y(3), T.qi[:, :], sc("be"), OP.mult, ("qi", "be"), ("y3",))
-    ts(y(2), L3, sc("th2"), OP.is_ge, ("L3", "th2", "w"), ("y2",), sc("w"), OP.mult)
-    ts(T.ui[:, :], L2, sc("ui"), OP.add, ("L2", "ui"), ("uil",))
     scan(T.s5[:, :], T.keep[:, :], T.y5[:, :], ("keep", "y0", "y1", "y2", "y3", "y4"), ("s5",))
-    fill(T.pl[:, :], BIG, ("pl",))
-    cp(T.x1[:, :], T.s5[:, 4:130:5], ("s5",), ("x1",))
-    ts(T.x3[:, :], L3, sc("u3"), OP.add, ("L3", "u3"), ("x3",))
-    op("V", lambda: g.vector.tensor_copy(T.mp[:, slot(0, 11)].indirect(T.x1[:, :]), T.iv[:, :]), ("iv", "x1"), ("big0", "big1", "big2", "big3", "big4", "inv"))
+    ts(T.x1[:, :], T.s5[:, 4:130:5], sc("c1"), OP.add, ("s5", "c1"), ("x1",))
+    node({"V": 0.08 + 3.5 * CYCLE * RING}, lambda e: g.vector.tensor_copy(T.mp[:, slot(0, 9)].indirect(T.x1[:, :]), T.iv[:, :]), ("iv", "x1"), ("big0", "big1", "big2", "inv"))
     for sem, tok, parts in (("dM", "mid", ((0, 7, 1, 12, 6), (1, 7, 0, 14, 8), (0, 1, 7, 14, 0))), ("dN", "odd", ((0, 7, 1, 13, 7), (1, 7, 0, 11, 7), (0, 1, 7, 19, 7)))):
-        dmas(sem, [("Y", T.mp[rows(a, n), slot(c)], T.mp[rows(b, n), slot(d)]) for a, n, b, c, d in parts], ("inv",), (tok,))
-    copies = []
-    for e, h, n in ((0, 7, 1), (0, 0, 2), (2, 1, 3), (4, 3, 3), (6, 5, 3)):
-        a = MO + EB + 20 * h + 300 * ((NC * h >= max(NC * e, 640)) + (h > e))
-        copies.append(("Y", T.pl[rows(h, n), 10 * e:10 * e + 20], T.mp[GRP * e:GRP * e + 1, a:a + NC * n]))
-    dmas("dF", copies, ("inv",), ("pl",))
-    idt = ("id0", ("id1", 0), ("id1", 1), ("id1", 2), "uil", "uv")
-    act(T.src[:, DBL:DBL + NC], ids(0, UI + 3 * NC).indirect(T.ui[:, 6:26]), idt, ("st0",), bias=sc("uv"))
-    act(T.src[:, DBL + NC:2 * DBL], ids(0, UI + 3 * NC).indirect(T.ui[:, 0:26]), idt, ("st1",), bias=sc("uv"))
-    dmas("dS", [("Y", T.src[rows(a, n), c:c + DBL], T.src[rows(b, n), DBL:2 * DBL]) for a, n, b, c in ((2, 6, 0, 0), (0, 2, 6, 0), (0, 6, 2, 2 * DBL), (6, 2, 0, 2 * DBL))],
-         ("st0", "st1"), ("src",))
-    gate("G", ("st0", "st1"), ())
-    for k in (1, 2):
-        iota(ids(2 * NC * k, NC), [[1, NC]], 2 * NC * k, 0, (("id2", k),))
-    ts(bi(3, 9), T.pI[:, 8:17], 127, OP.bitwise_and, (("pJ", 8), ("pJ", 13), ("pJ", 16)), ("pK",))
-    quant(T.qx, T.sx, 0, NC, T.xt, 0, ("xO", "xG"), ("qxO", "qxG"))
-    cp(T.bf[:, :], bi(0, 12), ("g", "pair", "pK"), ("bf",))
-    cp(T.ul[:, :], bi(3, 8), ("pK",), ("ul",))
+        dmas(sem, [(T.mp[rows(a, n), slot(c)], T.mp[rows(b, n), slot(d)]) for a, n, b, c, d in parts], ("inv",), (tok,), 4)
+    line("ui", bf(PAIR), ("bf",), -640.0, float(UI), "S")
+    line("u3", bf(EVEN), ("bf", "ui"), 6.0 * NC, sc("ui"), "S")
+    ts(T.ui[:, :], L2, sc("ui"), OP.add, ("L2", "ui"), ("uil",))
+    tt(T.mp[0:112, slot(12)], T.mp[0:112, slot(12)], T.mp[0:112, slot(14)], OP.min, (), ("mid",))
+    ts(T.x3[:, :], L3, sc("u3"), OP.add, ("L3", "u3"), ("x3",))
+    for e, c, a, b in (("V", 0, 6, 26), ("S", NC, 0, 22), ("V", NC + 16 * 22, 22, 26)):
+        affine(T.mp[:, OWN + c:OWN + c + 16 * (b - a)], T.mp[:, slot(0, 20)].indirect(T.x3[:, a:b]), ("inv", "mid", "odd", "x3"), (("ct", a),), who=e, pick=True)
+    cts = (("ct", 6), ("ct", 0), ("ct", 22))
+    dmas("dC", [(T.mp[rows(h), c:c + DBL], T.mp[rows(e), OWN:OWN + DBL])
+                for e in (0, 2, 4, 6) for h, c in ((e + 1, OWN + DBL), ((e - 1) % 8, OWN + 2 * DBL))], cts, ("near",), 4)
+    iota(T.pl[:, :], [[0, 40]], int(BIG), 0, ("pl",))
+    dmas("dF", [(T.pl[rows(h, n), c:c + 20], T.mp[GRP * e:GRP * e + 1, slot(k, n)])
+                for e in (0, 2, 4, 6) for h, n, c, k in ((e, 2, 0, 7), ((e - 1) % 8, 1, 20, 6 if e else 0))], ("inv",), ("pl",), 4)
+    node({"G": 0.2 + 2 * CYCLE * 516}, lambda e: g.affine_select(T.e1[:, :], T.ew[:, :], [[1, 516]], OP.is_equal, 0.0, -3, -4), ("ew",), ("e1",))
+    iota(T.pI[:, 8:18], [[32, 5], [0, 2]], 0, 0, ("pJ",), True)
+    quant(T.qx, T.sx, 0, NC, T.xt, 0, four("xO") + four("xG"), ("qxO", "qxG"))
     quant(T.qu, T.su, 0, 128, T.ut, 0, ("ut",), ("qu",))
+    ts(bi(14, 10), T.pI[:, 8:18], 127, OP.bitwise_and, ("pJ",), ("pK",))
+    ts(bi(24), part, 7, OP.bitwise_and, ("pI",), ("p8",))
+    cp(T.ul[:, 0:10], bi(14, 10), ("pK",), ("ul0",))
+    ts(T.ul[:, 10:11], bi(24), float(GRP), OP.mult, ("p8",), ("ul1",))
+    node({"V": picked("V", 176)}, lambda e: g.vector.tensor_copy(T.qu2[:, :].bitcast(dt.uint32), T.qu[:, 0:128].bitcast(dt.uint32).indirect(T.ul[:, 0:11])), ("qu", "ul0", "ul1"), ("qu2",))
+    node({"S": picked("S", 176)}, lambda e: g.scalar.activation(T.su2[:, :], T.su[:, 0:128].indirect(T.ul[:, 0:11]), FN.Copy), ("qu", "ul0", "ul1"), ("su2",))
     for b in range(4):
         quant(T.qe, T.se, 128 * b, 128 * b + 128, T.e1, 3 - b, ("e1",), (("qe", b),))
-    unpack(0, NC, ("qxO", "qxG"), LO)
-    op("V", lambda: g.vector.tensor_copy(T.qu2[:, 0:128].bitcast(dt.uint32), T.qu[:, 0:128].bitcast(dt.uint32).indirect(T.ul[:, 0:8])), ("qu", "ul"), ("qu2",))
-    op("S", lambda: g.scalar.activation(T.su2[:, 0:128], T.su[:, 0:128].indirect(T.ul[:, 0:8]), FN.Copy), ("qu", "ul"), ("su2",))
-    bf = lambda k: T.bf[:, k:k + 1]
-    line("a0", bf(1), ("bf",), -3.0 * DBL, float(OWN))
-    line("n", bf(0), ("bf",), -16.0, float(MO + CEN))
-    line("adj", bf(0), ("bf", "a0"), float(DBL), sc("a0"))
-    ts(bi(20, 4), T.pI[:, 20:24], 5, OP.arith_shift_right, ("pQ",), ("rq",), 3, OP.bitwise_and)
-    fill(T.ft[:, 4 * NP:512], 0.0, ("ftz",))
-    ts(T.rel[:, 4:8], bi(20, 4), -float(DBL), OP.mult, ("rq",), ("rl",), -float(DBL), OP.add)
-    fill(T.ft[:, 3:4 * NP:4], 0.0, ("ft3",))
-    tt(T.rel[:, 0:4], T.rel[:, 4:8], T.t4[:, :], OP.add, ("rl", "t4"), ("rel",))
-    window(0, NC, LO, "SSSS", ("wO", "wG"))
-    tt(T.mp[0:112, slot(12)], T.mp[0:112, slot(12)], T.mp[0:112, slot(14)], OP.min, (), ("mid",))
-    inv = T.mp[:, slot(0, 20)]
-    for e, c, a, b in (("V", 0, 6, 26), ("S", NC, 0, 24), ("V", NC + 16 * 24, 24, 26)):
-        move(e, T.mp[:, OWN + c:OWN + c + 16 * (b - a)], inv.indirect(T.x3[:, a:b]), ("inv", "mid", "odd", "x3"), (("ct", a),))
-    cts = (("ct", 6), ("ct", 0), ("ct", 24))
-    dmas("dC", [("YS"[e // 4], T.mp[rows(h), c:c + DBL], T.mp[rows(e), OWN:OWN + DBL])
-                for e in (0, 2, 4, 6) for h, c in ((e + 1, OWN + DBL), ((e - 1) % 8, OWN + 2 * DBL if e else DBL))], cts, ("near",))
-    spread(0, NC, 0, 16, ("wO", "wG"), "sh")
-    quant(T.qc, T.sct, 0, 128, T.ct, 0, ("ct",), ("qc",))
-    for r in range(4):
-        act(T.mt[:, r:80:4], T.pl[:, 20 * r:20 * r + 20], ("pl", "adj"), (("mt", r),), bias=sc("adj"))
-    act(T.nt[:, 0:80:4], T.j20[:, :], ("j20", "n"), ("nt",), bias=sc("n"))
-    line("p16", bf(11), ("bf",), -0.125, -0.5)
-    line("k4", bf(3), ("bf",), 1.0 / 128, -0.5)
-    line("f1", bf(11), ("bf",), -B / 8, 15 * B)
-    line("nf1", bf(11), ("bf",), B / 8, -15 * B)
-    line("p4", bf(11), ("bf", "k4"), -1.0 / 32, sc("k4"))
+    unpack(T.qx, T.sx, 0, NC, ("qxO", "qxG"), (0, 1, 2, 6))
+    line("uv", bf(PAIR), ("bf",), 640.0, -float(UI), "S")
+    for k in range(3):
+        affine(ids(UI + NC * k, NC), ids(0, NC), ("id0",), (("id1", k),), 1.0, float(UI + NC * k), "S")
+    idt = ("id0", ("id1", 0), ("id1", 1), ("id1", 2), "uil", "uv", "id2")
+    affine(T.src[:, DBL + NC:2 * DBL], ids(0, UI + 3 * NC).indirect(T.ui[:, 0:26]), idt, ("st1",), 1.0, sc("uv"), "S", True)
+    affine(T.src[:, DBL:DBL + NC], ids(0, UI + 3 * NC).indirect(T.ui[:, 6:26]), idt, ("st0",), 1.0, sc("uv"), "S", True)
+    dmas("dS", [(T.src[rows(a, n), c:c + DBL], T.src[rows(b, n), DBL:2 * DBL]) for a, n, b, c in ((2, 6, 0, 0), (0, 2, 6, 0), (0, 6, 2, 2 * DBL), (6, 2, 0, 2 * DBL))],
+         ("st0", "st1"), ("src",), 4)
 
-    def pattern(pat, j, sg, nm, beside):
-        act(sg[:, :], j[:, :], ("j" + nm, "p" + nm), ("g" + nm,), bias=sc("p" + nm), fn=FN.Sign)
-        line(*beside)
-        act(pat[:, :], sg[:, :], ("g" + nm,), ("P" + nm,), scale=8.5 * B, bias=-7.5 * B)
-    pattern(T.p16, T.j16, T.g16, "16", ("fa", sc("p4"), ("p4",), -4 * B, 4.0 * CEN - 14 * B))
-    act(T.th[:, :], T.t4[:, :], ("t4", "f1"), ("th",), bias=sc("f1"))
+    def entry_constants():
+        ts(bi(P16), part, 15, OP.bitwise_and, ("pI",), ("p16",))
+        ts(bi(Q4), part, 2, OP.arith_shift_right, ("pI",), ("q4",), 3, OP.bitwise_and)
+        cp(T.bf[:, 6:8], bi(6, 2), ("p16", "q4"), ("bg",))
+        line("n", bf(P16), ("bg",), 2.0, 2.0 * (MO + CEN))
+        line("aa", bf(PAR), ("bf",), 2.0 * DBL, 2.0 * OWN - NC)
+        affine(T.xc[:, 2:60:3], T.src[:, IDB:IDB + NC:GRP], ("id0", "n"), ("nt",), 2.0, sc("n"))
+        affine(T.ca[:, 0:20], T.pl[:, 0:20], ("pl", "aa"), (("ca", 0),), 2.0, sc("aa"))
+        affine(T.ca[:, 20:40], T.pl[:, 20:40], ("pl",), (("ca", 1),), 2.0, 2.0 * (OWN + 2 * DBL) - NC)
+        iota(T.lo[:, :], [[0, 60]], 0, 0, ("lo",))
+        iota(T.lo[:, 0:60:3], [[0, 20]], int(4 * BIG), 0, ("lo",))
 
-    def score(t):
-        a, toks = ((192, ("qxO",)), (0, ("qxG",)), (64, ("qxO", "qxG")))[t]
-        mm(ps[SB[t]][:, 0:128], T.qx, T.sx, a, T.qu2, T.su2, 0, 128, toks + ("qu2", "su2"), (("ps", SB[t]),))
+    def pattern(j, sg, pat, n, col):
+        iota(j[:, :], [[0, HALF // n], [2, n]], -1, 0, (("j", n),))
+        node({"S": span(HALF)}, lambda e: g.scalar.activation(sg[:, :], j[:, :], FN.Sign, bias=bf(col), scale=-0.5), (("j", n), "bg"), (("g", n),))
+        affine(pat[:, :], sg[:, :], (("g", n),), ("P%d" % n,), -8.5 * B, -7.5 * B)
 
-    def compare(t):
-        ts(T.ft[:, t:4 * NP:4], ps[SB[t]][:, 0:NP], 0.0, OP.is_gt, (("ps", SB[t]),), ("ft%d" % t,))
+    def turn_constants():
+        iota(T.ft[:, :], [[0, 512]], 0, 0, ("ft0", "ft1", "ft2"))
+        quant(T.qc, T.sct, 0, 128, T.ew, 0, ("ew",), ("qc",))
+        iota(T.pI[:, 20:24], [[32, 4]], 128 + 63, -1, ("pQ",), True)
+        iota(T.t4[:, :], [[DBL, 4]], DBL, 0, ("t4",))
+        ts(bi(26, 4), T.pI[:, 20:24], 5, OP.arith_shift_right, ("pQ",), ("rq",), 3, OP.bitwise_and)
+        ts(T.rel[:, 4:8], bi(26, 4), -float(DBL), OP.mult, ("rq",), ("rl",), -float(DBL), OP.add)
+        tt(T.rel[:, 0:4], T.rel[:, 4:8], T.t4[:, :], OP.add, ("rl", "t4"), ("rel",))
+        line("f1", bf(P16), ("bg",), -B, 15 * B)
+        line("nf1", bf(P16), ("bg",), B, -15 * B)
+        affine(T.th[:, :], T.t4[:, :], ("t4", "f1"), ("th",), 1.0, sc("f1"))
 
-    def counts():
-        quant(T.qf, T.sf, 0, 128, T.ft, 0, ("ft0", "ft1", "ft2", "ft3", "ftz"), ("qf",))
-        mm(ps[7][:, 0:128], T.qc, T.sct, 0, T.qf, T.sf, 0, 128, ("qc", "qf"), (("ps", 7),))
+    def offset_constants():
+        for k in (1, 2):
+            iota(ids(2 * NC * k, NC), [[1, NC]], 2 * NC * k, 0, ("id2",))
+        pattern(T.j4, T.g4, T.p4, 4, Q4)
+        line("fb", bf(GR), ("bf",), -1280.0, 4.0 * CEN - 12 * B)
+        line("fc", bf(P16), ("bg", "fb"), 1.0, sc("fb"))
+        line("fin", bf(Q4), ("bg", "fc"), 4 * B - 4, sc("fc"))
 
-    for t in range(3):
-        score(t)
-    for t in range(3):
-        compare(t)
-    counts()
+    def score(t, bank):
+        a, toks = ((192, ("qxO", "layer")), (0, ("qxG",)), (64, ("qxO", "qxG")))[t]
+        mm(bank, T.qx, T.sx, a, T.qu2, T.su2, 48, 128, toks + ("qu2", "su2"))
+        p = slice(64 if t == 2 else 0, 128)
+        ts(T.ft[p, t:32:4], ps[bank][p, 112:120], 0.0, OP.is_gt, (("ps", bank),), ("ft%d" % t,), 2.0 ** -5, OP.mult)
 
-    def lists(rd):
-        cn = lambda k: T.cnt[:, k:k + 1]
-        tt(T.xc[:, :], T.mt[:, :], ps[7][:, 0:80], OP.subtract, four("mt") + (("ps", 7),), ("xc",))
-        tt(T.cnt[:, :], ps[7][:, 81:NP:2], T.rel[:, 0:4], OP.add, (("ps", 7), "rel"), ("cnt",))
-        scan(T.xs[:, :], T.nt[:, :], T.xc[:, :], ("nt", "xc"), ("xs",), OP.max, OP.min)
-        tt(T.df[:, 0:3], T.cnt[:, 0:3], T.cnt[:, 1:4], OP.subtract, ("cnt",), ("dfc",))
-        cp(T.o1[:, :], T.xs[:, 3:80:4], ("xs",), ("o1",))
-        act(T.acs[:, rd:24:3], ps[7][:, 80:NP], (("ps", 7), "cnt"), (("ac", rd),))
-        line("zb", cn(0), ("cnt", "nf1"), -1.0, sc("nf1"))
-        tab = T.mp[:, 0:MO + 8 * NC]
-        for h in range(2):
-            move("VS"[h], T.r1[:, HALF * h:HALF * h + HALF], tab.indirect(T.o1[:, 10 * h:10 * h + 10]), ("o1", "near", "inv") + cts, (("r1", h),))
-        if rd == 0:
-            pattern(T.p4, T.j4, T.g4, "4", ("fb", bf(0), ("bf", "fa"), -1280.0, sc("fa")))
-            line("fin", bf(3), ("bf", "fb"), 1.0 / 32, sc("fb"))
-        for h in range(2):
-            scan(T.f1[:, HALF * h:HALF * h + HALF], T.p16[:, :], T.r1[:, HALF * h:HALF * h + HALF], ("P16", ("r1", h)), (("f1", h),), OP.add, OP.max)
-        x, xt = T.f1[:, 15:NC:16], (("f1", 0), ("f1", 1))
-        act(T.z5[:, 0:100:5], x, xt + ("zb",), (("z", 0),), bias=sc("zb"))
+    def sums(bank):
+        quant(T.qf, T.sf, 0, 128, T.ft, 0, ("ft0", "ft1", "ft2"), ("qf",))
+        mm(bank, T.qc, T.sct, 0, T.qf, T.sf, 0, 128, ("qc", "qf"))
+
+    def steps(bank):
+        tt(T.cn[:, 0:4], ps[bank][:, 1:8:2], T.rel[:, 0:4], OP.add, (("ps", bank), "rel"), ("cnt",), 1)
+        tt(T.df[:, 0:3], T.cn[:, 0:3], T.cn[:, 1:4], OP.subtract, ("cnt",), ("df",))
+        affine(T.df[:, 3:4], T.cn[:, 0:1], ("cnt", "nf1"), ("zb",), -1.0, sc("nf1"))
+
+    def even_count(k, lo, hi, toks, bank, out, tok):
+        n = hi - lo
+        mm(bank, T.qu2, T.su2, 32 * k, T.qx, T.sx, lo, n, toks + ("qu2", "su2"))
+        node({"S": span(n) + 0.02}, lambda e: g.scalar.activation(T.sg[:, NC * k:NC * k + n], ps[bank][:, 0:n], FN.Sign, bias=TINY, scale=-1.0, accum_out=out),
+             (("ps", bank),), (tok, ("sg", k)))
+
+    def entries(k, more):
+        ts(T.xc[:, k:60:3], T.ca[:, 20 * k:20 * k + 20], T.cn[:, 4 + k:5 + k], OP.add, (("no", k), ("n", k), ("ca", k)), (("xc", k),), more, OP.add)
+
+    def least():
+        scan(T.xs[:, :], T.lo[:, :], T.xc[:, :], ("lo", "nt", ("xc", 0), ("xc", 1)), ("xs",), OP.add, OP.min)
+        ts(T.o1[:, :], T.xs[:, 2:60:3], 0.5, OP.mult, ("xs",), ("o1",))
+
+    def lookup(cuts, out, table, off, r, tok):
+        for e, a, b in cuts:
+            affine(out[:, GRP * a:GRP * b], table.indirect(off[:, a:b]), r, [(tok, c) for c in range(a, b, 2)], who=e, pick=True)
+
+    def fold(h, out, pat, got, r, tok):
+        c = slice(HALF * h, HALF * h + HALF)
+        scan(out[:, c], pat[:, :], got[:, c], [r] + [("r" + tok, c) for c in range(10 * h, 10 * h + 10, 2)], (("f" + tok, h),), OP.add, OP.max)
+
+    def shared(h):
+        return (("V", 10 * h, 10 * h + 6), ("S", 10 * h + 6, 10 * h + 10))
+
+    def first(h):
+        lookup(shared(h), T.r1, T.mp[:, 0:MO + 8 * NC], T.o1, ("o1", "near", "inv") + cts, "r1")
+
+    def turn(h):
+        x, xt, c = T.f1[:, HALF * h + 15:HALF * h + HALF:16], (("f1", h),), 50 * h
+        affine(T.z5[:, c:c + 50:5], x, xt + ("zb",), (("z", 0, h),), 1.0, T.df[:, 3:4])
         for q in range(4):
-            ts(T.z5[:, q + 1:100:5], x, T.th[:, q:q + 1], OP.is_ge, xt + ("th", "dfc", "cnt"), (("z", q + 1),), T.df[:, q:q + 1] if q < 3 else cn(3), OP.mult)
-        scan(T.zs[:, :], T.keep[:, 0:100], T.z5[:, :], ("keep",) + tuple(("z", q) for q in range(5)), ("zs",))
-        cp(T.o2[:, :], T.zs[:, 4:100:5], ("zs",), ("o2",))
-        for h in range(2):
-            move("VS"[h], T.r2[:, HALF * h:HALF * h + HALF], T.src[:, :].indirect(T.o2[:, 10 * h:10 * h + 10]), ("o2", "src", "st0", "st1", ("id2", 1), ("id2", 2)) + idt, (("r2", h),))
+            ts(T.z5[:, c + q + 1:c + 50:5], x, T.th[:, q:q + 1], OP.is_ge, xt + ("th", "cnt", "df"), (("z", q + 1, h),), T.df[:, q:q + 1] if q < 3 else T.cn[:, 3:4], OP.mult)
+        scan(T.zs[:, c:c + 50], T.keep[:, 0:50], T.z5[:, c:c + 50], ["keep"] + [("z", q, h) for q in range(5)], (("zs", h),))
+        cp(T.o2[:, 10 * h:10 * h + 10], T.zs[:, c + 4:c + 50:5], (("zs", h),), (("o2", h),))
 
-    def fold(h):
-        scan(T.f2[:, HALF * h:HALF * h + HALF], T.p4[:, :], T.r2[:, HALF * h:HALF * h + HALF], ("P4", ("r2", h)), (("f2", h),), OP.add, OP.max)
-
-    def offsets(h):
+    def second(h):
+        lookup(shared(h), T.r2, T.src[:, :], T.o2, (("o2", h), "src", "st0", "st1") + idt, "r2")
+        fold(h, T.f2, T.p4, T.r2, "P4", "2")
         ts(T.l4[:, 40 * h:40 * h + 40], T.f2[:, HALF * h + 3:HALF * h + HALF:4], 4.0, OP.mult, (("f2", h), "fin"), (("l4", h),), sc("fin"), OP.add)
 
-    def gather(h, tile, tok):
-        for k in range(2):
-            c = 40 * h + 20 * k
-            move("VS"[k], tile[:, NC * k:NC * k + NC], T.win[:, :].indirect(T.l4[:, c:c + 20]), ("wO", "wG", "sh", "shO", "shG", ("l4", h)), ((tok, k),))
+    def gather(h, tile, tok, cut):
+        for k, (a, b) in enumerate(((0, cut), (cut, 40))):
+            affine(tile[:, GRP * a:GRP * b], T.win[:, :].indirect(T.l4[:, 40 * h + a:40 * h + b]), four("wO") + four("wG") + ("sh", "shO", "shG", ("l4", h)),
+                   ((tok, k), (tok, k + 2)), who="VS"[k], pick=True)
 
-    def layer(base, b, q, s, qt, start):
-        tok = ("ps", base + b)
-        if not start:
-            writer[tok] = [x for x in writer[tok] if x[0] != "cT"]
-        mm(ps[base + b][:, 0:HALF], T.wq, T.wsb, 128 * b, q, s, 0, HALF, ("wq",) + qt, (tok,), start, True)
+    def packed(lo, tok):
+        dmas("dOut", [(T.oc[:, 4 * lo:4 * (lo + HALF)], T.qx[:, lo:lo + HALF].bitcast(dt.uint8))]
+             + [(T.osc[4 * k:4 * k + 4, lo:lo + HALF], T.sx[32 * k:32 * k + 4, lo:lo + HALF]) for k in range(4)], (tok,), (), 1)
 
-    def packed(lo, tok, e):
-        dmas("dOut", [(e, T.oc[:, 4 * lo:4 * (lo + HALF)], T.qx[:, lo:lo + HALF].bitcast(dt.uint8))]
-             + [(e, T.osc[4 * k:4 * k + 4, lo:lo + HALF], T.sx[32 * k:32 * k + 4, lo:lo + HALF]) for k in range(4)], (tok,), ())
-
-    def result(lo, bank, e):
-        move(e, T.yt[:, lo:lo + HALF], ps[bank][:, 0:HALF], (("ps", bank),), (("y", lo),))
-        dma("S", "dOut", T.y[:, lo:lo + HALF], T.yt[:, lo:lo + HALF], (("y", lo),), ())
+    def result(lo, tok, bank):
+        mm(bank, T.qv, T.sv, 0, T.qx, T.sx, lo, HALF, ("qv", tok))
+        affine(T.yt[:, lo:lo + HALF], ps[bank][:, 0:HALF], (("ps", bank),), (("y", lo),))
+        dmas("dOut", [(T.y[:, lo:lo + HALF], T.yt[:, lo:lo + HALF])], (("y", lo),), (), 4)
 
     for rd in range(3):
-        last = rd == 2
-        lists(rd)
-        fold(0)
-        fold(1)
-        offsets(0)
-        offsets(1)
-        gather(0, T.gt, "gt")
-        quant(T.q2, T.s2, 0, HALF, T.gt, 0, two("gt"), ("q2",))
-        dst = T.cores[rank ^ MASKS[rd]]
-        rid, pid = topo.addr(dst)[0], topo.addr(dst)[1]
-        ne, mask = len(topo.engines(core, dst)), topo.mask(core, dst)
-        arr = "arr%d" % rd
-        lc, ls = T["lc%d" % rd], T["ls%d" % rd]
-        gate("G", ("q2",), ())
-        g.remote_dma(lc[:, :].bitcast(dt.uint8), T.q2[:, :].bitcast(dt.uint8), T.sem[arr], T.sem.sent, pid, rid, mask)
-        g.remote_dma(ls[:, :], T.s2[:, :], T.sem[arr], T.sem.sent, pid, rid, mask)
-        total["sent"] += 2 * ne
-        total[arr] += 2 * ne
-        mark("G", "sent", total["sent"], ("q2",), ())
-        land = ("land", rd)
-        writer[land] = [(arr, 2 * ne, {})]
-        gather(1, T.zo, "zo")
-        quant(T.qz, T.sz, 0, HALF, T.zo, 0, two("zo"), ("qz",))
-        for b in range(4):
-            act(T.z32[:, HALF * b:HALF * b + HALF], T.zo[:, b:4 * HALF:4], two("zo"), (("z32", b),), scale=32.0)
         if rd == 0:
-            quant(T.qv, T.sv, 0, 128, T.vt, 0, ("vt",), ("qv",))
-        for b in range(4):
-            layer(0, b, T.qz, T.sz, ("qz",), True)
-        gate("S", (), ("xO",))
-        for b in range(4):
-            part = T.sm[:, HALF * b:HALF * b + HALF]
-            tt(part, ps[b][:, 0:HALF], T.z32[:, HALF * b:HALF * b + HALF], OP.add, (("ps", b), ("z32", b)), (("sm", b),))
-            act(T.xt[:, 4 * HALF + b:4 * NC:4], part, (("sm", b),), (("xo", b),), scale=2.0 ** -5)
-        join("xO", four("xo"))
-        quant(T.qx, T.sx, HALF, NC, T.xt, 4 * HALF, ("xO",), ("qxO",))
-        for b in range(4):
-            mm(ps[4 + b][:, 0:HALF], T.qe, T.se, 128 * b, lc, ls, 0, HALF, (("qe", b), land), (("ps", 4 + b),), True, False)
-            layer(4, b, lc, ls, (land,), False)
-        if last:
-            dma("Y", "dOut", T.ac[:, :], T.acs[0:1, 0:24], (("ac", 0), ("ac", 1), ("ac", 2)), ())
-            packed(HALF, "qxO", "Y")
-            mm(ps[0][:, 0:HALF], T.qv, T.sv, 0, T.qx, T.sx, HALF, HALF, ("qv", "qxO"), (("ps", 0),))
+            for k in range(2):
+                even_count(k, 0, NC, ("qxO", "qxG"), 3 + k, T.cn[:, 4 + k:5 + k], ("n", k))
+            out_of((0, 1, 2, 6), NC, T.win, 4 * CEN, ("wO", "wG"))
+            spread(0, NC, 0, 16, four("wO") + four("wG"), "sh")
+            entry_constants()
+            pattern(T.j16, T.g16, T.p16, 16, P16)
         else:
-            score(0)
-        for e in "VS":
-            gate(e, (), ("xG",))
+            quant(T.qx, T.sx, 0, HALF, T.xt, 0, four("xG"), ("qxG",))
+            unpack(T.qx, T.sx, HALF, NC, ("qxO", "layer"), (0, 1, 2, 3))
+            for k in range(2):
+                even_count(k, HALF, NC, ("qxO", "layer"), 4 + k, T.no[:, k:k + 1], ("no", k))
+            out_of((0, 1, 2, 3), HALF, T.win, 4 * (CEN + HALF), ("wO",))
+            for k in range(2):
+                even_count(k, 0, HALF, ("qxG",), (6, 0)[k], T.cn[:, 4 + k:5 + k], ("n", k))
+        for k in range(2):
+            entries(k, T.no[:, k:k + 1] if rd else 0.0)
+        least()
+        if rd:
+            spread(HALF, NC, 0, 8, four("wO"), "shO")
+            for t in range(3):
+                score(t, (7, 4, 5)[t])
+            unpack(T.qx, T.sx, 0, HALF, ("qxG",), (1, 2, 3, 6))
+            sums(7)
+            out_of((1, 2, 3, 6), HALF, T.win, 4 * CEN, ("wG",))
+            spread(0, HALF, 0, 8, four("wG"), "shG")
+            spread(0, NC, 8, 16, four("wO") + four("wG"), "sh")
+        first(0)
+        if rd == 0:
+            turn_constants()
+            for t in range(3):
+                score(t, (5, 7, 3)[t])
+            sums(7)
+        steps(7)
+        fold(0, T.f1, T.p16, T.r1, "P16", "1")
+        turn(0)
+        if rd == 0:
+            offset_constants()
+        second(0)
+        affine(T.acs[:, rd:24:3], ps[7][:, 0:8], (("ps", 7),), (("ac", rd),))
+        lc, ls, land = T["lc%d" % rd], T["ls%d" % rd], "land%d" % rd
+        gather(0, T.gt, "gt", 20)
+        quant(T.q2, T.s2, 0, HALF, T.gt, 0, four("gt"), ("q2",))
+        first(1)
+        fold(1, T.f1, T.p16, T.r1, "P16", "1")
+        turn(1)
+        second(1)
+        send(rd, [(lc[:, :].bitcast(dt.uint8), T.q2[:, :].bitcast(dt.uint8), 4 * HALF), (ls[:, :], T.s2[:, :], HALF)], ("q2",), land)
         for b in range(4):
-            move("VS"[b % 2], T.xt[:, b:4 * HALF:4], ps[4 + b][:, 0:HALF], (("ps", 4 + b),), (("xg", b),), 2.0 ** -5)
-        join("xG", four("xg"))
-        if not last:
-            compare(0)
-            unpack(HALF, NC, ("qxO",), HI)
-        quant(T.qx, T.sx, 0, HALF, T.xt, 0, ("xG",), ("qxG",))
-        if last:
-            result(HALF, 0, "S")
-            mm(ps[1][:, 0:HALF], T.qv, T.sv, 0, T.qx, T.sx, 0, HALF, ("qv", "qxG"), (("ps", 1),))
-            packed(0, "qxG", "Y")
-            result(0, 1, "V")
-        else:
-            gate("Y", (), ("sh",))
-            window(HALF, NC, HI, "VSSS", ("wO",))
-            spread(HALF, NC, 0, 8, ("wO",), "shO")
-            score(1)
-            score(2)
-            unpack(0, HALF, ("qxG",), LO)
-            compare(1)
-            compare(2)
-            counts()
-            window(0, HALF, LO, "SSSV", ("wG",))
-            spread(0, HALF, 0, 8, ("wG",), "shG")
-            spread(0, NC, 8, 16, ("wO", "wG"), "sh")
+            mm(4 + b, T.qe, T.se, 128 * b, lc, ls, 0, HALF, (("qe", b), land), True, False)
+            mm(4 + b, T.wq, T.wsb, 128 * b, lc, ls, 0, HALF, ("wq", land), False, True, ("layer",))
+        out_of((4, 5, 6, 7), HALF, T.xt, 0, ("xG",))
+        gather(1, T.zo, "zo", 14)
+        quant(T.qz, T.sz, 0, HALF, T.zo, 0, four("zo"), ("qz",))
+        for b in range(4):
+            mm(b, T.wq, T.wsb, 128 * b, T.qz, T.sz, 0, HALF, ("wq", "qz"))
+        for b in range(4):
+            affine(T.z32[:, HALF * b:HALF * b + HALF], T.zo[:, b:4 * HALF:4], four("zo"), (("z32", b),), 32.0, who="S")
+            piece = T.sm[:, HALF * b:HALF * b + HALF]
+            tt(piece, ps[b][:, 0:HALF], T.z32[:, HALF * b:HALF * b + HALF], OP.add, (("ps", b), ("z32", b)), (("sm", b),), 1)
+            affine(T.xt[:, 4 * HALF + b:4 * NC:4], piece, (("sm", b),), (("xO", b),), 2.0 ** -5)
+        quant(T.qx, T.sx, HALF, NC, T.xt, 4 * HALF, four("xO"), ("qxO",))
+    quant(T.qx, T.sx, 0, HALF, T.xt, 0, four("xG"), ("qxG",))
+    quant(T.qv, T.sv, 0, 128, T.vt, 0, ("vt",), ("qv",))
+    result(0, "qxG", 1)
+    packed(0, "qxG")
+    result(HALF, "qxO", 0)
+    packed(HALF, "qxO")
+    dmas("dOut", [(T.ac[:, :], T.acs[0:1, 0:24])], (("ac", 0), ("ac", 1), ("ac", 2)), (), 4)
+
+    total = {s: 0 for s in SEMAPHORES}
+    known = {e: {} for e in eng}
+    for i, e in plan(nodes):
+        x = nodes[i]
+        need = []
+        for d in x["deps"] - x["loose"]:
+            need.append(nodes[d]["left"] if "left" in nodes[d] and nodes[d]["sem"][3] not in x["toks"] else nodes[d]["mark"])
+        best = {}
+        for sem, val, clk in need:
+            best[sem] = max(best.get(sem, 0), total[sem] if sem in LOCAL else val)
+        for sem, v in sorted(best.items()):
+            implied = any(s != sem and clk.get(sem, 0) >= v for s, val, clk in need)
+            if known[e].get(sem, 0) < v and (sem in LOCAL or not implied):
+                eng[e].wait_ge(T.sem[sem], v)
+        for sem, val, clk in need:
+            for s, v in clk.items():
+                known[e][s] = max(known[e].get(s, 0), v)
+        for sem, v in best.items():
+            known[e][sem] = max(known[e].get(sem, 0), v)
+        made = x["call"](e)
+        if e == "G" and x["sem"]:
+            arr, sent, n, land = x["sem"]
+            total[arr], total[sent] = n, n
+            x["mark"], x["left"] = (arr, n, {}), (sent, n, dict(known[e]))
+            continue
+        sem = x["sem"] or "c" + e
+        for c in made if x["sem"] else [made]:
+            c.then_inc(T.sem[sem], 16 if x["sem"] else 1)
+            total[sem] += 16 if x["sem"] else 1
+        x["mark"] = (sem, total[sem], dict(known[e]))
     for s in SEMAPHORES:
         if total[s] and known["Y"].get(s, 0) < total[s]:
             g.sync.wait_ge(T.sem[s], total[s])

import numpy as np
from concourse.mybir import dt, AluOpType, ActivationFunctionType

N = 4
MASKS = (1, 2, 3)
NC, HALF, GRP, RING, DBL = 320, 160, 16, 416, 736
CEN = 7 * NC
WINC = 15 * NC
OWN = 0
MO = OWN + 3 * DBL
IDB = 4 * DBL
UI = 6 * NC
BIG = 1.0e6
B = 8192.0
TINY = 2.0 ** -100
OP = AluOpType
FN = ActivationFunctionType
F32, BF16, I32, U16, U8, X4 = "float32", "bfloat16", "int32", "uint16", "uint8", "float8_e4m3fn_x4"

WIDTHS = {
    BF16: {"win": 4 * WINC, "sg": 2 * NC, "xt": 4 * NC, "ew": 516, "e1": 516, "ft": 512, "ut": 512, "vt": 512,
           "gt": 4 * HALF, "zo": 4 * HALF, "z32": 4 * HALF},
    F32: {"mp": MO + 20 * NC, "src": IDB + UI + 3 * NC, "iv": RING, "sc": 32, "bf": 12, "y5": 130, "s5": 130, "keep": 130,
          "j16": HALF, "j4": HALF, "g16": HALF, "tg": 2, "g4": HALF, "p16": HALF, "xc": 60, "xs": 60, "lo": 60, "p4": HALF, "t4": 4, "th": 4, "pl": 40,
          "ca": 40, "rel": 8, "cn": 8, "no": 2, "df": 4, "r1": NC, "f1": NC, "r2": NC, "f2": NC,
          "z5": 100, "zs": 100, "acs": 24, "sm": 4 * HALF, "yt": NC},
    I32: {"ri": 84, "qi": 26, "pI": 24, "bi": 32},
    U16: {"x1": 26, "x3": 26, "ui": 26, "ul": 12, "o1": 20, "o2": 20, "l4": 80},
    X4: {"qe": 512, "qc": 128, "qf": 128, "qu": 128, "qu2": 176, "qv": 128, "wq": 512, "qx": NC, "q2": HALF, "qz": HALF, "lc0": HALF, "lc1": HALF, "lc2": HALF},
    U8: {"se": 512, "sct": 128, "sf": 128, "su": 128, "su2": 176, "sv": 128, "wsb": 512, "sx": NC, "s2": HALF, "sz": HALF, "ls0": HALF, "ls1": HALF, "ls2": HALF},
}
SCRATCH = {name: ("sbuf", [128, n], t) for t, d in WIDTHS.items() for name, n in d.items()}
for _b in range(8):
    SCRATCH["ps%d" % _b] = ("psum", [128, 512], "float32")
LOCAL = ("dM", "dN", "d2", "d3", "dX", "dU", "dV", "dW", "sh", "shO", "shG", "dS", "dF", "dC", "dOut")
SEMAPHORES = ["cV", "cS", "cT", "cG", "arr0", "arr1", "arr2", "sent0", "sent1", "sent2"] + list(LOCAL)

CYCLE, CALL, WAKE, PE = 0.92e-3, 0.0, 0.21, 0.7e-3
ISSUE, START, ROW, BYTE = 0.05, 0.8, 0.015, 1 / 45.0e3
RISSUE, RFIRST, RSTART, RBYTE = 0.1, 0.65, 0.8, 1 / 45.0e3
SLACK = 0.03


def shifts():
    out = []
    for d in (1, -1, 2, -2):
        k = GRP * (d % 8)
        out += [(0, 128 - k, k, 7 + d % 8), (128 - k, 128, 0, d % 8 - 1)]
    for h in (1, 3, 5, 7):
        out += [(GRP * h, GRP * h + GRP, GRP * ((h + d) % 8), (h + d) % 8 - h + 7) for d in (3, -3)]
    return out


def fit(busy, t, d):
    for a, b in busy:
        if t + d <= a + SLACK:
            break
        t = max(t, b)
    return t


def plan(nodes):
    busy = {e: [] for e in "VSTGYW"}
    for x in nodes:
        t = max([nodes[d]["done"] + (0.0 if d in x["loose"] else WAKE) for d in x["deps"]] + [0.0])
        if x["wire"]:
            e = list(x["cost"])[0]
            if e == "G":
                t = fit(busy[e], t, x["cost"][e])
                busy[e] = sorted(busy[e] + [(t, t + x["cost"][e])])
            lead = x["lead"] + x["late"] / 2
            w = fit(busy["W"], t + lead, x["wire"])
            busy["W"] = sorted(busy["W"] + [(w, w + x["wire"])])
            x["start"], x["done"] = t if e == "G" else w - lead, w + max(x["wire"], x["cost"][e] - x["lead"]) + x["late"] / 2
        else:
            x["done"], e = min((fit(busy[e], t, d) + d, e) for e, d in x["cost"].items())
            x["start"] = x["done"] - x["cost"][e]
            busy[e] = sorted(busy[e] + [(x["start"], x["done"])])
        x["on"] = e
    return [(i, nodes[i]["on"]) for i in sorted(range(len(nodes)), key=lambda i: (nodes[i]["start"], i))]


def rank_program(g, core, T, topo):
    rank = T.rank_of(core)
    if rank is None:
        return
    eng = {"V": g.vector, "S": g.scalar, "T": g.tensor, "G": g, "Y": g.sync}
    nodes, writer, reader = [], {}, {}

    def node(cost, call, r, w, late=0.0, wire=0.0, sem=None, lead=0.0):
        r, w = tuple(r), tuple(w)
        w += tuple(t for t in r if t[0] == "ps")
        deps = set()
        for t in r + w:
            deps.update(writer.get(t, ()))
        for t in w:
            deps.update(reader.get(t, ()))
        i = len(nodes)
        loose = set(d for d in deps if "T" in cost and "T" in nodes[d]["cost"])
        nodes.append({"cost": cost, "call": call, "deps": deps, "loose": loose, "late": late, "wire": wire, "sem": sem, "toks": r + w, "lead": lead})
        for t in r:
            reader.setdefault(t, []).append(i)
        for t in w:
            writer[t], reader[t] = [i], []

    def width(ap):
        return int(ap.shape[1])

    def span(n):
        return CALL + CYCLE * max(n, 64)

    def picked(e, n):
        return CALL + {"V": 0.06, "S": 0.08}[e] + 1.5 * CYCLE * n

    def dmas(sem, copies, r, w, size):
        wire = sum((int(o.shape[0]) + 15) // 16 * (ROW + BYTE * size * width(o)) for o, i in copies)
        node({"Y": ISSUE * len(copies)}, lambda e: [g.sync.dma_start(o, i) for o, i in copies], r, w, START, wire, sem)

    def send(rd, pairs, r, land):
        dst = T.cores[rank ^ MASKS[rd]]
        rid, pid = topo.addr(dst)[0], topo.addr(dst)[1]
        ne, arr, sent, lead = len(topo.engines(core, dst)), "arr%d" % rd, "sent%d" % rd, 0.0 if rd else RFIRST
        call = lambda e: [g.remote_dma(o, i, T.sem[arr], T.sem[sent], pid, rid, topo.mask(core, dst)) for o, i, n in pairs]
        node({"G": RISSUE * len(pairs) + lead}, call, r, (land,), RSTART, sum(128 // ne * (ROW + RBYTE * n) for o, i, n in pairs), (arr, sent, ne * len(pairs), land), lead)

    def ts(out, in0, s1, o1, r, w, s2=None, o2=None):
        if o2 is None:
            node({"V": span(width(out))}, lambda e: g.vector.tensor_scalar(out, in0, s1, None, o1), r, w)
        else:
            node({"V": span(width(out))}, lambda e: g.vector.tensor_scalar(out, in0, s1, s2, o1, o2), r, w)

    def tt(out, in0, in1, o, r, w, both=2):
        node({"V": span(both * width(out))}, lambda e: g.vector.tensor_tensor(out, in0, in1, o), r, w)

    def cp(out, in_, r, w):
        node({"V": span(width(out))}, lambda e: g.vector.tensor_copy(out, in_), r, w)

    def affine(out, in_, r, w, scale=1.0, bias=0.0, who="VS", pick=False):
        def call(e):
            plain = isinstance(bias, float) and bias == 0.0
            if e == "S":
                return g.scalar.activation(out, in_, FN.Copy, scale=scale) if plain else g.scalar.activation(out, in_, FN.Identity, bias=bias, scale=scale)
            if isinstance(scale, float) and scale == 1.0:
                return g.vector.tensor_copy(out, in_) if plain else g.vector.tensor_scalar(out, in_, bias, None, OP.add)
            return g.vector.tensor_scalar(out, in_, scale, None, OP.mult) if plain else g.vector.tensor_scalar(out, in_, scale, bias, OP.mult, OP.add)
        node({e: picked(e, width(out)) if pick else span(width(out)) for e in who}, call, r, w)

    def fill(ap, c, w, e, half=False):
        n = width(ap)
        if e == "V":
            node({e: span(n // 2 if half else n)}, lambda e: g.vector.memset(ap, c), (), w)
        else:
            affine(ap, T.ew[:, 0:n], ("ew",), w, 0.0, c, e)

    def iota(out, pattern, base, step, w, whole=False):
        call = lambda e: g.iota(out, pattern, base, step) if whole else g.iota(out, pattern, base, step, allow_small_or_imprecise_dtypes=True)
        node({"G": 0.16 + 2 * CYCLE * width(out)}, call, (), w)

    def scan(out, k, d, r, w, o0=OP.mult, o1=OP.add):
        node({"V": span(width(out))}, lambda e: g.vector.tensor_tensor_scan(out, k, d, 0.0, o0, o1), r, w)

    def quant(q, s, a, b, tile, c0, r, w):
        node({"V": CALL + 0.014 + 1.06 * CYCLE * (b - a)}, lambda e: g.vector.quantize_mx(q[:, a:b], s[:, a:b], tile[:, c0:c0 + 4 * (b - a)]), r, w)

    def mm(bank, l, ls, la, m, ms, ma, n, r, start=True, stop=True, w=()):
        node({"T": PE * (n + 16)}, lambda e: g.tensor.matmul_mx(ps[bank][:, 0:n], l[:, la:la + 128], ls[:, la:la + 128], m[:, ma:ma + n], ms[:, ma:ma + n], start, stop),
             r, (("ps", bank),) + w)

    ps = [T["ps%d" % b] for b in range(8)]
    rows = lambda h, n=1: slice(GRP * h, GRP * (h + n))
    slot = lambda k, n=1: slice(MO + NC * k, MO + NC * (k + n))
    four = lambda t: tuple((t, b) for b in range(4))
    names = {}

    def sc(name):
        k = names.setdefault(name, len(names))
        return T.sc[:, k:k + 1]

    def scalar(name, in0, r, s1, o1, s2=None, o2=None):
        ts(sc(name), in0, s1, o1, r, (name,), s2, o2)

    def line(name, in0, r, scale, bias, who="VS"):
        affine(sc(name), in0, r, (name,), scale, bias, who)

    def unpack(q, s, lo, hi, toks, banks):
        for b, k in enumerate(banks):
            mm(k, T.qe, T.se, 128 * b, q, s, lo, hi - lo, (("qe", b),) + toks)

    def out_of(banks, n, tile, c0, toks):
        for b, k in enumerate(banks):
            affine(tile[:, c0 + b:c0 + 4 * n:4], ps[k][:, 0:n], (("ps", k),), [(t, b) for t in toks], 2.0 ** -5)

    def spread(lo, hi, a, b, r, sem):
        dmas(sem, [(T.win[p0:p1, 4 * (NC * k + lo):4 * (NC * k + hi)], T.win[q0:q0 + p1 - p0, 4 * (CEN + lo):4 * (CEN + hi)])
                   for p0, p1, q0, k in shifts()[a:b]], r, (sem,), 2)

    L3, L2 = T.ri[:, 0:26], T.ri[:, 28:54]
    dmas("d3", [(L3, T.ring[:, :])], (), ("L3",), 4)
    dmas("dX", [(T.xt[:, :], T.x[:, :])], (), four("xO") + four("xG"), 2)
    dmas("dU", [(T.ut[:, :], T.u[:, :])], (), ("ut",), 2)
    dmas("d2", [(T.ri[rows(h), 28:54], T.ring[rows(h | 1), :]) for h in range(8)], (), ("L2",), 4)
    dmas("dW", [(T.wq[:, :].bitcast(dt.uint8), T.wc[:, :]), (T.wsb[:, :], T.ws[:, :])], (), ("wq",), 1)
    dmas("dV", [(T.vt[:, :], T.v[:, :])], (), ("vt",), 2)

    ids = lambda a, n: T.src[:, IDB + a:IDB + a + n]
    bi = lambda k, n=1: T.bi[:, k:k + n]
    bf = lambda k: T.bf[:, k:k + 1]
    GR, PAIR, PAR, EVEN, P16, Q4 = 0, 2, 4, 5, 6, 7
    part = T.pI[:, 0:1]
    iota(T.pI[:, 0:2], [[GRP, 2]], 0, 1, ("pI",), True)
    iota(ids(0, RING), [[1, RING]], 0, 0, ("id0",))
    fill(T.ew[:, :], 32.0, ("ew",), "V", True)
    ts(bi(GR, 2), T.pI[:, 0:2], 4, OP.arith_shift_right, ("pI",), ("g",))
    ts(bi(PAR, 2), T.pI[:, 0:2], 4, OP.arith_shift_right, ("pI",), ("par",), 1, OP.bitwise_and)
    ts(bi(PAIR, 2), T.pI[:, 0:2], 5, OP.arith_shift_right, ("pI",), ("pair",))
    fill(T.mp[:, slot(8)], BIG, ("big0",), "S")
    fill(T.mp[:, slot(0)], BIG, ("big1",), "S")
    scalar("w", bi(EVEN), ("par",), 300.0, OP.mult)
    cp(T.bf[:, 0:6], bi(0, 6), ("g", "pair", "par"), ("bf",))
    scalar("al", bi(EVEN), ("par",), 19.0, OP.mult, 1.0, OP.add)
    scalar("c0", bi(GR), ("g", "w"), -1.0, OP.add, sc("w"), OP.mult)
    ts(T.tg[:, :], bi(GR, 2), 320.0, OP.mult, ("g",), ("tg",))
    scalar("be", bi(EVEN), ("par",), -319.0, OP.mult)
    scalar("w3", bi(GR), ("g",), 0.0, OP.is_equal, -2680.0, OP.mult)
    line("a6", bf(GR), ("bf",), 320.0, IDB - NC - BIG, "S")
    line("vv", bf(PAIR), ("bf",), float(DBL), 0.0, "S")
    line("c1", bf(GR), ("bf",), -320.0, float(CEN), "S")
    line("d6", sc("a6"), ("a6", "bf"), bf(PAR), BIG, "S")
    line("v", sc("vv"), ("vv", "bf"), bf(PAR), 320.0, "S")
    affine(T.mp[:, slot(6)], ids(0, NC), ("id0", "d6", "bf"), ("big2",), bf(PAR), sc("d6"), "S")
    affine(T.iv[:, :], ids(0, RING), ("id0", "v"), ("iv",), 1.0, sc("v"), "S")

    y = lambda k: T.y5[:, k:130:5]
    ts(T.qi[:, :], L3, 4, OP.arith_shift_right, ("L3",), ("qi",))
    ts(y(0), L3, sc("al"), OP.mult, ("L3", "al", "c0"), ("y0",), sc("c0"), OP.add)
    fill(T.keep[:, :], 1.0, ("keep",), "V")
    for k in range(2):
        ts(y(1 + k), L3, T.tg[:, k:k + 1], OP.is_ge, ("L3", "tg", "w"), ("y%d" % (1 + k),), sc("w"), OP.mult)
    fill(T.keep[:, 0:130:5], 0.0, ("keep",), "V")
    ts(y(4), L3, 2.0 * NC, OP.is_ge, ("L3", "w3"), ("y4",), sc("w3"), OP.mult)
    ts(y(3), T.qi[:, :], sc("be"), OP.mult, ("qi", "be"), ("y3",))
    scan(T.s5[:, :], T.keep[:, :], T.y5[:, :], ("keep", "y0", "y1", "y2", "y3", "y4"), ("s5",))
    ts(T.x1[:, :], T.s5[:, 4:130:5], sc("c1"), OP.add, ("s5", "c1"), ("x1",))
    node({"V": 0.08 + 3.5 * CYCLE * RING}, lambda e: g.vector.tensor_copy(T.mp[:, slot(0, 9)].indirect(T.x1[:, :]), T.iv[:, :]), ("iv", "x1"), ("big0", "big1", "big2", "inv"))
    for sem, tok, parts in (("dM", "mid", ((0, 7, 1, 12, 6), (1, 7, 0, 14, 8), (0, 1, 7, 14, 0))), ("dN", "odd", ((0, 7, 1, 13, 7), (1, 7, 0, 11, 7), (0, 1, 7, 19, 7)))):
        dmas(sem, [(T.mp[rows(a, n), slot(c)], T.mp[rows(b, n), slot(d)]) for a, n, b, c, d in parts], ("inv",), (tok,), 4)
    line("ui", bf(PAIR), ("bf",), -640.0, float(UI), "S")
    line("u3", bf(EVEN), ("bf", "ui"), 6.0 * NC, sc("ui"), "S")
    ts(T.ui[:, :], L2, sc("ui"), OP.add, ("L2", "ui"), ("uil",))
    tt(T.mp[0:112, slot(12)], T.mp[0:112, slot(12)], T.mp[0:112, slot(14)], OP.min, (), ("mid",))
    ts(T.x3[:, :], L3, sc("u3"), OP.add, ("L3", "u3"), ("x3",))
    for e, c, a, b in (("V", 0, 6, 26), ("S", NC, 0, 22), ("V", NC + 16 * 22, 22, 26)):
        affine(T.mp[:, OWN + c:OWN + c + 16 * (b - a)], T.mp[:, slot(0, 20)].indirect(T.x3[:, a:b]), ("inv", "mid", "odd", "x3"), (("ct", a),), who=e, pick=True)
    cts = (("ct", 6), ("ct", 0), ("ct", 22))
    dmas("dC", [(T.mp[rows(h), c:c + DBL], T.mp[rows(e), OWN:OWN + DBL])
                for e in (0, 2, 4, 6) for h, c in ((e + 1, OWN + DBL), ((e - 1) % 8, OWN + 2 * DBL))], cts, ("near",), 4)
    iota(T.pl[:, :], [[0, 40]], int(BIG), 0, ("pl",))
    dmas("dF", [(T.pl[rows(h, n), c:c + 20], T.mp[GRP * e:GRP * e + 1, slot(k, n)])
                for e in (0, 2, 4, 6) for h, n, c, k in ((e, 2, 0, 7), ((e - 1) % 8, 1, 20, 6 if e else 0))], ("inv",), ("pl",), 4)
    node({"G": 0.2 + 2 * CYCLE * 516}, lambda e: g.affine_select(T.e1[:, :], T.ew[:, :], [[1, 516]], OP.is_equal, 0.0, -3, -4), ("ew",), ("e1",))
    iota(T.pI[:, 8:18], [[32, 5], [0, 2]], 0, 0, ("pJ",), True)
    quant(T.qx, T.sx, 0, NC, T.xt, 0, four("xO") + four("xG"), ("qxO", "qxG"))
    quant(T.qu, T.su, 0, 128, T.ut, 0, ("ut",), ("qu",))
    ts(bi(14, 10), T.pI[:, 8:18], 127, OP.bitwise_and, ("pJ",), ("pK",))
    ts(bi(24), part, 7, OP.bitwise_and, ("pI",), ("p8",))
    cp(T.ul[:, 0:10], bi(14, 10), ("pK",), ("ul0",))
    ts(T.ul[:, 10:11], bi(24), float(GRP), OP.mult, ("p8",), ("ul1",))
    node({"V": picked("V", 176)}, lambda e: g.vector.tensor_copy(T.qu2[:, :].bitcast(dt.uint32), T.qu[:, 0:128].bitcast(dt.uint32).indirect(T.ul[:, 0:11])), ("qu", "ul0", "ul1"), ("qu2",))
    node({"S": picked("S", 176)}, lambda e: g.scalar.activation(T.su2[:, :], T.su[:, 0:128].indirect(T.ul[:, 0:11]), FN.Copy), ("qu", "ul0", "ul1"), ("su2",))
    for b in range(4):
        quant(T.qe, T.se, 128 * b, 128 * b + 128, T.e1, 3 - b, ("e1",), (("qe", b),))
    unpack(T.qx, T.sx, 0, NC, ("qxO", "qxG"), (0, 1, 2, 6))
    line("uv", bf(PAIR), ("bf",), 640.0, -float(UI), "S")
    for k in range(3):
        affine(ids(UI + NC * k, NC), ids(0, NC), ("id0",), (("id1", k),), 1.0, float(UI + NC * k), "S")
    idt = ("id0", ("id1", 0), ("id1", 1), ("id1", 2), "uil", "uv", "id2")
    affine(T.src[:, DBL + NC:2 * DBL], ids(0, UI + 3 * NC).indirect(T.ui[:, 0:26]), idt, ("st1",), 1.0, sc("uv"), "S", True)
    affine(T.src[:, DBL:DBL + NC], ids(0, UI + 3 * NC).indirect(T.ui[:, 6:26]), idt, ("st0",), 1.0, sc("uv"), "S", True)
    dmas("dS", [(T.src[rows(a, n), c:c + DBL], T.src[rows(b, n), DBL:2 * DBL]) for a, n, b, c in ((2, 6, 0, 0), (0, 2, 6, 0), (0, 6, 2, 2 * DBL), (6, 2, 0, 2 * DBL))],
         ("st0", "st1"), ("src",), 4)

    def entry_constants():
        ts(bi(P16), part, 15, OP.bitwise_and, ("pI",), ("p16",))
        ts(bi(Q4), part, 2, OP.arith_shift_right, ("pI",), ("q4",), 3, OP.bitwise_and)
        cp(T.bf[:, 6:8], bi(6, 2), ("p16", "q4"), ("bg",))
        line("n", bf(P16), ("bg",), 2.0, 2.0 * (MO + CEN))
        line("aa", bf(PAR), ("bf",), 2.0 * DBL, 2.0 * OWN - NC)
        affine(T.xc[:, 2:60:3], T.src[:, IDB:IDB + NC:GRP], ("id0", "n"), ("nt",), 2.0, sc("n"))
        affine(T.ca[:, 0:20], T.pl[:, 0:20], ("pl", "aa"), (("ca", 0),), 2.0, sc("aa"))
        affine(T.ca[:, 20:40], T.pl[:, 20:40], ("pl",), (("ca", 1),), 2.0, 2.0 * (OWN + 2 * DBL) - NC)
        iota(T.lo[:, :], [[0, 60]], 0, 0, ("lo",))
        iota(T.lo[:, 0:60:3], [[0, 20]], int(4 * BIG), 0, ("lo",))

    def pattern(j, sg, pat, n, col):
        iota(j[:, :], [[0, HALF // n], [2, n]], -1, 0, (("j", n),))
        node({"S": span(HALF)}, lambda e: g.scalar.activation(sg[:, :], j[:, :], FN.Sign, bias=bf(col), scale=-0.5), (("j", n), "bg"), (("g", n),))
        affine(pat[:, :], sg[:, :], (("g", n),), ("P%d" % n,), -8.5 * B, -7.5 * B)

    def turn_constants():
        iota(T.ft[:, :], [[0, 512]], 0, 0, ("ft0", "ft1", "ft2"))
        quant(T.qc, T.sct, 0, 128, T.ew, 0, ("ew",), ("qc",))
        iota(T.pI[:, 20:24], [[32, 4]], 128 + 63, -1, ("pQ",), True)
        iota(T.t4[:, :], [[DBL, 4]], DBL, 0, ("t4",))
        ts(bi(26, 4), T.pI[:, 20:24], 5, OP.arith_shift_right, ("pQ",), ("rq",), 3, OP.bitwise_and)
        ts(T.rel[:, 4:8], bi(26, 4), -float(DBL), OP.mult, ("rq",), ("rl",), -float(DBL), OP.add)
        tt(T.rel[:, 0:4], T.rel[:, 4:8], T.t4[:, :], OP.add, ("rl", "t4"), ("rel",))
        line("f1", bf(P16), ("bg",), -B, 15 * B)
        line("nf1", bf(P16), ("bg",), B, -15 * B)
        affine(T.th[:, :], T.t4[:, :], ("t4", "f1"), ("th",), 1.0, sc("f1"))

    def offset_constants():
        for k in (1, 2):
            iota(ids(2 * NC * k, NC), [[1, NC]], 2 * NC * k, 0, ("id2",))
        pattern(T.j4, T.g4, T.p4, 4, Q4)
        line("fb", bf(GR), ("bf",), -1280.0, 4.0 * CEN - 12 * B)
        line("fc", bf(P16), ("bg", "fb"), 1.0, sc("fb"))
        line("fin", bf(Q4), ("bg", "fc"), 4 * B - 4, sc("fc"))

    def score(t, bank):
        a, toks = ((192, ("qxO", "layer")), (0, ("qxG",)), (64, ("qxO", "qxG")))[t]
        mm(bank, T.qx, T.sx, a, T.qu2, T.su2, 48, 128, toks + ("qu2", "su2"))
        p = slice(64 if t == 2 else 0, 128)
        ts(T.ft[p, t:32:4], ps[bank][p, 112:120], 0.0, OP.is_gt, (("ps", bank),), ("ft%d" % t,), 2.0 ** -5, OP.mult)

    def sums(bank):
        quant(T.qf, T.sf, 0, 128, T.ft, 0, ("ft0", "ft1", "ft2"), ("qf",))
        mm(bank, T.qc, T.sct, 0, T.qf, T.sf, 0, 128, ("qc", "qf"))

    def steps(bank):
        tt(T.cn[:, 0:4], ps[bank][:, 1:8:2], T.rel[:, 0:4], OP.add, (("ps", bank), "rel"), ("cnt",), 1)
        tt(T.df[:, 0:3], T.cn[:, 0:3], T.cn[:, 1:4], OP.subtract, ("cnt",), ("df",))
        affine(T.df[:, 3:4], T.cn[:, 0:1], ("cnt", "nf1"), ("zb",), -1.0, sc("nf1"))

    def even_count(k, lo, hi, toks, bank, out, tok):
        n = hi - lo
        mm(bank, T.qu2, T.su2, 32 * k, T.qx, T.sx, lo, n, toks + ("qu2", "su2"))
        node({"S": span(n) + 0.02}, lambda e: g.scalar.activation(T.sg[:, NC * k:NC * k + n], ps[bank][:, 0:n], FN.Sign, bias=TINY, scale=-1.0, accum_out=out),
             (("ps", bank),), (tok, ("sg", k)))

    def entries(k, more):
        ts(T.xc[:, k:60:3], T.ca[:, 20 * k:20 * k + 20], T.cn[:, 4 + k:5 + k], OP.add, (("no", k), ("n", k), ("ca", k)), (("xc", k),), more, OP.add)

    def least():
        scan(T.xs[:, :], T.lo[:, :], T.xc[:, :], ("lo", "nt", ("xc", 0), ("xc", 1)), ("xs",), OP.add, OP.min)
        ts(T.o1[:, :], T.xs[:, 2:60:3], 0.5, OP.mult, ("xs",), ("o1",))

    def lookup(cuts, out, table, off, r, tok):
        for e, a, b in cuts:
            affine(out[:, GRP * a:GRP * b], table.indirect(off[:, a:b]), r, [(tok, c) for c in range(a, b, 2)], who=e, pick=True)

    def fold(h, out, pat, got, r, tok):
        c = slice(HALF * h, HALF * h + HALF)
        scan(out[:, c], pat[:, :], got[:, c], [r] + [("r" + tok, c) for c in range(10 * h, 10 * h + 10, 2)], (("f" + tok, h),), OP.add, OP.max)

    def shared(h):
        return (("V", 10 * h, 10 * h + 6), ("S", 10 * h + 6, 10 * h + 10))

    def first(h):
        lookup(shared(h), T.r1, T.mp[:, 0:MO + 8 * NC], T.o1, ("o1", "near", "inv") + cts, "r1")

    def turn(h):
        x, xt, c = T.f1[:, HALF * h + 15:HALF * h + HALF:16], (("f1", h),), 50 * h
        affine(T.z5[:, c:c + 50:5], x, xt + ("zb",), (("z", 0, h),), 1.0, T.df[:, 3:4])
        for q in range(4):
            ts(T.z5[:, c + q + 1:c + 50:5], x, T.th[:, q:q + 1], OP.is_ge, xt + ("th", "cnt", "df"), (("z", q + 1, h),), T.df[:, q:q + 1] if q < 3 else T.cn[:, 3:4], OP.mult)
        scan(T.zs[:, c:c + 50], T.keep[:, 0:50], T.z5[:, c:c + 50], ["keep"] + [("z", q, h) for q in range(5)], (("zs", h),))
        cp(T.o2[:, 10 * h:10 * h + 10], T.zs[:, c + 4:c + 50:5], (("zs", h),), (("o2", h),))

    def second(h):
        lookup(shared(h), T.r2, T.src[:, :], T.o2, (("o2", h), "src", "st0", "st1") + idt, "r2")
        fold(h, T.f2, T.p4, T.r2, "P4", "2")
        ts(T.l4[:, 40 * h:40 * h + 40], T.f2[:, HALF * h + 3:HALF * h + HALF:4], 4.0, OP.mult, (("f2", h), "fin"), (("l4", h),), sc("fin"), OP.add)

    def gather(h, tile, tok, cut):
        for k, (a, b) in enumerate(((0, cut), (cut, 40))):
            affine(tile[:, GRP * a:GRP * b], T.win[:, :].indirect(T.l4[:, 40 * h + a:40 * h + b]), four("wO") + four("wG") + ("sh", "shO", "shG", ("l4", h)),
                   ((tok, k), (tok, k + 2)), who="VS"[k], pick=True)

    def packed(lo, tok):
        dmas("dOut", [(T.oc[:, 4 * lo:4 * (lo + HALF)], T.qx[:, lo:lo + HALF].bitcast(dt.uint8))]
             + [(T.osc[4 * k:4 * k + 4, lo:lo + HALF], T.sx[32 * k:32 * k + 4, lo:lo + HALF]) for k in range(4)], (tok,), (), 1)

    def result(lo, tok, bank):
        mm(bank, T.qv, T.sv, 0, T.qx, T.sx, lo, HALF, ("qv", tok))
        affine(T.yt[:, lo:lo + HALF], ps[bank][:, 0:HALF], (("ps", bank),), (("y", lo),))
        dmas("dOut", [(T.y[:, lo:lo + HALF], T.yt[:, lo:lo + HALF])], (("y", lo),), (), 4)

    for rd in range(3):
        if rd == 0:
            for k in range(2):
                even_count(k, 0, NC, ("qxO", "qxG"), 3 + k, T.cn[:, 4 + k:5 + k], ("n", k))
            out_of((0, 1, 2, 6), NC, T.win, 4 * CEN, ("wO", "wG"))
            spread(0, NC, 0, 16, four("wO") + four("wG"), "sh")
            entry_constants()
            pattern(T.j16, T.g16, T.p16, 16, P16)
        else:
            quant(T.qx, T.sx, 0, HALF, T.xt, 0, four("xG"), ("qxG",))
            unpack(T.qx, T.sx, HALF, NC, ("qxO", "layer"), (0, 1, 2, 3))
            for k in range(2):
                even_count(k, HALF, NC, ("qxO", "layer"), 4 + k, T.no[:, k:k + 1], ("no", k))
            out_of((0, 1, 2, 3), HALF, T.win, 4 * (CEN + HALF), ("wO",))
            for k in range(2):
                even_count(k, 0, HALF, ("qxG",), (6, 0)[k], T.cn[:, 4 + k:5 + k], ("n", k))
        for k in range(2):
            entries(k, T.no[:, k:k + 1] if rd else 0.0)
        least()
        if rd:
            spread(HALF, NC, 0, 8, four("wO"), "shO")
            for t in range(3):
                score(t, (7, 4, 5)[t])
            unpack(T.qx, T.sx, 0, HALF, ("qxG",), (1, 2, 3, 6))
            sums(7)
            out_of((1, 2, 3, 6), HALF, T.win, 4 * CEN, ("wG",))
            spread(0, HALF, 0, 8, four("wG"), "shG")
            spread(0, NC, 8, 16, four("wO") + four("wG"), "sh")
        first(0)
        if rd == 0:
            turn_constants()
            for t in range(3):
                score(t, (5, 7, 3)[t])
            sums(7)
        steps(7)
        fold(0, T.f1, T.p16, T.r1, "P16", "1")
        turn(0)
        if rd == 0:
            offset_constants()
        second(0)
        affine(T.acs[:, rd:24:3], ps[7][:, 0:8], (("ps", 7),), (("ac", rd),))
        lc, ls, land = T["lc%d" % rd], T["ls%d" % rd], "land%d" % rd
        gather(0, T.gt, "gt", 20)
        quant(T.q2, T.s2, 0, HALF, T.gt, 0, four("gt"), ("q2",))
        first(1)
        fold(1, T.f1, T.p16, T.r1, "P16", "1")
        turn(1)
        second(1)
        send(rd, [(lc[:, :].bitcast(dt.uint8), T.q2[:, :].bitcast(dt.uint8), 4 * HALF), (ls[:, :], T.s2[:, :], HALF)], ("q2",), land)
        for b in range(4):
            mm(4 + b, T.qe, T.se, 128 * b, lc, ls, 0, HALF, (("qe", b), land), True, False)
            mm(4 + b, T.wq, T.wsb, 128 * b, lc, ls, 0, HALF, ("wq", land), False, True, ("layer",))
        out_of((4, 5, 6, 7), HALF, T.xt, 0, ("xG",))
        gather(1, T.zo, "zo", 14)
        quant(T.qz, T.sz, 0, HALF, T.zo, 0, four("zo"), ("qz",))
        for b in range(4):
            mm(b, T.wq, T.wsb, 128 * b, T.qz, T.sz, 0, HALF, ("wq", "qz"))
        for b in range(4):
            affine(T.z32[:, HALF * b:HALF * b + HALF], T.zo[:, b:4 * HALF:4], four("zo"), (("z32", b),), 32.0, who="S")
            piece = T.sm[:, HALF * b:HALF * b + HALF]
            tt(piece, ps[b][:, 0:HALF], T.z32[:, HALF * b:HALF * b + HALF], OP.add, (("ps", b), ("z32", b)), (("sm", b),), 1)
            affine(T.xt[:, 4 * HALF + b:4 * NC:4], piece, (("sm", b),), (("xO", b),), 2.0 ** -5)
        quant(T.qx, T.sx, HALF, NC, T.xt, 4 * HALF, four("xO"), ("qxO",))
    quant(T.qx, T.sx, 0, HALF, T.xt, 0, four("xG"), ("qxG",))
    quant(T.qv, T.sv, 0, 128, T.vt, 0, ("vt",), ("qv",))
    result(0, "qxG", 1)
    packed(0, "qxG")
    result(HALF, "qxO", 0)
    packed(HALF, "qxO")
    dmas("dOut", [(T.ac[:, :], T.acs[0:1, 0:24])], (("ac", 0), ("ac", 1), ("ac", 2)), (), 4)

    total = {s: 0 for s in SEMAPHORES}
    known = {e: {} for e in eng}
    for i, e in plan(nodes):
        x = nodes[i]
        need = []
        for d in x["deps"] - x["loose"]:
            need.append(nodes[d]["left"] if "left" in nodes[d] and nodes[d]["sem"][3] not in x["toks"] else nodes[d]["mark"])
        best = {}
        for sem, val, clk in need:
            best[sem] = max(best.get(sem, 0), total[sem] if sem in LOCAL else val)
        for sem, v in sorted(best.items()):
            implied = any(s != sem and clk.get(sem, 0) >= v for s, val, clk in need)
            if known[e].get(sem, 0) < v and (sem in LOCAL or not implied):
                eng[e].wait_ge(T.sem[sem], v)
        for sem, val, clk in need:
            for s, v in clk.items():
                known[e][s] = max(known[e].get(s, 0), v)
        for sem, v in best.items():
            known[e][sem] = max(known[e].get(sem, 0), v)
        made = x["call"](e)
        if e == "G" and x["sem"]:
            arr, sent, n, land = x["sem"]
            total[arr], total[sent] = n, n
            x["mark"], x["left"] = (arr, n, {}), (sent, n, dict(known[e]))
            continue
        sem = x["sem"] or "c" + e
        for c in made if x["sem"] else [made]:
            c.then_inc(T.sem[sem], 16 if x["sem"] else 1)
            total[sem] += 16 if x["sem"] else 1
        x["mark"] = (sem, total[sem], dict(known[e]))
    for s in SEMAPHORES:
        if total[s] and known["Y"].get(s, 0) < total[s]:
            g.sync.wait_ge(T.sem[s], total[s])
